import numpy as np, ml_dtypes
CORES = [9,25,41,57]
N = 4
BF = ml_dtypes.bfloat16
W, H, Q, L, V, TH, TH2 = 4096, 256, 16, 4, 8, 2345, 820
J = Q - L + 1
HALF = (J - 1) // 2
B = HALF + L - 1
def which(s, z):
    return np.maximum(1, np.add.reduce((s <= z[:, None, :]).astype(np.int64), axis=1)) - 1
def place(s, c, k, p):
    sk = np.take_along_axis(s, k[:, None, :], 1); ck = np.take_along_axis(c, k[:, None, :], 1)
    return ((p - sk) * (2 * ck + 1) + 37 * ck) & (W - 1)
def pick(x, f):
    return np.take_along_axis(x, f.reshape(8, 1, -1), 2).reshape(8, 16, -1, H)
def seen(x, s, c, z):
    o = (5 * np.arange(H)) & (H - 1); got = []
    for q in range(N):
        so = s[q][..., o]; co = c[q][..., o]
        got.append(pick(x[q], place(so, co, which(so, z[q]), z[q][:, None, :] + np.arange(Q)[None, :, None] - B)))
    return np.stack(got)
def parts(rng):
    span = rng.integers(116, 141, (N, 8, 1, 1))
    x = 128 + np.floor((rng.random((N, 8, 16, W), dtype=np.float32) - 0.5) * span).astype(np.int64)
    tm = 128 + np.floor((rng.random((N, 8, 16, L, H)) - 0.5) * span[..., None]).astype(np.int64)
    s = np.sort(rng.integers(0, W, (N, 8, 16, H)), axis=2); c = rng.integers(0, 1024, (N, 8, 16, H)); z = rng.integers(16, 3001, (N, 8, H))
    return x, s, c, z, tm
def pack(x, s, c, z, tm):
    return {"xl": np.ascontiguousarray(x).reshape(N, 128, W).astype(np.float32).astype(BF), "s0": np.ascontiguousarray(s).reshape(N, 128, H).astype(np.int32),
            "cf": np.ascontiguousarray(c).reshape(N, 128, H).astype(np.int32), "z0": np.ascontiguousarray(z).astype(np.int32),
            "t0": np.ascontiguousarray(tm).reshape(N, 128, L * H).astype(np.float32).astype(BF)}
def setup_inputs(rng):
    return pack(*parts(rng))
def setup_inputs_spread(rng):
    amps = np.array([4, 16, 32, 64, 96, 128])
    x = np.clip(128 + np.floor((2 * rng.random((N, 8, 16, W), dtype=np.float32) - 1) * rng.choice(amps, (N, 8, 1, W))), 0, 255).astype(np.int64)
    tm = np.clip(128 + np.floor((2 * rng.random((N, 8, 16, L, H)) - 1) * rng.choice(amps, (N, 8, 1, L, H))), 0, 255).astype(np.int64)
    s = np.where(rng.random((N, 8, 1, H)) < 0.5, rng.integers(0, W, (N, 8, 16, H)), np.clip(np.floor(np.exp2(12 * rng.random((N, 8, 16, H)))).astype(np.int64) - 1, 0, W - 1))
    c = np.clip(np.floor(np.exp2(10 * rng.random((N, 8, 16, H)))).astype(np.int64) - 1, 0, 1023)
    z = np.where(rng.random((N, 8, H)) < 0.5, rng.integers(16, 3001, (N, 8, H)), np.clip(np.floor(np.exp2(11.6 * rng.random((N, 8, H)))).astype(np.int64), 16, 3000))
    return pack(x, np.sort(s, axis=2), c, z, tm)
def turns(w, u):
    return np.where((u & 1) == 1, 255 - w, w)
def setup_inputs_ends(rng):
    x = 255 * (rng.random((N, 8, 16, W), dtype=np.float32) < 0.125).astype(np.int64); tm = 255 * (rng.random((N, 8, 16, L, H)) < 0.125).astype(np.int64)
    flip = rng.permutation(np.array([0, 0, 1, 1]))
    for g in range(2, 6):
        if flip[g - 2] == 1: x[:, g] = 255 - x[:, g]; tm[:, g] = 255 - tm[:, g]
    nz = rng.integers(0, 17, (N, 8, 1, H)); low = np.where(np.arange(16).reshape(1, 1, 16, 1) < nz, 0, W - 1)
    s = np.where(rng.random((N, 8, 1, H)) < 0.5, low, (W - 1) * rng.integers(0, 2, (N, 8, 16, H))); s[..., 0] = 0; s[..., H - 1] = W - 1
    c = 1023 * rng.integers(0, 2, (N, 8, 16, H)); z = 16 + 2984 * rng.integers(0, 2, (N, 8, H)); z[..., 0] = 16; z[..., H - 1] = 3000
    level = 255 * int(rng.integers(0, 2)); turn = int(rng.integers(0, 2))
    x[:, 7] = level; rec = 255 * rng.integers(0, 2, (N, 1, 1, H)); rec[..., 0] = 255 - level; rec[..., H - 1] = 255 - level; rec[..., 1] = level; rec[..., H - 2] = level; tm[:, 7] = rec
    for q in range(N): x[q, 0] = 255 * ((q + turn) % 2)
    tm[:, 0] = 255 * rng.integers(0, 2, (N, 1, 1, H))
    x[:, 1, :, 0::2] = 0; x[:, 1, :, 1::2] = 255; tm[:, 1] = 255 * rng.integers(0, 2, (N, 1, L, H))
    code = 255 * rng.integers(0, 2, (16, HALF * N))
    for q in range(N): x[q, 6] = code[:, (np.arange(W) - HALF * q) % (HALF * N)]
    s[:, 6] = 0; c[:, 6] = 0
    b = int(rng.integers(0, N)); s[:, 5] = W - 1; c[:, 5] = 1023; z[:, 5] = 3000; z[b, 5] = 16
    u = np.arange(W) - 4300; col = (u * 2047 + 37 * 1023) & (W - 1)
    far = W - 1 + HALF * (V - 1 - (V - 1) // N)
    p = 255 * rng.integers(0, 2, (16, 1)); other = np.where(rng.permutation(16).reshape(16, 1) < 8, 255 - p, p)
    period = HALF * (N - 1); ring = 255 * rng.integers(0, 2, (16, period)); ring[:, int(u[np.argmin(col)]) % period] = (255 - turns(p, far - HALF))[:, 0]
    for d in range(N):
        near = turns(p if d % 2 == 0 else other, u)
        if d == N - 1: near = np.where((u >= -far - HALF) & (u < -far - HALF + L), turns(p, u), near)
        x[(b + d) % N, 5][:, col] = np.where(u < -2600, near, ring[:, (u + HALF * d) % period])
    y = seen(x, s, c, z)
    tm[:, 6] = y[:, 6, :, J - 1:J - 1 + L]; tm[:, 5] = y[:, 5, :, :L]; tm[b, 5] = turns(other, np.arange(L))[:, :, None]
    return pack(x, s, c, z, tm)
def setup_inputs_corners(rng):
    x, s1, c, z, tm = parts(rng); gs = rng.permutation(8)
    x[:, gs[0]] = 120 + (x[:, gs[0]] & 15); x[:, gs[1]] = rng.integers(0, 256, (N, 16, W))
    kind = rng.integers(0, 8, (N, 8, 1, H)); s = np.where(kind == 1, s1[:, :, 5:6], s1); s = np.where(kind == 2, s1[:, :, ::-1], s); s = np.where(kind == 3, W - 1, s)
    s = np.where(kind == 4, np.arange(16).reshape(1, 1, 16, 1), s); s = np.where(kind == 5, rng.permuted(s1, axis=2), s)
    c = np.where(rng.random((N, 8, 16, H)) < 0.3, rng.choice(np.array([0, 1, 511, 512, 1023]), (N, 8, 16, H)), c)
    so = s[..., (5 * np.arange(H)) & (H - 1)]; near = np.take_along_axis(so, rng.integers(0, 16, (N, 8, 1, H)), 2)[:, :, 0]
    z = np.clip(near + rng.choice(np.array([-6, -1, 0, 1, 5, Q - 1, Q, Q + 1]), (N, 8, H)), 16, 3000)
    y = seen(x, s, c, z); j0 = rng.choice(np.array([0, 1, HALF, J - 1]), (N, 8, 1, 1, H)); m = np.take_along_axis(y, j0 + np.arange(L).reshape(1, 1, 1, L, 1), 3)
    tm = np.where(rng.random((N, 8, 1, 1, H)) < 0.6, m, tm)
    tm[:, gs[2]] = 255 * rng.integers(0, 2, (N, 1, L, H)); tm[:, gs[3]] = m[:, gs[3]]
    tm[:, gs[4]] = 255 * rng.integers(0, 2, (N, 1, L, H)); tm[:, gs[4], :, :, H - 1] = m[:, gs[4], :, :, H - 1]
    return pack(x, s, c, z, tm)
def steps(rng):
    b = TH2 // 16; e = rng.integers(-8, 9, 8)
    return b + np.concatenate([e, -e]) + (np.arange(16) < TH2 - 16 * b).astype(np.int64)
def pairs(rng, total, w):
    a = np.zeros(16, np.int64); a[[0, 9]] = (w + 1) // 2; a[[1, 8]] = w // 2
    rest = total - 2 * w; b = rest // 12; e = rng.integers(-8, 9, 6)
    a[[2, 3, 4, 5, 6, 7, 10, 11, 12, 13, 14, 15]] = b + np.concatenate([e, -e]) + (np.arange(12) < rest - 12 * b).astype(np.int64)
    return a
def setup_inputs_edges(rng):
    x, s, c, z, tm = parts(rng)
    for g in range(8):
        if g % 4 == 1: continue
        p0 = rng.integers(50, 71, 16); p1 = p0 + steps(rng); p2 = p1 + steps(rng); p3 = p2 - steps(rng); p3[int(rng.integers(0, 16))] -= 1
        p = np.stack([p0, p1, p2, p3], axis=1)
        for q in range(N): x[q, g] = p[:, (np.arange(W) + int(rng.integers(0, 4))) & 3]
    w = 257 + 4 * int(rng.integers(0, 6)); p0 = rng.integers(20, 61, 16); p1 = p0 + pairs(rng, TH2 + 1, w); p2 = p1 + rng.integers(1, 4, 16); p3 = p2 - pairs(rng, TH2, w + 2)
    p = np.stack([p0, p1, p2, p3], axis=1)
    for q in range(N): x[q, 5] = p[:, (np.arange(W) + int(rng.integers(0, 4))) & 3]
    y = seen(x, s, c, z); dist = rng.choice(np.array([0, TH - 1, TH, TH + 1]), (N, 8, 1, 1, H)); j0 = rng.integers(0, 4, (N, 8, 1, 1, H))
    m = np.take_along_axis(y, j0 + np.arange(L).reshape(1, 1, 1, L, 1), 3); each = dist // (16 * L)
    d = each + (np.arange(16 * L).reshape(1, 1, 16, L, 1) < dist - 16 * L * each)
    sign = np.where(m < 80, -1, np.where(m > 135, 1, 1 - 2 * (np.arange(16).reshape(1, 1, 16, 1, 1) & 1)))
    planted = (np.arange(8) % 4 != 1).reshape(1, 8, 1, 1, 1)
    return pack(x, s, c, z, np.where(planted, m + sign * d, tm))
def check_inputs(d):
    bad = []
    for k, lo, hi in (("xl", 0, 255), ("s0", 0, W - 1), ("cf", 0, 1023), ("z0", 16, 3000), ("t0", 0, 255)):
        a = np.asarray(d[k]).astype(np.float64)
        if not (np.min(a) >= lo and np.max(a) <= hi): bad.append("range of " + k)
        elif np.any(a != np.floor(a)): bad.append("whole numbers in " + k)
    return bad
def reference(xl, s0, cf, z0, t0):
    x = xl.astype(np.int32).reshape(N, 8, 16, W); s = s0.astype(np.int64).reshape(N, 8, 16, H); c = cf.astype(np.int64).reshape(N, 8, 16, H)
    z = z0.astype(np.int64); tm = t0.astype(np.int32).reshape(N, 8, 16, L, H); ties = np.zeros((N, 8), np.int64)
    row = np.arange(16)[None, :, None]; m = np.arange(Q)[None, :, None]
    for t in range(V):
        for r in range(N):
            q = (r + t) % N
            o = ((5 * np.arange(H)[None, :] + ties[r][:, None]) & (H - 1))[:, None, :]
            so = np.take_along_axis(s[q], o, 2); co = np.take_along_axis(c[q], o, 2)
            k = which(so, z[r])
            y = pick(x[q], place(so, co, k, z[r][:, None, :] + m - B))
            e = np.stack([np.add.reduce(np.abs(y[:, :, j:j + L] - tm[r]), axis=(1, 2)) for j in range(J)])
            best = np.argmin(e, axis=0); tie = np.min(e, axis=0) < TH
            so = so + np.where(tie[:, None, :] & (row >= k[:, None, :]), HALF - best[:, None, :], 0)
            np.put_along_axis(s[q], o, so, 2)
            zz = np.where(tie, z[r], np.maximum(z[r] - Q, 0)); k = np.where(tie, k, which(so, zz))
            v = pick(x[q], place(so, co, k, zz[:, None, :] + m))
            over = (np.add.reduce(np.abs(v[:, :, 1:] - v[:, :, :-1]), axis=1) > TH2)[:, L - 1:]
            n = np.where(np.any(over, axis=1), L + np.argmax(over, axis=1), Q)
            tm[r] = np.take_along_axis(v, n[:, None, None, :] - L + np.arange(L)[None, None, :, None], 2)
            z[r] = zz + n - 1
            ties[r] = np.add.reduce(tie.astype(np.int64), axis=1)
    return {"ys": s.reshape(N, 128, H).astype(np.float32), "yz": z.astype(np.float32), "yt": tm.reshape(N, 128, L * H).astype(np.float32).astype(BF)}

@@ -1,0 +1,570 @@
+import numpy as np
+from concourse.mybir import dt, AluOpType as Op, ActivationFunctionType as AF
+
+NV = 8
+J = 13
+JA = (11, 11)
+NM = 4
+GP = 4
+EY = (0, 1)
+VG = (("v2", 1, 1), ("y2", 0, 1), ("y2", 0, 3), ("v2", 1, 3))
+VG0, VGL = VG, VG
+WIN = 0.02
+BONUS = {("F", 0): -96.8, ("H", 0): -145.4, ("D", 0): 78.0, ("N", 0): 229.2, ("E", 0): -208.8, ("L", 0): 199.4, ("C", 0): -76.6,
+         ("F", 1): -136.4, ("H", 1): -204.6, ("D", 1): -162.2, ("N", 1): 211.4, ("E", 1): -111.2}
+OPB = {}
+MAGIC = 201326592.0
+EARLY, LATE = 37528.0, 1.0e9
+
+F32, BF, F16, I32, U16 = "float32", "bfloat16", "float16", "int32", "uint16"
+SCRATCH = {
+    "x": ("sbuf", [128, 4096], BF), "t0s": ("sbuf", [128, 1024], BF), "ytb": ("sbuf", [128, 1024], BF),
+    "s0s": ("sbuf", [128, 256], I32), "cfs": ("sbuf", [128, 256], I32), "z0s": ("sbuf", [8, 256], I32), "z0f": ("sbuf", [8, 256], F32),
+    "st0": ("sbuf", [128, 256], F32), "st1": ("sbuf", [128, 256], F32), "sg": ("sbuf", [128, 256], F32),
+    "dg0": ("sbuf", [128, 256], F32), "dg1": ("sbuf", [128, 256], F32), "ysb": ("sbuf", [128, 256], F32),
+    "zb": ("sbuf", [128, 256], F32), "zl": ("sbuf", [128, 8 * 256], F32), "zm": ("sbuf", [128, 8 * 256], F32),
+    "al": ("sbuf", [128, 64], F32), "am": ("sbuf", [128, 64], F32),
+    "li": ("sbuf", [128, 16], I32), "lm": ("sbuf", [128, 16], I32), "lu": ("sbuf", [128, 16], U16),
+    "iP": ("sbuf", [128, 128], I32), "iQ": ("sbuf", [128, 128], I32), "iC": ("sbuf", [128, 104], I32), "iJ": ("sbuf", [128, 104], I32),
+    "iL": ("sbuf", [128, 16], I32), "i64": ("sbuf", [128, 32], I32),
+    "pg": ("sbuf", [128, 128], I32), "qg": ("sbuf", [128, 128], I32), "pm": ("sbuf", [128, 128], I32), "qm": ("sbuf", [128, 128], I32),
+    "sh": ("sbuf", [128, 32], I32), "q1": ("sbuf", [128, 32], I32), "q2": ("sbuf", [128, 32], I32), "l5": ("sbuf", [128, 16], I32),
+    "w9": ("sbuf", [128, 128], F32), "w18": ("sbuf", [128, 128], F32), "mu": ("sbuf", [128, 32], F32), "shf": ("sbuf", [128, 8], F32),
+    "gf": ("sbuf", [128, 8], F32), "gr": ("sbuf", [128, 104], F32), "sg1": ("sbuf", [128, 104], F32), "sg2": ("sbuf", [128, 104], F32),
+    "B32": ("sbuf", [128, 128], F32), "Bb": ("sbuf", [128, 128], BF), "Ib": ("sbuf", [128, 128], BF), "I16": ("sbuf", [128, 128], BF),
+    "Im": ("sbuf", [128, 128], BF), "Ih": ("sbuf", [128, 128], F16), "W0": ("sbuf", [128, 128], F16), "W1": ("sbuf", [128, 128], F16),
+    "Wu": ("sbuf", [128, 512], BF), "G1": ("sbuf", [128, 8], BF), "G32": ("sbuf", [128, 8], BF), "Z": ("sbuf", [128, 8, 32], BF),
+    "RT0": ("sbuf", [128, 104], BF), "RT1": ("sbuf", [128, 104], BF), "cj": ("sbuf", [128, 104], BF), "cpad": ("sbuf", [128, 104], BF), "KD": ("sbuf", [128, 104], F32),
+    "ONE": ("sbuf", [128, 104], F32), "RD": ("sbuf", [128, 128], BF), "Qc": ("sbuf", [128, 32], F16), "rp1": ("sbuf", [128, 8], F32),
+    "LB": ("sbuf", [128, 16], F32), "LF": ("sbuf", [128, 16], F32), "R8": ("sbuf", [8, 128], F32),
+    "w7": ("sbuf", [128, 128], BF), "c185": ("sbuf", [128, 128], BF), "cm16": ("sbuf", [128, 128], BF), "c3": ("sbuf", [128, 128], BF),
+    "c205": ("sbuf", [128, 8], BF),
+    "yps": ("psum", [128, 128, 16], F32), "dif": ("psum", [128, 512], F32), "vt": ("psum", [128, 512], F32),
+    "kb": ("psum", [128, 512], F32), "sm": ("psum", [128, 512], F32),
+}
+_HALF = {"cmp": (128, BF), "geb": (128, BF), "Hb": (128, F32), "oH": (128, F32), "oD": (128, F16), "fi": (128, I32), "fm": (128, I32),
+         "of": (128, U16), "y2": (2048, BF), "v2": (2064, BF), "Va": (1536, BF), "ks": (104, F32), "rr": (8, F32), "dd": (8, F32),
+         "Xs": (256, BF), "Xr": (256, BF), "dge": (128, F32), "zp": (128, F32), "nx": (104, F32), "ns": (104, F32), "Xn": (128, BF),
+         "Xnr": (128, BF), "nsb": (128, BF), "tof": (32, U16), "Ma": (512 * (J - min(JA)), BF)}
+for _n, (_c, _d) in _HALF.items():
+    SCRATCH[_n] = ("sbuf", [128, 2 * _c], _d)
+for _m in range(NM):
+    SCRATCH["mb%d" % _m] = ("sbuf", [128, 128, 4], BF)
+SCRATCH["Vb"] = ("sbuf", [128, 256, 12], BF)
+SCRATCH["ts"] = ("sbuf", [128, NV * 1024], BF)
+for _t in range(NV + 1):
+    SCRATCH["tl%d" % _t] = ("sbuf", [128, 256, 4], BF)
+SEMAPHORES = ["v", "a", "p", "q", "lx", "ls", "lc", "lz", "lt", "loc", "sto"]
+for _t in range(1, NV + 1):
+    SEMAPHORES += ["rA%d" % _t, "rz%d0" % _t, "rz%d1" % _t, "rT%d0" % _t, "rT%d1" % _t]
+SEMAPHORES.remove("rA%d" % NV)
+
+
+def build(T, gs, nxt):
+    ops, lastw, readers, accs, nums, tag = [], {}, {}, {}, {}, [("I", 0, 0)]
+
+    def add(eng, fns, cost, rd=(), wr=(), acc=None, acq=None, use=None, after=(), pin=None):
+        i = len(ops)
+        deps = {}
+        nums[tag[0]] = nums.get(tag[0], -1) + 1
+        for k in rd:
+            for o in ([lastw[k]] if k in lastw else []) + accs.get(k, []):
+                deps[o] = True
+            readers.setdefault(k, []).append(i)
+        if acc is not None:
+            deps[lastw[acc]] = deps.get(lastw[acc], False)
+            accs.setdefault(acc, []).append(i)
+        for k in wr:
+            for o in readers.get(k, []) + ([lastw[k]] if k in lastw else []) + accs.get(k, []):
+                if o != i:
+                    deps[o] = deps.get(o, False)
+            lastw[k], readers[k], accs[k] = i, [], []
+        for o in after:
+            deps[o] = deps.get(o, False)
+        if acq is not None:
+            use = i
+        ops.append(dict(eng=eng, fns=fns, cost=cost, deps=deps, acq=acq, use=use, sym=pin, bonus=BONUS.get(tag[0][:2], 0.0) + OPB.get(tag[0][:2] + (nums[tag[0]],), 0.0), tag=tag[0], num=nums[tag[0]], wr=tuple(wr)))
+        return i
+
+    v, s, p, g = gs["v"], gs["a"], gs["p"], gs["q"]
+
+    def V(fn, c, rd=(), wr=(), **kw):
+        return add("v", [fn], 0.05 + max(64, c) * 0.001, rd, wr, **kw)
+
+    def A(fn, c, rd=(), wr=(), **kw):
+        return add("a", [fn], 0.065 + c * 0.001, rd, wr, **kw)
+
+    def P(fns, c, rd=(), wr=(), **kw):
+        return add("p", fns, c * 0.0005, rd, wr, **kw)
+
+    def mm(out, l, r, start=True, stop=True):
+        return lambda last: p.matmul(out, l, r, start, stop or last)
+
+    def ts(out, a, s1, s2, o0, o1=None):
+        if o1 is None:
+            return lambda last: v.tensor_scalar(out, a, s1, None, o0)
+        return lambda last: v.tensor_scalar(out, a, s1, s2, o0, o1)
+
+    def tt(out, a, b, o):
+        return lambda last: v.tensor_tensor(out, a, b, o)
+
+    def cp(out, a):
+        return lambda last: v.tensor_copy(out, a)
+
+    def act(out, a, f=AF.Copy, bias=0.0, scale=1.0):
+        return lambda last: s.activation(out, a, f, bias=bias, scale=scale)
+
+    def scan(out, a, b, o0, o1):
+        return lambda last: v.tensor_tensor_scan(out, a, b, 0.0, o0, o1)
+
+    def load(out, a, sem, key, lat, after=()):
+        return add("d", [lambda last: gs["d"].dma_start(out, a)], lat, (), [key], pin=(sem, 16), after=after)
+
+    def H(name, h, a=0, b=None, step=None):
+        n = _HALF[name][0]
+        return T[name][:, n * h + a: n * h + (n if b is None else b): (step or 1)]
+
+    load(T.z0s[:, :], T.z0[:, :], "lz", "z0s", 2.5)
+    load(T.s0s[:, :], T.s0[:, :], "ls", "s0s", 3.0)
+    load(T.cfs[:, :], T.cf[:, :], "lc", "cfs", 3.5)
+    load(T.x[:, :], T.xl[:, :], "lx", "x", 9.0)
+    load(T.t0s[:, :], T.t0[:, :], "lt", "t0s", 10.0)
+
+    def iota(name, pat, base, cm):
+        add("q", [lambda last: g.iota(T[name][:, :], pat, base, cm)], 0.4, (), [name])
+    iota("iP", [[0, 128]], 0, 1)
+    iota("iQ", [[1, 128]], 0, 0)
+    iota("iL", [[16, 16]], 0, 0)
+    iota("iC", [[1, 8], [0, 13]], 0, 0)
+    iota("iJ", [[0, 8], [1, 13]], 0, 0)
+    iota("i64", [[64, 32]], 6, 0)
+
+    def C(fn, c, rd, wr):
+        return V(fn, c, rd, [wr])
+
+    def fill(name, val, c):
+        C(lambda last: v.memset(T[name][:, :], val) if name != "Z" else v.memset(T.Z[:, :, :], val), c, [], name)
+    A0 = lambda n, a=0, b=None: T[n][:, a:b] if b is not None else T[n][:, :]
+    C(ts(A0("pm"), A0("iP"), 15, None, Op.bitwise_and), 128, ["iP"], "pm")
+    C(tt(A0("LB"), A0("iL"), A0("pm", 0, 16), Op.add), 16, ["iL", "pm"], "LB")
+    C(ts(A0("l5"), A0("LB"), 5.0, None, Op.mult), 16, ["LB"], "l5")
+    C(ts(A0("LF"), A0("LB"), 205.0, None, Op.mult), 16, ["LB"], "LF")
+    C(ts(A0("qg"), A0("iQ"), 4, None, Op.arith_shift_right), 128, ["iQ"], "qg")
+    C(ts(A0("pg"), A0("iP"), 4, None, Op.arith_shift_right), 128, ["iP"], "pg")
+    C(ts(A0("qm"), A0("iQ"), 15, None, Op.bitwise_and), 128, ["iQ"], "qm")
+    C(ts(T.rp1[:, 0:1], T.pm[:, 0:1], 1.0, None, Op.add), 1, ["pm"], "rp1")
+    C(tt(A0("B32"), A0("pg"), A0("qg"), Op.is_equal), 256, ["pg", "qg"], "B32")
+    C(tt(T.R8[:, :], T.iP[0:8, :], T.qg[0:8, :], Op.is_equal), 256, ["iP", "qg"], "R8")
+    A(act(A0("Bb"), A0("B32")), 128, ["B32"], ["Bb"])
+    C(tt(A0("Ib"), A0("iP"), A0("iQ"), Op.is_equal), 256, ["iP", "iQ"], "Ib")
+    A(act(A0("I16"), A0("Ib"), scale=16.0), 128, ["Ib"], ["I16"])
+    A(act(A0("Im"), A0("Ib"), scale=-1.0), 128, ["Ib"], ["Im"])
+    C(cp(A0("Ih"), A0("Ib")), 64, ["Ib"], "Ih")
+    C(ts(A0("w9"), A0("qm"), 0.5, None, Op.add), 128, ["qm"], "w9")
+    C(tt(A0("W0"), A0("w9"), A0("B32"), Op.mult), 256, ["w9", "B32"], "W0")
+    C(tt(A0("gf"), T.pg[:, 0:8], T.iQ[:, 0:8], Op.is_equal), 16, ["pg", "iQ"], "gf")
+    C(cp(A0("G1"), A0("gf")), 8, ["gf"], "G1")
+    C(ts(A0("G32"), A0("gf"), 32.0, None, Op.mult), 8, ["gf"], "G32")
+    fill("Z", 0.0, 256)
+    for k in range(4):
+        C(ts(T.Z[:, :, 16 + k], A0("gf"), -16.0, None, Op.mult), 8, ["gf", "Z"], "Z")
+    C(ts(A0("cj"), A0("iJ"), 10.0, None, Op.add), 104, ["iJ"], "cj")
+    C(ts(A0("cpad"), A0("iJ"), 0.0, 1000.0, Op.is_equal, Op.mult), 104, ["iJ"], "cpad")
+    C(ts(A0("KD"), A0("iJ"), 0.0, LATE, Op.is_equal, Op.mult), 104, ["iJ"], "KD")
+    C(tt(A0("gr"), T.pg[:, 0:104], A0("iC"), Op.is_equal), 208, ["pg", "iC"], "gr")
+    for h in range(2 if JA[0] != JA[1] else 1):
+        C(ts(A0("sg1"), A0("iJ"), float(JA[h]), 32.0, Op.is_ge, Op.mult), 104, ["iJ"], "sg1")
+        C(ts(A0("sg2"), A0("sg1"), -16.0, None, Op.add), 104, ["sg1"], "sg2")
+        C(tt(A0("RT%d" % h), A0("sg2"), A0("gr"), Op.mult), 208, ["sg2", "gr"], "RT%d" % h)
+    RT = ["RT0", "RT%d" % (JA[0] != JA[1])]
+    C(ts(T.RD[:, 0:128], A0("qm"), 0.0, None, Op.is_gt), 128, ["qm"], "RD")
+    C(ts(A0("sh"), T.pm[:, 0:32], 2, None, Op.arith_shift_right), 32, ["pm"], "sh")
+    C(ts(A0("q1"), A0("sh"), 12.0, None, Op.mult), 32, ["sh"], "q1")
+    C(tt(A0("q2"), A0("q1"), T.pm[:, 0:32], Op.add), 64, ["q1", "pm"], "q2")
+    C(tt(A0("Qc"), A0("q2"), A0("i64"), Op.add), 64, ["q2", "i64"], "Qc")
+    for u in range(4):
+        C(ts(T.mu[:, 8 * u:8 * u + 1], T.sh[:, 0:1], float(u), None, Op.is_equal), 1, ["sh"], "mu%d" % u)
+        C(ts(T.Wu[:, 128 * u:128 * u + 128], A0("Ib"), T.mu[:, 8 * u:8 * u + 1], None, Op.mult), 64, ["Ib", "mu%d" % u], "Wu%d" % u)
+    fill("w7", 2.0 ** -7, 64)
+    fill("c185", -18.5, 64)
+    fill("cm16", -16.0, 64)
+    fill("c3", -6.0, 64)
+    fill("c205", 205.0, 8)
+    fill("ONE", 1.0, 104)
+    for h in EY:
+        C((lambda h: lambda last: v.memset(H("v2", h, 2048, 2064), 0.0))(h), 16, [], "v2p%d" % h)
+    for h in range(2):
+        C((lambda h: lambda last: v.memset(H("Xs", h), 0.0))(h), 128, [], "Xs%d" % h)
+        C((lambda h: lambda last: v.memset(H("Xn", h), 0.0))(h), 64, [], "Xn%d" % h)
+
+    C(cp(T.z0f[:, :], T.z0s[:, :]), 256, ["z0s"], "z0f")
+    tx = P([mm(T.sm[:, 0:256], T.R8[:, :], T.z0f[:, :])], 1024, ["R8", "z0f"], ["sm"], acq="sm")
+    for h in range(2):
+        V(ts(T.zb[:, 128 * h:128 * h + 128], T.sm[:, 128 * h:128 * h + 128], 9.0, None, Op.add), 128, ["sm"], ["z0%d" % h], use=tx)
+    C(cp(A0("st0"), A0("s0s")), 256, ["s0s"], "st0_0")
+    lastw["st0_1"] = lastw["st0_0"]
+    C(ts(A0("dg1"), A0("cfs"), 2.0, 1.0, Op.mult, Op.add), 256, ["cfs"], "dg1")
+    for h in range(2):
+        for a in range(4):
+            src = T.t0s[:, 256 * a + 128 * h:256 * a + 128 * h + 128]
+            dst = T.tl0[:, 128 * h:128 * h + 128, a]
+            if a < 2:
+                V(cp(dst, src), 64, ["t0s"], ["T0%d" % h] if a == 0 else ["T0%d_%d" % (h, a)])
+            else:
+                A(act(dst, src), 128, ["t0s"], ["T0%d_%d" % (h, a)])
+
+    mcount = [0]
+    tx_of = {}
+
+    def gatherlist(t):
+        if t == 0:
+            C(ts(A0("lm"), A0("l5"), 255, None, Op.bitwise_and), 16, ["l5"], "lm")
+        else:
+            b = T.al[:, 4 * t:4 * t + 1]
+            if t == 1:
+                V(ts(A0("li"), A0("LB"), b, None, Op.add), 16, ["LB", "A1"], ["li"])
+            else:
+                V(ts(A0("li"), A0("LB"), b, T.al[:, 4 * t - 4:4 * t - 3], Op.add, Op.subtract), 16, ["LB", "A%d" % t, "A%d" % (t - 1)], ["li"])
+            C(ts(A0("lm"), A0("li"), 255, None, Op.bitwise_and), 16, ["li"], "lm")
+        C(cp(A0("lu"), A0("lm")), 16, ["lm"], "lu")
+        st, dn, do = "st%d" % (t % 2), "dg%d" % (t % 2), "dg%d" % ((t + 1) % 2)
+        A(act(A0("sg"), T[st][:, :].indirect(T.lu[:, :])), 256 * 1.5, ["lu", st + "_0", st + "_1"], ["sg"])
+        A(act(A0(dn), T[do][:, :].indirect(T.lu[:, :])), 256 * 1.5, ["lu", do], [dn])
+
+    def zref(t, h):
+        return T.zb[:, 128 * h:128 * h + 128] if t == 0 else T.zl[:, 256 * (t - 1) + 128 * h:256 * (t - 1) + 128 * h + 128]
+
+    def select(t, h, W, tail):
+        hs, c0 = str(h), 128 * h
+        X = T.vt[:, 256 * h:256 * h + 128]
+        Y = T.vt[:, 256 * h + 128:256 * h + 256]
+        dn = "dg%d" % (t % 2)
+        OHS, OK = (Y, "vY") if tail == 0 else (X, "vX")
+        tx = P([mm(T.sm[:, 0:128], A0("Bb"), H("cmp", h))], 128, ["Bb", "cmp" + hs], ["cnt" + hs], acq="sm")
+        V(ts(OHS, T.sm[:, 0:128], 1.0, T.rp1[:, 0:1], Op.max, Op.is_equal), 128, ["cnt" + hs, "rp1"], [OK + hs], use=tx)
+        if tail == 0:
+            V(ts(H("geb", h), T.sm[:, 0:128], T.rp1[:, 0:1], None, Op.is_le), 128, ["cnt" + hs, "rp1"], ["geb" + hs], use=tx)
+        V(tt(H("oD", h), OHS, T[dn][:, c0:c0 + 128], Op.mult), 128, [OK + hs, dn], ["oD" + hs])
+        V(tt(H("oH", h), OHS, H("Hb", h), Op.mult), 128, [OK + hs, "Hb" + hs], ["oH" + hs])
+        tx = P([mm(T.sm[:, 0:128], A0("w7"), A0("c185"), True, False), mm(T.sm[:, 0:128], A0(W), H("oD", h), False, False)], 256,
+               ["w7", "c185", W, "oD" + hs], ["F" + hs], acq="sm")
+        P([mm(T.sm[:, 0:128], A0("B32"), H("oH", h), False, True)], 512, ["oH" + hs, "B32"], ["F" + hs], use=tx)
+        V(cp(H("fi", h), T.sm[:, 0:128]), 128, ["F" + hs], ["fi" + hs], use=tx)
+        V(ts(H("fm", h), H("fi", h), 4095, None, Op.bitwise_and), 128, ["fi" + hs], ["fm" + hs])
+        V(cp(H("of", h), H("fm", h)), 128, ["fm" + hs], ["of" + hs])
+
+    def samples(t, h, buf):
+        hs, k = str(h), 128 // GP
+        for q in range(GP):
+            on_v = (buf, h, q) in (VG0 if t == 0 else VGL if t == NV - 1 else VG)
+            (V if on_v else A)((cp if on_v else act)(H(buf, h, 16 * k * q, 16 * k * q + 16 * k), T.x[:, :].indirect(H("of", h, k * q, k * q + k))),
+                               16 * k * 1.5, ["x", "of" + hs], [buf + hs + "_%d" % q])
+    YK = lambda b, h: [b + str(h) + "_%d" % q for q in range(GP)]
+
+    def front(t, h):
+        hs, c0 = str(h), 128 * h
+        X = T.vt[:, 256 * h:256 * h + 128]
+        dn = "dg%d" % (t % 2)
+        V(tt(X, zref(t, h), T.sg[:, c0:c0 + 128], Op.subtract), 256, ["z%d%d" % (t, h), "sg"], ["vX" + hs])
+        V(ts(H("cmp", h), X, 9.0, None, Op.is_ge), 128, ["vX" + hs], ["cmp" + hs])
+        V(tt(H("Hb", h), X, T[dn][:, c0:c0 + 128], Op.mult), 128, ["vX" + hs, dn], ["Hb" + hs])
+        select(t, h, "W0", 0)
+        samples(t, h, "y2")
+
+    def heavy(t, h):
+        hs = str(h)
+        tl = T["tl%d" % t][:, 128 * h:128 * h + 128, :]
+        ta = lambda a: T["tl%d" % t][:, 128 * h:128 * h + 128, a]
+        TK = ["T%d%d" % (t, h)] + (["T0%d_%d" % (h, a) for a in (1, 2, 3)] if t == 0 else [])
+        K = T.kb[:, 0:104]
+        kx = P([mm(K, A0("w7"), A0("cj"), True, False)], 104, ["w7", "cj"] + YK("y2", h), ["K" + hs], acq="kb")
+        P([mm(K, ta(a), A0(RT[h]), False, False) for a in range(4)], 416, TK + [RT[h]], [], acc="K" + hs, use=kx)
+        P([mm(K, H("y2", h, m, None, 16), T.Z[:, :, 19 - m:32 - m], False, False) for m in range(16)], 1664,
+          YK("y2", h) + ["Z"], [], acc="K" + hs, use=kx)
+        yx = None
+        for b in range(4):
+            fill_b = [mm(T.yps[:, 32 * b:32 * b + 32, :], A0("Ib"), H("y2", h, 512 * b, 512 * b + 512))]
+            y = P(fill_b, 512, ["y2%s_%d" % (hs, b * GP // 4), "Ib"], ["yps%s%d" % (hs, b)], **({"acq": "yps"} if b == 0 else {"use": yx, "after": [yx]}))
+            yx = y if b == 0 else yx
+        ja, jv = list(range(JA[h], J)), list(range(JA[h]))
+        for x, j in enumerate(ja):
+            dx = P([mm(T.dif[:, 128 * a:128 * a + 128], A0("Ib"), H("y2", h, j + a, None, 16), True, False) if w == 0 else
+                    mm(T.dif[:, 128 * a:128 * a + 128], A0("Im"), ta(a), False, True) for a in range(4) for w in range(2)], 1024,
+                   YK("y2", h) + TK + ["Ib", "Im"], ["dif" + hs], acq="dif")
+            b = x
+            A(act(H("Ma", h, 512 * b, 512 * b + 512), T.dif[:, :], AF.Relu), 512, ["dif" + hs], ["Ma%s%d" % (hs, b)], use=dx)
+            P([mm(T.kb[:, j:104:13], H("Ma", h, 512 * b + 128 * a, 512 * b + 128 * a + 128), A0("G32"), False, False) for a in range(4)],
+              256, ["Ma%s%d" % (hs, b), "G32"], [], acc="K" + hs, use=kx)
+        for j in jv:
+            n = mcount[0] % NM
+            mcount[0] += 1
+            M = T["mb%d" % n]
+            V(tt(M[:, :, :], T.yps[:, :, j:j + 4], tl, Op.max), 512, ["yps%s%d" % (hs, b) for b in range(4)] + TK, ["mb%d" % n], use=yx)
+            P([mm(T.kb[:, j:104:13], M[:, :, a], A0("G32"), False, False) for a in range(4)], 256, ["mb%d" % n, "G32"], [], acc="K" + hs, use=kx)
+        V(scan(H("ks", h), A0("KD"), K, Op.max, Op.min), 104, ["K" + hs, "KD"], ["ks" + hs], use=kx)
+
+    def decide(t, h):
+        hs = str(h)
+        best = H("ks", h, 12, None, 13)
+        tie, dlt = H("Xs", h, 0, 128, 16), H("Xs", h, 128, 256, 16)
+        V(ts(tie, best, EARLY, None, Op.is_lt), 8, ["ks" + hs, "Xs" + hs], ["Xt" + hs])
+        V(scan(H("Xr", h, 0, 128), T.RD[:, 0:128], H("Xs", h, 0, 128), Op.mult, Op.add), 64, ["RD", "Xt" + hs], ["Xr" + hs])
+        V(ts(H("rr", h), best, MAGIC, MAGIC, Op.add, Op.subtract), 8, ["ks" + hs], ["rr" + hs])
+        V(tt(H("dd", h), H("rr", h), best, Op.subtract), 16, ["rr" + hs, "ks" + hs], ["dd" + hs])
+        V(tt(dlt, H("dd", h), tie, Op.mult), 16, ["dd" + hs, "Xt" + hs], ["Xd" + hs])
+        V(scan(H("Xr", h, 128, 256), T.RD[:, 0:128], H("Xs", h, 128, 256), Op.mult, Op.add), 64, ["RD", "Xd" + hs], ["Xe" + hs])
+
+    def fresh(t, h):
+        hs, c0 = str(h), 128 * h
+        X = T.vt[:, 256 * h:256 * h + 128]
+        Y = T.vt[:, 256 * h + 128:256 * h + 256]
+        dn, sn = "dg%d" % (t % 2), "st%d" % ((t + 1) % 2)
+        zk = "z%d%d" % (t, h)
+        if True:
+            tx = P([mm(T.sm[:, 0:128], A0("w7"), A0("cm16"), True, False), mm(T.sm[:, 0:128], H("Xr", h, 0, 128), A0("I16"), False, True),
+                    mm(T.sm[:, 128:256], H("Xr", h, 128, 256), A0("Ib"))], 384, ["w7", "cm16", "I16", "Ib", "Xr" + hs, "Xe" + hs], ["tz" + hs], acq="sm")
+            V(tt(Y, zref(t, h), T.sm[:, 0:128], Op.add), 128, [zk, "tz" + hs], ["vY" + hs], use=tx)
+            V(tt(H("dge", h), T.sm[:, 128:256], H("geb", h), Op.mult), 128, ["tz" + hs, "geb" + hs], ["dge" + hs], use=tx)
+            V(ts(H("zp", h), Y, 9.0, 9.0, Op.max, Op.add), 128, ["vY" + hs], ["zp" + hs])
+        V(tt(X, H("zp", h), T.sg[:, c0:c0 + 128], Op.subtract), 256, ["zp" + hs, "sg"], ["vX" + hs])
+        V(ts(H("cmp", h), X, 18.0, None, Op.is_ge), 128, ["vX" + hs], ["cmp" + hs])
+        V(tt(Y, X, H("dge", h), Op.subtract), 128, ["vX" + hs, "dge" + hs], ["vY" + hs])
+        V(tt(H("Hb", h), Y, T[dn][:, c0:c0 + 128], Op.mult), 128, ["vY" + hs, dn], ["Hb" + hs])
+        V(tt(T[sn][:, c0:c0 + 128], H("dge", h), T.sg[:, c0:c0 + 128], Op.add), 256, ["dge" + hs, "sg"], ["%s_%d" % (sn, h)])
+        select(t, h, "W0", 1)
+        samples(t, h, "v2")
+
+    def counts(t):
+        tx = P([mm(T.sm[:, 0:1], H("Xr", 0, 0, 128), T.c205[:, 0:1], True, False), mm(T.sm[:, 0:1], H("Xr", 1, 0, 128), T.c205[:, 0:1], False, True)],
+               128, ["Xr0", "Xr1", "c205"], ["Aps"], acq="sm")
+        V(cp(T.am[:, 4 * t:4 * t + 1], T.sm[:, 0:1]), 1, ["Aps"], ["am%d" % t], use=tx)
+        send(t, "A", None, T.al[:, 4 * t + 4:4 * t + 5], T.am[:, 4 * t:4 * t + 1], "am%d" % t)
+
+    def send(t, kind, h, out, in_, key):
+        sem = "r%s%d%s" % (kind, t + 1, "" if h is None else h)
+        rid, pid, mask = nxt
+
+        def fn(last):
+            return g.remote_dma(out, in_, T.sem[sem], T.sem.loc, pid, rid, mask)
+        i = add("q", [fn], 0.9, [key], [], pin=("send",))
+        add("n", [], 3.0, [], ["%s%d%s" % (kind, t + 1, "" if h is None else h)], after=[i], pin=(sem, gs["neng"]))
+
+    def finish(t, h):
+        hs = str(h)
+        ex = None
+        for b in range(4 if h in EY else 0):
+            e = P([mm(T.yps[:, 32 * b:32 * b + 32, :], A0("Ib"), H("v2", h, 512 * b + 1, 512 * b + 513), True, False),
+                   mm(T.yps[:, 32 * b:32 * b + 32, :], A0("Im"), H("v2", h, 512 * b, 512 * b + 512), False, True)], 1024,
+                  ["v2%s_%d" % (hs, k) for k in sorted({b * GP // 4, min(b + 1, 3) * GP // 4})] + ["v2p" + hs, "Ib", "Im"], ["yps%s%d" % (hs, b)],
+                  **({"acq": "yps"} if b == 0 else {"use": ex, "after": [ex]}))
+            ex = e if b == 0 else ex
+            A(act(T.Vb[:, 128 * h + 32 * b:128 * h + 32 * b + 32, :], T.yps[:, 32 * b:32 * b + 32, 3:15], AF.Abs), 384,
+              ["yps%s%d" % (hs, b)], ["Vb%s%d" % (hs, b)], use=ex)
+        for q in range(0 if h in EY else 3):
+            fns = []
+            for w in range(4):
+                m = 4 + 4 * q + w
+                fns += [mm(T.dif[:, 128 * w:128 * w + 128], A0("Ib"), H("v2", h, m, 2048, 16), True, False),
+                        mm(T.dif[:, 128 * w:128 * w + 128], A0("Im"), H("v2", h, m - 1, 2048, 16), False, True)]
+            dx = P(fns, 1024, YK("v2", h) + ["Ib", "Im"], ["dif" + hs], acq="dif")
+            A(act(H("Va", h, 512 * q, 512 * q + 512), T.dif[:, :], AF.Abs), 512, ["dif" + hs], ["Va%s%d" % (hs, q)], use=dx)
+        fns = [mm(T.sm[:, 0:104], A0("w7"), A0("cpad"), True, False)]
+        for w in range(12):
+            fns.append(mm(T.sm[:, 12 - w:104:13], T.Vb[:, 128 * h:128 * h + 128, w] if h in EY else H("Va", h, 128 * w, 128 * w + 128), A0("G1"),
+                          False, w == 11))
+        tx = P(fns, 104 + 768, ["w7", "cpad", "G1"] + (["Vb%s%d" % (hs, b) for b in range(4)] if h in EY else ["Va%s%d" % (hs, q) for q in range(3)]),
+               ["S" + hs], acq="sm")
+        A(act(H("nx", h), T.sm[:, 0:104], AF.Relu, 26256.0, -32.0), 104, ["S" + hs], ["nx" + hs], use=tx)
+        V(scan(H("ns", h), A0("ONE"), H("nx", h), Op.add, Op.min), 104, ["ONE", "nx" + hs], ["ns" + hs])
+        V(cp(H("Xn", h, 0, 128, 16), H("ns", h, 12, None, 13)), 8, ["ns" + hs, "Xn" + hs], ["Xn" + hs])
+        V(scan(H("Xnr", h), T.RD[:, 0:128], H("Xn", h), Op.mult, Op.add), 64, ["RD", "Xn" + hs], ["Xnr" + hs])
+        tx = P([mm(T.sm[:, 0:128], A0("w7"), A0("c3"), True, False), mm(T.sm[:, 0:128], H("Xnr", h), A0("Ib"), False, True)], 256,
+               ["w7", "c3", "Xnr" + hs, "Ib"], ["n" + hs], acq="sm")
+        a = A(act(H("nsb", h), T.sm[:, 0:128]), 128, ["n" + hs], ["nsb" + hs], use=tx)
+        zo = T.zm[:, 256 * t + 128 * h:256 * t + 128 * h + 128]
+        V(tt(zo, H("zp", h), T.sm[:, 0:128], Op.add), 128, ["zp" + hs, "n" + hs], ["zm%d%d" % (t, h)], use=tx, after=[a])
+        send(t, "z", h, T.zl[:, 256 * t + 128 * h:256 * t + 128 * h + 128], zo, "zm%d%d" % (t, h))
+        tx = P([mm(T.sm[:, 0:32], A0("Ih"), A0("Qc"), True, False)] +
+               [mm(T.sm[:, 0:32], T.Wu[:, 128 * u:128 * u + 128], H("nsb", h, u, None, 4), False, u == 3) for u in range(4)], 320,
+               ["Ih", "Qc", "nsb" + hs] + ["Wu%d" % u for u in range(4)], ["Q" + hs], acq="sm")
+        V(cp(H("tof", h), T.sm[:, 0:32]), 32, ["Q" + hs], ["tof" + hs], use=tx)
+        to = T.ts[:, 1024 * t + 512 * h:1024 * t + 512 * h + 512]
+        A(act(to, H("v2", h, 0, 2048).indirect(H("tof", h))), 512 * 1.5, YK("v2", h) + ["tof" + hs], ["ts%d%d" % (t, h)])
+        send(t, "T", h, T["tl%d" % (t + 1)][:, 128 * h:128 * h + 128, :], to, "ts%d%d" % (t, h))
+
+    for t in range(NV):
+        tag[0] = ("L", 0, t)
+        gatherlist(t)
+        for h in range(2):
+            tag[0] = ("F", h, t)
+            front(t, h)
+        for h in range(2):
+            tag[0] = ("H", h, t)
+            heavy(t, h)
+            tag[0] = ("D", h, t)
+            decide(t, h)
+        if t < NV - 1:
+            tag[0] = ("C", 0, t)
+            counts(t)
+        for h in range(2):
+            tag[0] = ("N", h, t)
+            fresh(t, h)
+            tag[0] = ("E", h, t)
+            finish(t, h)
+    tag[0] = ("O", 0, 0)
+
+    st = "st%d" % (NV % 2)
+    V(ts(A0("li"), A0("LF"), T.al[:, 4 * NV - 4:4 * NV - 3], None, Op.subtract), 16, ["LF", "A%d" % (NV - 1)], ["li"])
+    C(ts(A0("lm"), A0("li"), 255, None, Op.bitwise_and), 16, ["li"], "lm")
+    C(cp(A0("lu"), A0("lm")), 16, ["lm"], "lu")
+    A(act(A0("ysb"), T[st][:, :].indirect(T.lu[:, :])), 256 * 1.5, ["lu", st + "_0", st + "_1"], ["ysb"])
+
+    def store(out, in_, rd):
+        add("d", [lambda last: gs["d"].dma_start(out, in_)], 2.0, rd, [], pin=("sto", 16))
+    store(T.ys[:, :], T.ysb[:, :], ["ysb"])
+    for h in range(2):
+        c = 256 * (NV - 1) + 128 * h
+        V(ts(T.zb[:, 128 * h:128 * h + 128], T.zl[:, c:c + 128], -9.0, None, Op.add), 128, ["z%d%d" % (NV, h)], ["z0%d" % h])
+        store(T.yz[:, 128 * h:128 * h + 128], T.zb[0:128:16, 128 * h:128 * h + 128], ["z0%d" % h])
+    fin = []
+    for h in range(2):
+        for a in range(4):
+            src = T["tl%d" % NV][:, 128 * h:128 * h + 128, a]
+            dst = T.ytb[:, 256 * a + 128 * h:256 * a + 128 * h + 128]
+            key = "yt%d%d" % (h, a)
+            fin.append(key)
+            if a < 2:
+                V(cp(dst, src), 64, ["T%d%d" % (NV, h)], [key])
+            else:
+                A(act(dst, src), 128, ["T%d%d" % (NV, h)], [key])
+    store(T.yt[:, :], T.ytb[:, :], fin)
+    return ops
+
+
+def schedule(ops):
+    n = len(ops)
+    succ = [[] for _ in range(n)]
+    for i, o in enumerate(ops):
+        for d in o["deps"]:
+            succ[d].append(i)
+    pr = [0.0] * n
+    for i in range(n - 1, -1, -1):
+        pr[i] = ops[i]["cost"] + 0.04 + max([pr[k] for k in succ[i]], default=0.0)
+    pr = [pr[i] + ops[i]["bonus"] for i in range(n)]
+    left = [len(o["deps"]) for o in ops]
+    members = {}
+    for i, o in enumerate(ops):
+        if o["use"] is not None:
+            members.setdefault(o["use"], []).append(i)
+    ready = {e: [] for e in "vapqdn"}
+    for i in range(n):
+        if left[i] == 0:
+            ready[ops[i]["eng"]].append(i)
+    free = {e: 0.0 for e in "vapqdn"}
+    end, order, holder, pend = [0.0] * n, [], {}, {}
+    dep_end = [0.0] * n
+    while len(order) < n:
+        best = None
+        for e in "vapqdn":
+            cand = []
+            for i in ready[e]:
+                o = ops[i]
+                b = o["acq"]
+                est = dep_end[i]
+                if b is not None and b in holder:
+                    tx = holder[b]
+                    if pend[tx] > 0:
+                        continue
+                    est = max(est, max(end[m] for m in members[tx]) + 0.04)
+                if e in "vapq":
+                    est = max(est, free[e])
+                cand.append((est, i))
+            if not cand:
+                continue
+            lo = min(c[0] for c in cand) + WIN
+            est, i = max((c for c in cand if c[0] <= lo), key=lambda c: pr[c[1]])
+            if best is None or est < best[0]:
+                best = (est, i, e)
+        est, i, e = best
+        o = ops[i]
+        ready[e].remove(i)
+        if o["acq"] is not None:
+            b = o["acq"]
+            if b in holder:
+                for m in members[holder[b]]:
+                    o["deps"].setdefault(m, False)
+            holder[b] = i
+            pend[i] = len(members[i])
+        if o["use"] is not None:
+            pend[o["use"]] -= 1
+        end[i] = est + o["cost"]
+        if e in "vapq":
+            free[e] = end[i]
+        order.append((est, i))
+        for k in succ[i]:
+            left[k] -= 1
+            dep_end[k] = max(dep_end[k], end[i] + 0.04)
+            if left[k] == 0:
+                ready[ops[k]["eng"]].append(k)
+    return [i for _, i in order], end
+
+
+def emit(ops, order, T, gs):
+    lastacc = {}
+    for i in order:
+        if ops[i]["eng"] == "p" and ops[i]["use"] is not None:
+            lastacc[ops[i]["use"]] = i
+    count = {}
+    done = {}
+    know = {e: {} for e in "vapqd"}
+
+    def after(e, i, raw):
+        o = ops[i]
+        sem, val, clk = done[i]
+        if o["eng"] == e == "p" and not raw:
+            return
+        if know[e].get(sem, 0) >= val:
+            return
+        gs[e].wait_ge(T.sem[sem], val)
+        for k, w in clk.items():
+            if know[e].get(k, 0) < w:
+                know[e][k] = w
+        know[e][sem] = max(val, know[e].get(sem, 0))
+    for i in order:
+        o = ops[i]
+        e = o["eng"]
+        if e == "n":
+            done[i] = (o["sym"][0], o["sym"][1], {})
+            continue
+        ds = sorted(o["deps"].items(), key=lambda d: -done[d[0]][1] if d[0] in done else 0)
+        for d, raw in ds:
+            after(e, d, raw)
+        for x, fn in enumerate(o["fns"]):
+            last = e == "p" and lastacc.get(o["use"]) == i and x == len(o["fns"]) - 1
+            c = fn(last)
+            if e in "vap" or (e == "q" and o["sym"] is None):
+                c.then_inc(T.sem[e], 1)
+                count[e] = count.get(e, 0) + 1
+            elif e == "d":
+                sem, add = o["sym"]
+                c.then_inc(T.sem[sem], add)
+                count[sem] = count.get(sem, 0) + add
+            else:
+                count["loc"] = count.get("loc", 0) + gs["neng"]
+        sem = e if e in "vap" or (e == "q" and o["sym"] is None) else ("loc" if e == "q" else o["sym"][0])
+        done[i] = (sem, count[sem], dict(know[e]))
+    gs["d"].wait_ge(T.sem.sto, count["sto"])
+    for sem in ("v", "a", "p", "q", "loc"):
+        gs["q"].wait_ge(T.sem[sem], count[sem])
+
+
+def rank_program(g, core, T, topo):
+    rank = T.rank_of(core)
+    if rank is None:
+        return
+    dst = T.cores[(rank + 1) % len(T.cores)]
+    rid, pid, _ = topo.addr(dst)
+    gs = {"v": g.vector, "a": g.scalar, "p": g.tensor, "q": g, "d": g.sync, "neng": len(topo.engines(core, dst))}
+    ops = build(T, gs, (rid, pid, topo.mask(core, dst)))
+    order, _ = schedule(ops)
+    emit(ops, order, T, gs)

@@ -3,70 +3,81 @@ from concourse.mybir import dt, AluOpType as Op, ActivationFunctionType as AF
 
 NV = 8
 J = 13
-JA = (11, 11)
-NM = 4
-GP = 4
-EY = (0, 1)
-VG = (("v2", 1, 1), ("y2", 0, 1), ("y2", 0, 3), ("v2", 1, 3))
-VG0, VGL = VG, VG
-WIN = 0.02
-BONUS = {("F", 0): -96.8, ("H", 0): -145.4, ("D", 0): 78.0, ("N", 0): 229.2, ("E", 0): -208.8, ("L", 0): 199.4, ("C", 0): -76.6,
-         ("F", 1): -136.4, ("H", 1): -204.6, ("D", 1): -162.2, ("N", 1): 211.4, ("E", 1): -111.2}
-OPB = {}
+PRM = dict(
+    JA=(11, 11),
+    NS=(2, 2),
+    SB=(1, 1),
+    NM=4,
+    XP=4,
+    WIN=0.02,
+    ENG={},
+    BONUS={},
+)
+PRM.update({'JA': (8, 10), 'NS': (2, 4), 'NM': 4, 'XP': 4, 'WIN': 0.02, 'ENG': {('Dc', 0): 'v', ('v23', 1): 'va', ('y22', 0): 'va', ('gC', 1): 'va', ('v21', 1): 'va', ('v22', 1): 'v', ('gT', 1): 'va', ('y21', 1): 'va'}, 'BONUS': {('ysum', 0): -0.5, ('E', 1): -16.0, ('L', 0): 16.0, ('dif', 0): 4.0, ('F', 0): 1.0, ('H', 0): 0.5, ('T', 1): -0.5}, 'SUMAFT': 2, 'SB': (2, 2), 'DUP': 1})
+PRM.update({'JA': (11, 13), 'NS': (2, 4), 'SB': (1, 1), 'NM': 6, 'XP': 4, 'WIN': 0.02, 'ENG': {('Dc', 0): 'v', ('v23', 1): 'va', ('y22', 0): 'va', ('gC', 1): 'va', ('v21', 1): 'va', ('v22', 1): 'v', ('gT', 1): 'va', ('y21', 1): 'va', ('geb', 1): 'a', ('gT', 0): 'a'}, 'BONUS': {('ysum', 0): -0.5, ('E', 1): -8.0, ('L', 0): 0.0, ('dif', 0): 4.0, ('F', 0): 2.0, ('H', 0): 1.0, ('T', 1): -0.5, ('C', 0): 2.0, ('D', 0): -8.0, ('H', 1): 0.5, ('L', 1): -16.0}, 'SUMAFT': 2, 'DUP': 0})
+PRM.update({'JA': (8, 9), 'NS': (1, 2), 'NM': 6, 'XP': 4, 'WIN': 0.02, 'ENG': {('Dc', 0): 'va', ('v23', 1): 'va', ('y22', 0): 'va', ('gC', 1): 'a', ('v21', 1): 'v', ('v22', 1): 'v', ('gT', 1): 'va', ('y21', 1): 'va', ('geb', 1): 'va', ('ind', 1): 'a', ('gT', 0): 'v', ('gC', 0): 'a', ('Dc', 1): 'a'}, 'BONUS': {('ysum', 0): -1.5, ('E', 1): -15.0, ('L', 0): 8.0, ('dif', 0): 4.0, ('F', 0): 3.0, ('H', 0): 0.5, ('T', 1): -0.5, ('T', 0): -8.0, ('ysum', 1): -0.5, ('S', 1): 2.0, ('L', 1): 15.5, ('N', 1): -8.0, ('H', 1): -1.0, ('dif', 1): -0.5, ('C', 0): -16.0}, 'SUMAFT': 0, 'SB': (2, 2)})
+PRM.update({'JA': (11, 10), 'NS': (0, 3), 'SB': (2, 2), 'NM': 5, 'XP': 4, 'WIN': 0.02, 'ENG': {('v21', 1): 'v', ('y20', 0): 'va', ('gT', 0): 'va'}, 'BONUS': {('L', 0): -1.0, ('N', 1): -8.0, ('C', 0): 2.0, ('E', 0): -2.0}, 'SUMAFT': 0, 'FAST': (1, 0)})
+PRM.update({'JA': (10, 8), 'NS': (2, 4), 'SB': (2, 2), 'NM': 4, 'XP': 4, 'WIN': 0.0, 'ENG': {'y20': 'va', 'y21': 'va', 'y22': 'va', 'y23': 'va', 'v20': 'va', 'v21': 'va', 'v22': 'va', 'v23': 'va', ('gT', 1): 'a', ('y22', 1): 'v', ('y20', 0): 'v', ('gC', 0): 'a', ('v22', 0): 'v', ('ind', 0): 'a', ('v23', 0): 'a', ('gT', 0): 'v', ('v20', 0): 'a', ('v20', 1): 'a', ('y22', 0): 'v'}, 'BONUS': {('G', 0): -6.0, ('F', 0): -1.0, ('L', 0): -4.0, ('D', 0): 0.5, ('D', 1): 14.0, ('S', 0): -19.5, ('H', 1): -1.0, ('G', 1): 4.0, ('T', 0): 16.0, ('N', 0): 0.5, ('N', 1): -0.5, ('E', 0): -0.5, ('S', 1): -0.5, ('T', 1): 0.5, ('H', 0): -0.5}, 'SUMAFT': 1, 'DUP': 0, 'FAST': (1, 0)})
+CYC, PEC, HOP, OWN = 0.00083, 0.00042, 0.22, 0.01
 MAGIC = 201326592.0
-EARLY, LATE = 37528.0, 1.0e9
+FAKE = 32.0 * 2344 + 16
+ZC = 1600.0
 
 F32, BF, F16, I32, U16 = "float32", "bfloat16", "float16", "int32", "uint16"
 SCRATCH = {
-    "x": ("sbuf", [128, 4096], BF), "t0s": ("sbuf", [128, 1024], BF), "ytb": ("sbuf", [128, 1024], BF),
+    "t0s": ("sbuf", [128, 1024], BF), "ytb": ("sbuf", [128, 1024], BF),
     "s0s": ("sbuf", [128, 256], I32), "cfs": ("sbuf", [128, 256], I32), "z0s": ("sbuf", [8, 256], I32), "z0f": ("sbuf", [8, 256], F32),
-    "st0": ("sbuf", [128, 256], F32), "st1": ("sbuf", [128, 256], F32), "sg": ("sbuf", [128, 256], F32),
-    "dg0": ("sbuf", [128, 256], F32), "dg1": ("sbuf", [128, 256], F32), "ysb": ("sbuf", [128, 256], F32),
-    "zb": ("sbuf", [128, 256], F32), "zl": ("sbuf", [128, 8 * 256], F32), "zm": ("sbuf", [128, 8 * 256], F32),
-    "al": ("sbuf", [128, 64], F32), "am": ("sbuf", [128, 64], F32),
+    "s0f": ("sbuf", [128, 256], F32), "c0f": ("sbuf", [128, 256], F32), "sg": ("sbuf", [128, 256], F32),
+    "CG": ("sbuf", [128, NV, 272], F32), "CL": ("sbuf", [128, NV, 272], F32),
+    "SN": ("sbuf", [128, NV, 256], F32), "SL": ("sbuf", [128, NV, 256], F32),
+    "ysb": ("sbuf", [128, 256], F32), "zb": ("sbuf", [128, 256], F32),
     "li": ("sbuf", [128, 16], I32), "lm": ("sbuf", [128, 16], I32), "lu": ("sbuf", [128, 16], U16),
     "iP": ("sbuf", [128, 128], I32), "iQ": ("sbuf", [128, 128], I32), "iC": ("sbuf", [128, 104], I32), "iJ": ("sbuf", [128, 104], I32),
     "iL": ("sbuf", [128, 16], I32), "i64": ("sbuf", [128, 32], I32),
     "pg": ("sbuf", [128, 128], I32), "qg": ("sbuf", [128, 128], I32), "pm": ("sbuf", [128, 128], I32), "qm": ("sbuf", [128, 128], I32),
-    "sh": ("sbuf", [128, 32], I32), "q1": ("sbuf", [128, 32], I32), "q2": ("sbuf", [128, 32], I32), "l5": ("sbuf", [128, 16], I32),
-    "w9": ("sbuf", [128, 128], F32), "w18": ("sbuf", [128, 128], F32), "mu": ("sbuf", [128, 32], F32), "shf": ("sbuf", [128, 8], F32),
-    "gf": ("sbuf", [128, 8], F32), "gr": ("sbuf", [128, 104], F32), "sg1": ("sbuf", [128, 104], F32), "sg2": ("sbuf", [128, 104], F32),
-    "B32": ("sbuf", [128, 128], F32), "Bb": ("sbuf", [128, 128], BF), "Ib": ("sbuf", [128, 128], BF), "I16": ("sbuf", [128, 128], BF),
-    "Im": ("sbuf", [128, 128], BF), "Ih": ("sbuf", [128, 128], F16), "W0": ("sbuf", [128, 128], F16), "W1": ("sbuf", [128, 128], F16),
-    "Wu": ("sbuf", [128, 512], BF), "G1": ("sbuf", [128, 8], BF), "G32": ("sbuf", [128, 8], BF), "Z": ("sbuf", [128, 8, 32], BF),
-    "RT0": ("sbuf", [128, 104], BF), "RT1": ("sbuf", [128, 104], BF), "cj": ("sbuf", [128, 104], BF), "cpad": ("sbuf", [128, 104], BF), "KD": ("sbuf", [128, 104], F32),
-    "ONE": ("sbuf", [128, 104], F32), "RD": ("sbuf", [128, 128], BF), "Qc": ("sbuf", [128, 32], F16), "rp1": ("sbuf", [128, 8], F32),
-    "LB": ("sbuf", [128, 16], F32), "LF": ("sbuf", [128, 16], F32), "R8": ("sbuf", [8, 128], F32),
-    "w7": ("sbuf", [128, 128], BF), "c185": ("sbuf", [128, 128], BF), "cm16": ("sbuf", [128, 128], BF), "c3": ("sbuf", [128, 128], BF),
-    "c205": ("sbuf", [128, 8], BF),
-    "yps": ("psum", [128, 128, 16], F32), "dif": ("psum", [128, 512], F32), "vt": ("psum", [128, 512], F32),
-    "kb": ("psum", [128, 512], F32), "sm": ("psum", [128, 512], F32),
+    "l5": ("sbuf", [128, 16], I32), "LB": ("sbuf", [128, 16], F32), "LF": ("sbuf", [128, 16], F32),
+    "E": ("sbuf", [128, 16], F32), "vec": ("sbuf", [128, 32], F32), "gf": ("sbuf", [128, 8], F32),
+    "B32": ("sbuf", [128, 128], F32), "Bb": ("sbuf", [128, 128], BF), "Ib": ("sbuf", [128, 128], BF), "Im": ("sbuf", [128, 128], BF),
+    "Ih": ("sbuf", [128, 128], F16), "R8": ("sbuf", [8, 128], F32), "R8n": ("sbuf", [8, 128], F32),
+    "Wx": ("sbuf", [128, 144], BF), "Wn": ("sbuf", [128, 144], F32), "Wc": ("sbuf", [128, 144], F16), "Wq": ("sbuf", [128, 144], BF),
+    "Wu": ("sbuf", [128, 128], F16), "Wz1": ("sbuf", [128, 128], F16), "Wz": ("sbuf", [128, 128], F32), "Wp": ("sbuf", [128, 128], BF),
+    "Wy": ("sbuf", [128, 128], F32), "Wv": ("sbuf", [128, 128], F32), "tm1": ("sbuf", [128, 128], F32), "tm2": ("sbuf", [128, 128], F32),
+    "Wd": ("sbuf", [128, 128], F16), "Wf": ("sbuf", [128, 128], F16), "Wk": ("sbuf", [128, 128], F16), "Wm": ("sbuf", [128, 128], F16),
+    "Bn": ("sbuf", [128, 128], F32),
+    "tm3": ("sbuf", [128, 128], F32), "tm4": ("sbuf", [128, 128], F32),
+    "G64": ("sbuf", [128, 8], BF), "Z": ("sbuf", [128, 8, 32], BF), "gr": ("sbuf", [128, 104], F32), "sg1": ("sbuf", [128, 104], F32),
+    "sg2": ("sbuf", [128, 104], F32), "RT0": ("sbuf", [128, 104], BF), "RT1": ("sbuf", [128, 104], BF), "cj": ("sbuf", [128, 104], BF),
+    "kd": ("sbuf", [128, 104], F32), "KD": ("sbuf", [128, 104], F32), "RD": ("sbuf", [128, 256], BF), "w7": ("sbuf", [128, 128], BF),
+    "c205": ("sbuf", [128, 8], BF), "sh": ("sbuf", [128, 32], I32), "q1": ("sbuf", [128, 32], I32), "q2": ("sbuf", [128, 32], I32),
+    "Qc": ("sbuf", [128, 32], F16),
+    "yps": ("psum", [128, 128, 16], F32), "kb": ("psum", [128, 512], F32),
+    "pb0": ("psum", [128, 512], F32), "pb1": ("psum", [128, 512], F32), "pb2": ("psum", [128, 512], F32),
 }
-_HALF = {"cmp": (128, BF), "geb": (128, BF), "Hb": (128, F32), "oH": (128, F32), "oD": (128, F16), "fi": (128, I32), "fm": (128, I32),
-         "of": (128, U16), "y2": (2048, BF), "v2": (2064, BF), "Va": (1536, BF), "ks": (104, F32), "rr": (8, F32), "dd": (8, F32),
-         "Xs": (256, BF), "Xr": (256, BF), "dge": (128, F32), "zp": (128, F32), "nx": (104, F32), "ns": (104, F32), "Xn": (128, BF),
-         "Xnr": (128, BF), "nsb": (128, BF), "tof": (32, U16), "Ma": (512 * (J - min(JA)), BF)}
+POOL = ("pb0", "pb1", "pb2")
+for _d in range(4):
+    SCRATCH["x%d" % _d] = ("sbuf", [128, 4096], BF)
+    SCRATCH["j%d" % _d] = ("sbuf", [128, 4096], BF)
+_HALF = {"cmp": (256, BF), "geb": (128, BF), "ze": (128, F16), "oS": (256, F32), "oC": (256, F16), "Dc": (128, F32), "Hb": (128, F32), "Left": (128, F32),
+         "prod": (128, F32), "fi": (128, I32), "fm": (128, I32), "of": (128, U16), "y2": (2048, BF), "v2": (2048, BF), "Va": (1536, BF),
+         "ks": (104, F32), "rr": (8, F32), "Xs": (256, BF), "Xr": (256, BF), "r1": (128, BF), "ind": (128, BF), "tof": (32, U16),
+         "tb": (512, BF), "Ma": (512 * 6, BF)}
 for _n, (_c, _d) in _HALF.items():
     SCRATCH[_n] = ("sbuf", [128, 2 * _c], _d)
-for _m in range(NM):
-    SCRATCH["mb%d" % _m] = ("sbuf", [128, 128, 4], BF)
-SCRATCH["Vb"] = ("sbuf", [128, 256, 12], BF)
-SCRATCH["ts"] = ("sbuf", [128, NV * 1024], BF)
-for _t in range(NV + 1):
-    SCRATCH["tl%d" % _t] = ("sbuf", [128, 256, 4], BF)
-SEMAPHORES = ["v", "a", "p", "q", "lx", "ls", "lc", "lz", "lt", "loc", "sto"]
-for _t in range(1, NV + 1):
-    SEMAPHORES += ["rA%d" % _t, "rz%d0" % _t, "rz%d1" % _t, "rT%d0" % _t, "rT%d1" % _t]
-SEMAPHORES.remove("rA%d" % NV)
+for _m in range(6):
+    SCRATCH["mb%d" % _m] = ("sbuf", [128, 512], BF)
+SEMAPHORES = ["v", "a", "p", "q", "ls", "lc", "lz", "lt", "loc", "sto"] + ["lx%d" % _k for _k in range(4)]
+for _t in range(NV):
+    SEMAPHORES += ["rC%d" % _t, "rS%d0" % _t, "rS%d1" % _t]
+SEMAPHORES += ["rX%d%d" % (_d, _k) for _d in range(1, 4) for _k in range(8)]
 
 
-def build(T, gs, nxt):
-    ops, lastw, readers, accs, nums, tag = [], {}, {}, {}, {}, [("I", 0, 0)]
+def build(T, gs, to, prm):
+    ops, lastw, readers, accs, tag = [], {}, {}, {}, [("I", 0, 0)]
+    JA, NS, NM, XP = prm["JA"], prm["NS"], prm["NM"], prm["XP"]
 
-    def add(eng, fns, cost, rd=(), wr=(), acc=None, acq=None, use=None, after=(), pin=None):
+    def add(fns, cost, rd=(), wr=(), acc=None, acq=None, use=None, after=(), pin=None, name=""):
         i = len(ops)
         deps = {}
-        nums[tag[0]] = nums.get(tag[0], -1) + 1
         for k in rd:
             for o in ([lastw[k]] if k in lastw else []) + accs.get(k, []):
                 deps[o] = True
@@ -82,69 +93,117 @@ def build(T, gs, nxt):
         for o in after:
             deps[o] = deps.get(o, False)
         if acq is not None:
-            use = i
-        ops.append(dict(eng=eng, fns=fns, cost=cost, deps=deps, acq=acq, use=use, sym=pin, bonus=BONUS.get(tag[0][:2], 0.0) + OPB.get(tag[0][:2] + (nums[tag[0]],), 0.0), tag=tag[0], num=nums[tag[0]], wr=tuple(wr)))
+            acq["first"] = i
+            use = acq
+        ops.append(dict(fns=fns, cost=cost, deps=deps, acq=acq, use=use, sym=pin, acc=acc, tag=tag[0], name=name,
+                        bonus=prm["BONUS"].get(tag[0][:2], 0.0) + prm["BONUS"].get((name, tag[0][1]), 0.0)))
         return i
 
     v, s, p, g = gs["v"], gs["a"], gs["p"], gs["q"]
 
+    def VA(fv, cv, fa, ca, rd=(), wr=(), dflt="va", **kw):
+        e = prm["ENG"].get((kw.get("name"), tag[0][1]), prm["ENG"].get(kw.get("name"), dflt))
+        fns, cost = {}, {}
+        if fv is not None and ("v" in e or fa is None):
+            fns["v"], cost["v"] = [fv], 0.01 + max(64, cv) * CYC
+        if fa is not None and ("a" in e or fv is None):
+            fns["a"], cost["a"] = [fa], 0.065 + ca * CYC
+        return add(fns, cost, rd, wr, **kw)
+
     def V(fn, c, rd=(), wr=(), **kw):
-        return add("v", [fn], 0.05 + max(64, c) * 0.001, rd, wr, **kw)
+        return VA(fn, c, None, 0, rd, wr, **kw)
 
     def A(fn, c, rd=(), wr=(), **kw):
-        return add("a", [fn], 0.065 + c * 0.001, rd, wr, **kw)
+        return VA(None, 0, fn, c, rd, wr, **kw)
 
     def P(fns, c, rd=(), wr=(), **kw):
-        return add("p", fns, c * 0.0005, rd, wr, **kw)
+        return add({"p": fns}, {"p": c * PEC}, rd, wr, **kw)
+
+    def ap(x):
+        return T[x[0]["bank"]][x[1]] if isinstance(x, tuple) else x
+
+    def pb(cell, a, b, step=1, rows=128):
+        return (cell, (slice(0, rows), slice(a, b, step)))
 
     def mm(out, l, r, start=True, stop=True):
-        return lambda last: p.matmul(out, l, r, start, stop or last)
+        return lambda last: p.matmul(ap(out), l, r, start, stop or last)
 
     def ts(out, a, s1, s2, o0, o1=None):
         if o1 is None:
-            return lambda last: v.tensor_scalar(out, a, s1, None, o0)
-        return lambda last: v.tensor_scalar(out, a, s1, s2, o0, o1)
+            return lambda last: v.tensor_scalar(ap(out), ap(a), ap(s1), None, o0)
+        return lambda last: v.tensor_scalar(ap(out), ap(a), ap(s1), ap(s2), o0, o1)
 
     def tt(out, a, b, o):
-        return lambda last: v.tensor_tensor(out, a, b, o)
+        return lambda last: v.tensor_tensor(ap(out), ap(a), ap(b), o)
 
     def cp(out, a):
-        return lambda last: v.tensor_copy(out, a)
+        return lambda last: v.tensor_copy(ap(out), ap(a))
 
     def act(out, a, f=AF.Copy, bias=0.0, scale=1.0):
-        return lambda last: s.activation(out, a, f, bias=bias, scale=scale)
+        return lambda last: s.activation(ap(out), ap(a), f, bias=bias, scale=scale)
 
     def scan(out, a, b, o0, o1):
         return lambda last: v.tensor_tensor_scan(out, a, b, 0.0, o0, o1)
 
-    def load(out, a, sem, key, lat, after=()):
-        return add("d", [lambda last: gs["d"].dma_start(out, a)], lat, (), [key], pin=(sem, 16), after=after)
+    def ms(out, val):
+        return lambda last: v.memset(out, val)
+
+    def load(q, out, a, sem, key, lat):
+        i = add({q: [lambda last: gs[q].dma_start(out, a)]}, {q: 0.05}, (), [key], pin=("dma", sem, lat))
+        ops[i]["bonus"] = 1000.0 - 10.0 * i
+        return i
+
+    def send(d, out, in_, sem, rd, key, lat, after=()):
+        rid, pid, mask = to[d]
+        i = add({"q": [lambda last: g.remote_dma(out, in_, T.sem[sem], T.sem.loc, pid, rid, mask)]}, {"q": 0.6}, rd, [], pin=("send",), after=after)
+        add({"n": []}, {"n": lat}, [], [key], after=[i], pin=("land", sem, gs["neng"]))
+        return i
 
     def H(name, h, a=0, b=None, step=None):
         n = _HALF[name][0]
         return T[name][:, n * h + a: n * h + (n if b is None else b): (step or 1)]
 
-    load(T.z0s[:, :], T.z0[:, :], "lz", "z0s", 2.5)
-    load(T.s0s[:, :], T.s0[:, :], "ls", "s0s", 3.0)
-    load(T.cfs[:, :], T.cf[:, :], "lc", "cfs", 3.5)
-    load(T.x[:, :], T.xl[:, :], "lx", "x", 9.0)
-    load(T.t0s[:, :], T.t0[:, :], "lt", "t0s", 10.0)
+    def gather(out, win, off, n, rd, wr, name, dflt="va", bias=None):
+        if bias is None:
+            VA(cp(out, win.indirect(off)), n * 1.5, act(out, win.indirect(off)), n * 1.5, rd, wr, name=name, dflt=dflt)
+        else:
+            VA(ts(out, win.indirect(off), bias, None, Op.add), n * 1.5, act(out, win.indirect(off), AF.Identity, bias), n * 1.5, rd, wr, name=name, dflt=dflt)
+
+    load("d", T.z0s[:, :], T.z0[:, :], "lz", "z0s", 2.2)
+    load("d", T.s0s[:, :], T.s0[:, :], "ls", "s0s", 2.6)
+    load("d", T.cfs[:, :], T.cf[:, :], "lc", "cfs", 3.0)
+    for k in range(2):
+        load("d", T.x0[:, 2048 * k:2048 * k + 2048], T.xl[:, 2048 * k:2048 * k + 2048], "lx%d" % k, "x0_%d" % k, 5.5 + 2.5 * k)
+    load("d", T.t0s[:, :], T.t0[:, :], "lt", "t0s", 9.0)
+    xw = 4096 // XP
+    XK = {0: ["x0_0", "x0_1"]}
+
+    def sendlog(d, after):
+        XK[d] = []
+        for k in range(XP):
+            send(d, T["x%d" % d][:, xw * k:xw * k + xw], T.x0[:, xw * k:xw * k + xw], "rX%d%d" % (d, k), ["x0_%d" % (xw * k // 2048), "x0_%d" % ((xw * k + xw - 1) // 2048)],
+                 "x%d_%d" % (d, k), 2.0 + 10.0 * (k + 1) / XP, after)
+            XK[d].append("x%d_%d" % (d, k))
+            if prm.get("DUP"):
+                send(d, T["j%d" % d][:, xw * k:xw * k + xw], T.x0[:, xw * k:xw * k + xw], "rX%d%d" % (d, k + 4), ["x0_0", "x0_1"], "j%d_%d" % (d, k), 2.0 + 10.0 * (k + 1) / XP, after)
+                XK[d].append("j%d_%d" % (d, k))
+    sendlog(1, ())
 
     def iota(name, pat, base, cm):
-        add("q", [lambda last: g.iota(T[name][:, :], pat, base, cm)], 0.4, (), [name])
+        add({"q": [lambda last: g.iota(T[name][:, :], pat, base, cm)]}, {"q": 0.35}, (), [name])
     iota("iP", [[0, 128]], 0, 1)
     iota("iQ", [[1, 128]], 0, 0)
     iota("iL", [[16, 16]], 0, 0)
     iota("iC", [[1, 8], [0, 13]], 0, 0)
     iota("iJ", [[0, 8], [1, 13]], 0, 0)
-    iota("i64", [[64, 32]], 6, 0)
+    iota("i64", [[64, 32]], -4, 0)
+    A0 = lambda n, a=0, b=None: T[n][:, a:b] if b is not None else T[n][:, :]
 
     def C(fn, c, rd, wr):
         return V(fn, c, rd, [wr])
 
-    def fill(name, val, c):
-        C(lambda last: v.memset(T[name][:, :], val) if name != "Z" else v.memset(T.Z[:, :, :], val), c, [], name)
-    A0 = lambda n, a=0, b=None: T[n][:, a:b] if b is not None else T[n][:, :]
+    def scaled(out, a, col, rd, wr, n):
+        VA(ts(out, a, col, None, Op.mult), n, act(out, a, AF.Identity, 0.0, col), n, rd, [wr])
     C(ts(A0("pm"), A0("iP"), 15, None, Op.bitwise_and), 128, ["iP"], "pm")
     C(tt(A0("LB"), A0("iL"), A0("pm", 0, 16), Op.add), 16, ["iL", "pm"], "LB")
     C(ts(A0("l5"), A0("LB"), 5.0, None, Op.mult), 16, ["LB"], "l5")
@@ -152,376 +211,406 @@ def build(T, gs, nxt):
     C(ts(A0("qg"), A0("iQ"), 4, None, Op.arith_shift_right), 128, ["iQ"], "qg")
     C(ts(A0("pg"), A0("iP"), 4, None, Op.arith_shift_right), 128, ["iP"], "pg")
     C(ts(A0("qm"), A0("iQ"), 15, None, Op.bitwise_and), 128, ["iQ"], "qm")
-    C(ts(T.rp1[:, 0:1], T.pm[:, 0:1], 1.0, None, Op.add), 1, ["pm"], "rp1")
     C(tt(A0("B32"), A0("pg"), A0("qg"), Op.is_equal), 256, ["pg", "qg"], "B32")
     C(tt(T.R8[:, :], T.iP[0:8, :], T.qg[0:8, :], Op.is_equal), 256, ["iP", "qg"], "R8")
-    A(act(A0("Bb"), A0("B32")), 128, ["B32"], ["Bb"])
+    scaled(T.R8n[:, :], T.R8[:, :], -1.0, ["R8"], "R8n", 128)
+    scaled(A0("Bb"), A0("B32"), 1.0, ["B32"], "Bb", 128)
     C(tt(A0("Ib"), A0("iP"), A0("iQ"), Op.is_equal), 256, ["iP", "iQ"], "Ib")
-    A(act(A0("I16"), A0("Ib"), scale=16.0), 128, ["Ib"], ["I16"])
-    A(act(A0("Im"), A0("Ib"), scale=-1.0), 128, ["Ib"], ["Im"])
-    C(cp(A0("Ih"), A0("Ib")), 64, ["Ib"], "Ih")
-    C(ts(A0("w9"), A0("qm"), 0.5, None, Op.add), 128, ["qm"], "w9")
-    C(tt(A0("W0"), A0("w9"), A0("B32"), Op.mult), 256, ["w9", "B32"], "W0")
+    scaled(A0("Im"), A0("Ib"), -1.0, ["Ib"], "Im", 128)
+    scaled(A0("Ih"), A0("Ib"), 1.0, ["Ib"], "Ih", 128)
     C(tt(A0("gf"), T.pg[:, 0:8], T.iQ[:, 0:8], Op.is_equal), 16, ["pg", "iQ"], "gf")
-    C(cp(A0("G1"), A0("gf")), 8, ["gf"], "G1")
-    C(ts(A0("G32"), A0("gf"), 32.0, None, Op.mult), 8, ["gf"], "G32")
-    fill("Z", 0.0, 256)
+    C(tt(A0("E"), T.pm[:, 0:16], T.iQ[:, 0:16], Op.is_equal), 32, ["pm", "iQ"], "E")
+    nvec = [0]
+
+    def column(terms):
+        n = nvec[0]
+        nvec[0] += 1
+        out, key = T.vec[:, n:n + 1], "vec%d" % n
+        for y, (x, c) in enumerate(terms.items()):
+            if y == 0:
+                C(ts(out, T.E[:, x:x + 1], float(c), None, Op.mult), 1, ["E"], key)
+            else:
+                C(ts(out, T.E[:, x:x + 1], float(c), out, Op.mult, Op.add), 1, ["E", key], key)
+        return out, key
+
+    def affine(c0, c1):
+        n = nvec[0]
+        nvec[0] += 1
+        C(ts(T.vec[:, n:n + 1], T.pm[:, 0:1], c1, c0, Op.mult, Op.add), 1, ["pm"], "vec%d" % n)
+        return T.vec[:, n:n + 1], "vec%d" % n
+    rp1, rp1k = affine(1.0, 1.0)
+    zsc, zsck = column({0: 1, 1: -1, 2: -1})
+    zbi, zbik = column({2: 16 - ZC, 3: 1})
+    dbs = column({1: -0.5, 2: 1, 4: -0.5, 5: -0.5, 6: 1, 7: 1, 9: 1})
+    dbf = (T.vec[:, 31:32], "vec31")
+    C(tt(dbf[0], dbs[0], T.E[:, 0:1], Op.add), 1, [dbs[1], "E"], dbf[1])
+    for n_ in ("Wx", "Wc", "Wq", "Wu"):
+        C(ms(A0(n_), 0.0), 72, [], n_)
+    scaled(T.Wx[:, 15:128:16], A0("gf"), 1.0, ["gf", "Wx"], "Wx", 8)
+    scaled(A0("Wn"), A0("Wx"), -1.0, ["Wx"], "Wn", 144)
+    for q_, c_ in ((3, 1.0), (4, 0.5), (8, 0.5)):
+        scaled(T.Wc[:, q_:128:16], A0("gf"), c_, ["gf", "Wc"], "Wc", 8)
+    C(cp(A0("Wd"), T.Wc[:, 3:131]), 64, ["Wc"], "Wd")
+    C(ms(T.Wd[:, 0:128:16], 0.0), 8, ["Wd"], "Wd")
+    scaled(A0("Bn"), A0("B32"), -1.0, ["B32"], "Bn", 128)
+    vK = column({3: -18.5})
+    scaled(A0("Wk"), A0("B32"), vK[0], ["B32", vK[1]], "Wk", 128)
+    C(ts(A0("tm4"), A0("qm"), 9.5, None, Op.add), 128, ["qm"], "tm4")
+    C(tt(A0("Wm"), A0("tm4"), A0("B32"), Op.mult), 256, ["tm4", "B32"], "Wm")
+    for q_ in range(12, 16):
+        scaled(T.Wq[:, q_:128:16], A0("gf"), 1.0, ["gf", "Wq"], "Wq", 8)
+    vA, vB, vD, vE = column({0: 1, 1: -1}), column({0: 1, 1: -1, 2: 1, 3: -16}), column({2: -1, 3: 16}), (T.E[:, 3:4], "E")
+    for q_, (c_, k_) in ((0, vA), (1, vE), (2, vD), (3, vB), (4, vE), (5, vE), (6, vE), (7, vB), (9, vE)):
+        scaled(T.Wu[:, q_:128:16], A0("gf"), c_, ["gf", "Wu", k_], "Wu", 8)
+    C(cp(A0("Wf"), A0("Wu")), 64, ["Wu"], "Wf")
+    C(ms(T.Wf[:, 0:128:16], 0.0), 8, ["Wf"], "Wf")
+    scaled(A0("Wz1"), A0("B32"), vB[0], ["B32", vB[1]], "Wz1", 128)
+    vZ = column({2: 1, 7: 1, 9: -1})
+    scaled(A0("Wz"), A0("B32"), vZ[0], ["B32", vZ[1]], "Wz", 128)
+    for w_, tm_, al, be in (("Wy", "tm1", {1: 2, 6: 1}, {0: 1, 1: 19, 6: -9}),
+                            ("Wv", "tm2", {1: 2, 4: 2, 9: 1}, {0: 1, 3: 1, 1: 37, 4: 37, 5: -2, 6: -1})):
+        (a_, ak), (b_, bk) = column(al), column(be)
+        C(ts(A0(tm_), A0("qm"), a_, b_, Op.mult, Op.add), 128, ["qm", ak, bk], tm_)
+        C(tt(A0(w_), A0(tm_), A0("B32"), Op.mult), 256, [tm_, "B32"], w_)
+    C(ts(A0("tm3"), A0("qm"), rp1, -1.0, Op.subtract, Op.is_ge), 128, ["qm", rp1k], "tm3")
+    C(tt(A0("Wp"), A0("tm3"), A0("B32"), Op.mult), 256, ["tm3", "B32"], "Wp")
+    scaled(A0("G64"), A0("gf"), 64.0, ["gf"], "G64", 8)
+    C(ms(T.Z[:, :, :], 0.0), 128, [], "Z")
     for k in range(4):
-        C(ts(T.Z[:, :, 16 + k], A0("gf"), -16.0, None, Op.mult), 8, ["gf", "Z"], "Z")
-    C(ts(A0("cj"), A0("iJ"), 10.0, None, Op.add), 104, ["iJ"], "cj")
-    C(ts(A0("cpad"), A0("iJ"), 0.0, 1000.0, Op.is_equal, Op.mult), 104, ["iJ"], "cpad")
-    C(ts(A0("KD"), A0("iJ"), 0.0, LATE, Op.is_equal, Op.mult), 104, ["iJ"], "KD")
+        scaled(T.Z[:, :, 16 + k], A0("gf"), -32.0, ["gf", "Z"], "Z", 8)
+    C(ts(A0("cj"), A0("iJ"), -6.0, None, Op.add), 104, ["iJ"], "cj")
+    C(ts(A0("kd"), A0("iJ"), 0.0, 2 * FAKE, Op.is_equal, Op.mult), 104, ["iJ"], "kd")
+    C(ts(A0("KD"), A0("kd"), -FAKE, None, Op.add), 104, ["kd"], "KD")
     C(tt(A0("gr"), T.pg[:, 0:104], A0("iC"), Op.is_equal), 208, ["pg", "iC"], "gr")
     for h in range(2 if JA[0] != JA[1] else 1):
-        C(ts(A0("sg1"), A0("iJ"), float(JA[h]), 32.0, Op.is_ge, Op.mult), 104, ["iJ"], "sg1")
-        C(ts(A0("sg2"), A0("sg1"), -16.0, None, Op.add), 104, ["sg1"], "sg2")
+        C(ts(A0("sg1"), A0("iJ"), float(JA[h]), 64.0, Op.is_ge, Op.mult), 104, ["iJ"], "sg1")
+        C(ts(A0("sg2"), A0("sg1"), -32.0, None, Op.add), 104, ["sg1"], "sg2")
         C(tt(A0("RT%d" % h), A0("sg2"), A0("gr"), Op.mult), 208, ["sg2", "gr"], "RT%d" % h)
     RT = ["RT0", "RT%d" % (JA[0] != JA[1])]
-    C(ts(T.RD[:, 0:128], A0("qm"), 0.0, None, Op.is_gt), 128, ["qm"], "RD")
+    C(ms(A0("RD"), 1.0), 128, [], "RD")
+    for a_, b_, c_ in ((0, 256, 0.0), (3, 128, -1.0), (5, 128, 0.0), (7, 128, 0.0)):
+        C(ms(T.RD[:, a_:b_:16], c_), 16, ["RD"], "RD")
     C(ts(A0("sh"), T.pm[:, 0:32], 2, None, Op.arith_shift_right), 32, ["pm"], "sh")
     C(ts(A0("q1"), A0("sh"), 12.0, None, Op.mult), 32, ["sh"], "q1")
     C(tt(A0("q2"), A0("q1"), T.pm[:, 0:32], Op.add), 64, ["q1", "pm"], "q2")
     C(tt(A0("Qc"), A0("q2"), A0("i64"), Op.add), 64, ["q2", "i64"], "Qc")
-    for u in range(4):
-        C(ts(T.mu[:, 8 * u:8 * u + 1], T.sh[:, 0:1], float(u), None, Op.is_equal), 1, ["sh"], "mu%d" % u)
-        C(ts(T.Wu[:, 128 * u:128 * u + 128], A0("Ib"), T.mu[:, 8 * u:8 * u + 1], None, Op.mult), 64, ["Ib", "mu%d" % u], "Wu%d" % u)
-    fill("w7", 2.0 ** -7, 64)
-    fill("c185", -18.5, 64)
-    fill("cm16", -16.0, 64)
-    fill("c3", -6.0, 64)
-    fill("c205", 205.0, 8)
-    fill("ONE", 1.0, 104)
-    for h in EY:
-        C((lambda h: lambda last: v.memset(H("v2", h, 2048, 2064), 0.0))(h), 16, [], "v2p%d" % h)
+    C(ms(A0("w7"), 2.0 ** -7), 64, [], "w7")
+    C(ms(A0("c205"), 205.0), 8, [], "c205")
+    C(ms(T.CG[:, :, 256:272], 0.0), 128, [], "pad")
+    C(ms(A0("Xs"), 0.0), 256, [], "Xs")
     for h in range(2):
-        C((lambda h: lambda last: v.memset(H("Xs", h), 0.0))(h), 128, [], "Xs%d" % h)
-        C((lambda h: lambda last: v.memset(H("Xn", h), 0.0))(h), 64, [], "Xn%d" % h)
+        C(ms(H("Xs", h, 3, 128, 4), 1.0), 32, ["Xs"], "Xs%d" % h)
+        C(ms(H("Xs", h, 11, 128, 16), 0.0), 8, ["Xs%d" % h], "Xs%d" % h)
+        C(ms(H("Xs", h, 15, 128, 16), 0.0), 8, ["Xs%d" % h], "Xs%d" % h)
 
-    C(cp(T.z0f[:, :], T.z0s[:, :]), 256, ["z0s"], "z0f")
-    tx = P([mm(T.sm[:, 0:256], T.R8[:, :], T.z0f[:, :])], 1024, ["R8", "z0f"], ["sm"], acq="sm")
-    for h in range(2):
-        V(ts(T.zb[:, 128 * h:128 * h + 128], T.sm[:, 128 * h:128 * h + 128], 9.0, None, Op.add), 128, ["sm"], ["z0%d" % h], use=tx)
-    C(cp(A0("st0"), A0("s0s")), 256, ["s0s"], "st0_0")
-    lastw["st0_1"] = lastw["st0_0"]
-    C(ts(A0("dg1"), A0("cfs"), 2.0, 1.0, Op.mult, Op.add), 256, ["cfs"], "dg1")
+    C(ts(T.z0f[:, :], T.z0s[:, :], -ZC, None, Op.add), 256, ["z0s"], "z0f")
+    C(ts(A0("s0f"), A0("s0s"), -ZC, None, Op.add), 256, ["s0s"], "s0f")
+    C(ts(A0("c0f"), A0("cfs"), 2.0, 1.0, Op.mult, Op.add), 256, ["cfs"], "c0f")
     for h in range(2):
         for a in range(4):
             src = T.t0s[:, 256 * a + 128 * h:256 * a + 128 * h + 128]
-            dst = T.tl0[:, 128 * h:128 * h + 128, a]
-            if a < 2:
-                V(cp(dst, src), 64, ["t0s"], ["T0%d" % h] if a == 0 else ["T0%d_%d" % (h, a)])
-            else:
-                A(act(dst, src), 128, ["t0s"], ["T0%d_%d" % (h, a)])
+            VA(cp(H("tb", h, a, None, 4), src), 64, act(H("tb", h, a, None, 4), src), 128, ["t0s"], ["tb%d" % h] if a == 0 else ["tb%d_%d" % (h, a)])
 
     mcount = [0]
-    tx_of = {}
 
-    def gatherlist(t):
+    def rotation(t, base):
         if t == 0:
             C(ts(A0("lm"), A0("l5"), 255, None, Op.bitwise_and), 16, ["l5"], "lm")
         else:
-            b = T.al[:, 4 * t:4 * t + 1]
-            if t == 1:
-                V(ts(A0("li"), A0("LB"), b, None, Op.add), 16, ["LB", "A1"], ["li"])
-            else:
-                V(ts(A0("li"), A0("LB"), b, T.al[:, 4 * t - 4:4 * t - 3], Op.add, Op.subtract), 16, ["LB", "A%d" % t, "A%d" % (t - 1)], ["li"])
+            c = {}
+            fns = [mm(pb(c, 0, 1), T.R8n[:, :], T.CL[0:8, t - 1, 256:257], True, t == NV)]
+            if t < NV:
+                fns.append(mm(pb(c, 0, 1), T.R8[:, :], T.CG[0:8, t, 256:257], False, True))
+            P(fns, 512, ["R8", "R8n", "C%d" % (t - 1)] + (["B%d" % t] if t < NV else []), ["dB"], acq=c)
+            V(ts(A0("li"), A0(base), pb(c, 0, 1), None, Op.add), 16, [base, "dB"], ["li"], use=c)
             C(ts(A0("lm"), A0("li"), 255, None, Op.bitwise_and), 16, ["li"], "lm")
         C(cp(A0("lu"), A0("lm")), 16, ["lm"], "lu")
-        st, dn, do = "st%d" % (t % 2), "dg%d" % (t % 2), "dg%d" % ((t + 1) % 2)
-        A(act(A0("sg"), T[st][:, :].indirect(T.lu[:, :])), 256 * 1.5, ["lu", st + "_0", st + "_1"], ["sg"])
-        A(act(A0(dn), T[do][:, :].indirect(T.lu[:, :])), 256 * 1.5, ["lu", do], [dn])
 
-    def zref(t, h):
-        return T.zb[:, 128 * h:128 * h + 128] if t == 0 else T.zl[:, 256 * (t - 1) + 128 * h:256 * (t - 1) + 128 * h + 128]
+    def tables(t):
+        rotation(t, "LB")
+        sw, sk = (T.s0f[:, :], ["s0f"]) if t == 0 else (T.SL[:, t - 1, :], ["S%d0" % (t - 1), "S%d1" % (t - 1)])
+        cw, ck = (T.c0f[:, :], ["c0f"]) if t == 0 else (T.CL[:, t - 1, 0:256], ["C%d" % (t - 1)])
+        for h in range(2):
+            tag[0] = ("L", h, t)
+            gather(T.sg[:, 128 * h:128 * h + 128], sw, T.lu[:, 8 * h:8 * h + 8], 128, ["lu"] + sk, ["sg%d" % h], "gS")
+            gather(T.CG[:, t, 128 * h:128 * h + 128], cw, T.lu[:, 8 * h:8 * h + 8], 128, ["lu"] + ck, ["cg%d%d" % (t, h)], "gC")
+        a = 0 if t < NV - 1 else 256
+        send(1, T.CL[:, t, a:272], T.CG[:, t, a:272], "rC%d" % t, ["cg%d0" % t, "cg%d1" % t, "pad", "B%d" % t], "C%d" % t, 3.0)
 
-    def select(t, h, W, tail):
-        hs, c0 = str(h), 128 * h
-        X = T.vt[:, 256 * h:256 * h + 128]
-        Y = T.vt[:, 256 * h + 128:256 * h + 256]
-        dn = "dg%d" % (t % 2)
-        OHS, OK = (Y, "vY") if tail == 0 else (X, "vX")
-        tx = P([mm(T.sm[:, 0:128], A0("Bb"), H("cmp", h))], 128, ["Bb", "cmp" + hs], ["cnt" + hs], acq="sm")
-        V(ts(OHS, T.sm[:, 0:128], 1.0, T.rp1[:, 0:1], Op.max, Op.is_equal), 128, ["cnt" + hs, "rp1"], [OK + hs], use=tx)
-        if tail == 0:
-            V(ts(H("geb", h), T.sm[:, 0:128], T.rp1[:, 0:1], None, Op.is_le), 128, ["cnt" + hs, "rp1"], ["geb" + hs], use=tx)
-        V(tt(H("oD", h), OHS, T[dn][:, c0:c0 + 128], Op.mult), 128, [OK + hs, dn], ["oD" + hs])
-        V(tt(H("oH", h), OHS, H("Hb", h), Op.mult), 128, [OK + hs, "Hb" + hs], ["oH" + hs])
-        tx = P([mm(T.sm[:, 0:128], A0("w7"), A0("c185"), True, False), mm(T.sm[:, 0:128], A0(W), H("oD", h), False, False)], 256,
-               ["w7", "c185", W, "oD" + hs], ["F" + hs], acq="sm")
-        P([mm(T.sm[:, 0:128], A0("B32"), H("oH", h), False, True)], 512, ["oH" + hs, "B32"], ["F" + hs], use=tx)
-        V(cp(H("fi", h), T.sm[:, 0:128]), 128, ["F" + hs], ["fi" + hs], use=tx)
+    def position(t, h, c, extra):
+        hs = str(h)
+        if t == 0:
+            P([mm(pb(c, 0, 128), T.R8[:, :], T.z0f[:, 128 * h:128 * h + 128])], 512, ["R8", "z0f"] + extra, ["zn" + hs], acq=c)
+        else:
+            P([mm(pb(c, 0, 128), A0("Wz"), H("prod", h), True, False), mm(pb(c, 0, 128), A0("Bb"), H("ind", h), False, True)], 640,
+              ["Wz", "Bb", "prod" + hs, "ind" + hs] + extra, ["zn" + hs], acq=c)
+
+    def columns(h, terms, buf, t):
+        hs, c = str(h), {}
+        P([mm(pb(c, 0, 128), A0(x[0]), x[1], y == 0, y == len(terms) - 1) for y, x in enumerate(terms)], sum(x[3] for x in terms),
+          [x[0] for x in terms] + [x[2] for x in terms], ["F" + hs], acq=c)
+        V(cp(H("fi", h), pb(c, 0, 128)), 128, ["F" + hs], ["fi" + hs], use=c)
         V(ts(H("fm", h), H("fi", h), 4095, None, Op.bitwise_and), 128, ["fi" + hs], ["fm" + hs])
         V(cp(H("of", h), H("fm", h)), 128, ["fm" + hs], ["of" + hs])
-
-    def samples(t, h, buf):
-        hs, k = str(h), 128 // GP
-        for q in range(GP):
-            on_v = (buf, h, q) in (VG0 if t == 0 else VGL if t == NV - 1 else VG)
-            (V if on_v else A)((cp if on_v else act)(H(buf, h, 16 * k * q, 16 * k * q + 16 * k), T.x[:, :].indirect(H("of", h, k * q, k * q + k))),
-                               16 * k * 1.5, ["x", "of" + hs], [buf + hs + "_%d" % q])
-    YK = lambda b, h: [b + str(h) + "_%d" % q for q in range(GP)]
+        for q in range(4):
+            gather(H(buf, h, 512 * q, 512 * q + 512), T["x%d" % (t % 4)][:, :], H("of", h, 32 * q, 32 * q + 32), 512, XK[t % 4] + ["of" + hs],
+                   [buf + hs + "_%d" % q], buf + str(q), dflt="a")
+    YK = lambda b, h: [b + str(h) + "_%d" % q for q in range(4)]
 
     def front(t, h):
-        hs, c0 = str(h), 128 * h
-        X = T.vt[:, 256 * h:256 * h + 128]
-        dn = "dg%d" % (t % 2)
-        V(tt(X, zref(t, h), T.sg[:, c0:c0 + 128], Op.subtract), 256, ["z%d%d" % (t, h), "sg"], ["vX" + hs])
-        V(ts(H("cmp", h), X, 9.0, None, Op.is_ge), 128, ["vX" + hs], ["cmp" + hs])
-        V(tt(H("Hb", h), X, T[dn][:, c0:c0 + 128], Op.mult), 128, ["vX" + hs, dn], ["Hb" + hs])
-        select(t, h, "W0", 0)
-        samples(t, h, "y2")
-
-    def heavy(t, h):
         hs = str(h)
-        tl = T["tl%d" % t][:, 128 * h:128 * h + 128, :]
-        ta = lambda a: T["tl%d" % t][:, 128 * h:128 * h + 128, a]
-        TK = ["T%d%d" % (t, h)] + (["T0%d_%d" % (h, a) for a in (1, 2, 3)] if t == 0 else [])
+        sg, cg, sk, ck = T.sg[:, 128 * h:128 * h + 128], T.CG[:, t, 128 * h:128 * h + 128], "sg" + hs, "cg%d%d" % (t, h)
+        c = {}
+        position(t, h, c, ["lu"])
+        A(act(H("ze", h), pb(c, 0, 128), AF.Relu, zbi, zsc), 128, ["zn" + hs, zsck, zbik], ["ze" + hs], use=c)
+        V(tt(H("cmp", h, 0, 128), pb(c, 0, 128), sg, Op.is_ge), 128, ["zn" + hs, sk], ["cmp0" + hs], use=c)
+        fast = prm["FAST"][h]
+        if fast:
+            V(tt(pb(c, 128, 256), sg, pb(c, 0, 128), Op.subtract), 128, ["zn" + hs, sk], ["X" + hs], use=c)
+            V(tt(H("Hb", h), pb(c, 128, 256), cg, Op.mult), 128, ["X" + hs, ck], ["Hb" + hs], use=c)
+        for b in range(2):
+            c, bs = {}, str(b) + hs
+            if b == 1:
+                tag[0] = ("G" if fast else "F", h, t)
+                P([mm(pb(c, 0, 128), A0("Wz1"), H("ze", h))], 128, ["Wz1", "ze" + hs], ["z1" + hs], acq=c)
+                V(tt(H("cmp", h, 128, 256), pb(c, 0, 128), sg, Op.is_ge), 128, ["z1" + hs, sk], ["cmp1" + hs], use=c)
+                c = {}
+            src, srck = (H("Hb", h), "Hb" + hs) if fast and b == 0 else (sg, sk)
+            P([mm(pb(c, 0, 128), A0("Bb"), H("cmp", h, 128 * b, 128 * b + 128))], 128, ["Bb", "cmp" + bs], ["cnt" + bs], acq=c)
+            V(ts(pb(c, 128, 256), pb(c, 0, 128), 1.0, rp1, Op.max, Op.is_equal), 128, ["cnt" + bs, rp1k], ["OH" + bs], use=c)
+            V(tt(H("oC", h, 128 * b, 128 * b + 128), pb(c, 128, 256), cg, Op.mult), 128, ["OH" + bs, ck], ["oC" + bs], use=c)
+            V(tt(H("oS", h, 128 * b, 128 * b + 128), pb(c, 128, 256), src, Op.mult), 128, ["OH" + bs, srck], ["oS" + bs], use=c)
+            if b == 0:
+                V(ts(H("geb", h), pb(c, 0, 128), rp1, None, Op.is_le), 128, ["cnt" + bs, rp1k], ["geb" + hs], use=c, name="geb")
+                if fast:
+                    columns(h, [("Wk", H("ze", h), "ze" + hs, 128), ("Wm", H("oC", h, 0, 128), "oC0" + hs, 128), ("Bn", H("oS", h, 0, 128), "oS0" + hs, 512)], "y2", t)
+        c = {}
+        wu, wc, (db, dbk) = ("Wf", T.Wd[:, :], dbf) if fast else ("Wu", T.Wc[:, 3:131], dbs)
+        P([mm(pb(c, 0, 128), A0(wu), H("ze", h), True, False), mm(pb(c, 0, 128), T.Wn[:, 15:143], H("oS", h, 0, 128), False, False),
+           mm(pb(c, 0, 128), T.Wn[:, 12:140], H("oS", h, 128, 256), False, True)], 1152, [wu, "Wn", "ze" + hs, "oS0" + hs, "oS1" + hs], ["U" + hs], acq=c)
+        P([mm(pb(c, 128, 256), wc, H("oC", h, 0, 128), True, False), mm(pb(c, 128, 256), T.Wc[:, 0:128], H("oC", h, 128, 256), False, True)], 256,
+          ["Wc", "Wd", "oC0" + hs, "oC1" + hs], ["Cr" + hs], use=c, after=[c["first"]])
+        VA(ts(H("Dc", h), pb(c, 128, 256), db, None, Op.add), 128, act(H("Dc", h), pb(c, 128, 256), AF.Identity, db), 128, ["Cr" + hs, dbk], ["Dc" + hs], use=c, name="Dc")
+        V(tt(H("Left", h), pb(c, 0, 128), H("Dc", h), Op.mult), 128, ["U" + hs, "Dc" + hs], ["Left" + hs], use=c)
+        if not fast:
+            columns(h, [("Wy", H("Left", h), "Left" + hs, 512)], "y2", t)
+
+    def match(t, h):
+        hs = str(h)
+        TK = ["tb" + hs] + (["tb%d_%d" % (h, a) for a in (1, 2, 3)] if t == 0 else [])
         K = T.kb[:, 0:104]
-        kx = P([mm(K, A0("w7"), A0("cj"), True, False)], 104, ["w7", "cj"] + YK("y2", h), ["K" + hs], acq="kb")
-        P([mm(K, ta(a), A0(RT[h]), False, False) for a in range(4)], 416, TK + [RT[h]], [], acc="K" + hs, use=kx)
-        P([mm(K, H("y2", h, m, None, 16), T.Z[:, :, 19 - m:32 - m], False, False) for m in range(16)], 1664,
-          YK("y2", h) + ["Z"], [], acc="K" + hs, use=kx)
-        yx = None
+        P([mm(K, A0("w7"), A0("cj"), True, False)] + [mm(K, H("tb", h, a, None, 4), A0(RT[h]), False, False) for a in range(4)], 520,
+          ["w7", "cj", RT[h], "y2%s_0" % hs] + TK, ["K"])
+        P([mm(K, H("y2", h, m, None, 16), T.Z[:, :, 19 - m:32 - m], False, False) for m in range(16)], 1664, YK("y2", h) + ["Z"], [], acc="K", name="ysum")
         for b in range(4):
-            fill_b = [mm(T.yps[:, 32 * b:32 * b + 32, :], A0("Ib"), H("y2", h, 512 * b, 512 * b + 512))]
-            y = P(fill_b, 512, ["y2%s_%d" % (hs, b * GP // 4), "Ib"], ["yps%s%d" % (hs, b)], **({"acq": "yps"} if b == 0 else {"use": yx, "after": [yx]}))
-            yx = y if b == 0 else yx
-        ja, jv = list(range(JA[h], J)), list(range(JA[h]))
-        for x, j in enumerate(ja):
-            dx = P([mm(T.dif[:, 128 * a:128 * a + 128], A0("Ib"), H("y2", h, j + a, None, 16), True, False) if w == 0 else
-                    mm(T.dif[:, 128 * a:128 * a + 128], A0("Im"), ta(a), False, True) for a in range(4) for w in range(2)], 1024,
-                   YK("y2", h) + TK + ["Ib", "Im"], ["dif" + hs], acq="dif")
-            b = x
-            A(act(H("Ma", h, 512 * b, 512 * b + 512), T.dif[:, :], AF.Relu), 512, ["dif" + hs], ["Ma%s%d" % (hs, b)], use=dx)
-            P([mm(T.kb[:, j:104:13], H("Ma", h, 512 * b + 128 * a, 512 * b + 128 * a + 128), A0("G32"), False, False) for a in range(4)],
-              256, ["Ma%s%d" % (hs, b), "G32"], [], acc="K" + hs, use=kx)
-        for j in jv:
-            n = mcount[0] % NM
+            P([mm(T.yps[:, 32 * b:32 * b + 32, :], A0("Ib"), H("y2", h, 512 * b, 512 * b + 512))], 512, ["y2%s_%d" % (hs, b), "Ib"], ["yps%d" % b])
+        for x, j in enumerate(range(JA[h], J)):
+            c = {}
+            P([mm(pb(c, 0, 512), A0("Im"), H("tb", h), True, False)] +
+              [mm(pb(c, a, 512, 4), A0("Ib"), H("y2", h, j + a, None, 16), False, a == 3) for a in range(4)], 1024,
+              YK("y2", h) + TK + ["Ib", "Im"], ["dif%s%d" % (hs, x)], acq=c, name="dif")
+            A(act(H("Ma", h, 512 * x, 512 * x + 512), pb(c, 0, 512), AF.Relu), 512, ["dif%s%d" % (hs, x)], ["Ma%s%d" % (hs, x)], use=c)
+            P([mm(T.kb[:, j:104:13], H("Ma", h, 512 * x + a, 512 * x + 512, 4), A0("G64"), False, False) for a in range(4)],
+              256, ["Ma%s%d" % (hs, x), "G64"], [], acc="K")
+        bufs = []
+        for j in range(JA[h]):
+            bufs.append(mcount[0] % NM)
             mcount[0] += 1
-            M = T["mb%d" % n]
-            V(tt(M[:, :, :], T.yps[:, :, j:j + 4], tl, Op.max), 512, ["yps%s%d" % (hs, b) for b in range(4)] + TK, ["mb%d" % n], use=yx)
-            P([mm(T.kb[:, j:104:13], M[:, :, a], A0("G32"), False, False) for a in range(4)], 256, ["mb%d" % n, "G32"], [], acc="K" + hs, use=kx)
-        V(scan(H("ks", h), A0("KD"), K, Op.max, Op.min), 104, ["K" + hs, "KD"], ["ks" + hs], use=kx)
+        order = [(j, 0, 2) for j in range(NS[h])] + [(j, 2, 4) for j in range(NS[h])] + [(j, 0, 4) for j in range(NS[h], JA[h])]
+        prev = []
+        for j, b0, b1 in order:
+            M, mk = T["mb%d" % bufs[j]], "mb%d" % bufs[j]
+            prev = [V(tt(M[:, 128 * b0:128 * b1], T.yps[:, 32 * b0:32 * b1, j:j + 4], H("tb", h, 128 * b0, 128 * b1), Op.max), 128 * (b1 - b0),
+                      ["yps%d" % b for b in range(b0, b1)] + TK, [mk + "_%d" % b for b in range(b0, b1, 2)], after=prev)]
+            if b1 == 4:
+                P([mm(T.kb[:, j:104:13], M[:, a:512:4], A0("G64"), False, False) for a in range(4)], 256, [mk + "_0", mk + "_2", "G64"], [], acc="K")
+        V(scan(H("ks", h), A0("KD"), K, Op.max, Op.min), 104, ["K", "KD"], ["ks" + hs])
 
     def decide(t, h):
         hs = str(h)
         best = H("ks", h, 12, None, 13)
-        tie, dlt = H("Xs", h, 0, 128, 16), H("Xs", h, 128, 256, 16)
-        V(ts(tie, best, EARLY, None, Op.is_lt), 8, ["ks" + hs, "Xs" + hs], ["Xt" + hs])
-        V(scan(H("Xr", h, 0, 128), T.RD[:, 0:128], H("Xs", h, 0, 128), Op.mult, Op.add), 64, ["RD", "Xt" + hs], ["Xr" + hs])
         V(ts(H("rr", h), best, MAGIC, MAGIC, Op.add, Op.subtract), 8, ["ks" + hs], ["rr" + hs])
-        V(tt(H("dd", h), H("rr", h), best, Op.subtract), 16, ["rr" + hs, "ks" + hs], ["dd" + hs])
-        V(tt(dlt, H("dd", h), tie, Op.mult), 16, ["dd" + hs, "Xt" + hs], ["Xd" + hs])
-        V(scan(H("Xr", h, 128, 256), T.RD[:, 0:128], H("Xs", h, 128, 256), Op.mult, Op.add), 64, ["RD", "Xd" + hs], ["Xe" + hs])
-
-    def fresh(t, h):
-        hs, c0 = str(h), 128 * h
-        X = T.vt[:, 256 * h:256 * h + 128]
-        Y = T.vt[:, 256 * h + 128:256 * h + 256]
-        dn, sn = "dg%d" % (t % 2), "st%d" % ((t + 1) % 2)
-        zk = "z%d%d" % (t, h)
-        if True:
-            tx = P([mm(T.sm[:, 0:128], A0("w7"), A0("cm16"), True, False), mm(T.sm[:, 0:128], H("Xr", h, 0, 128), A0("I16"), False, True),
-                    mm(T.sm[:, 128:256], H("Xr", h, 128, 256), A0("Ib"))], 384, ["w7", "cm16", "I16", "Ib", "Xr" + hs, "Xe" + hs], ["tz" + hs], acq="sm")
-            V(tt(Y, zref(t, h), T.sm[:, 0:128], Op.add), 128, [zk, "tz" + hs], ["vY" + hs], use=tx)
-            V(tt(H("dge", h), T.sm[:, 128:256], H("geb", h), Op.mult), 128, ["tz" + hs, "geb" + hs], ["dge" + hs], use=tx)
-            V(ts(H("zp", h), Y, 9.0, 9.0, Op.max, Op.add), 128, ["vY" + hs], ["zp" + hs])
-        V(tt(X, H("zp", h), T.sg[:, c0:c0 + 128], Op.subtract), 256, ["zp" + hs, "sg"], ["vX" + hs])
-        V(ts(H("cmp", h), X, 18.0, None, Op.is_ge), 128, ["vX" + hs], ["cmp" + hs])
-        V(tt(Y, X, H("dge", h), Op.subtract), 128, ["vX" + hs, "dge" + hs], ["vY" + hs])
-        V(tt(H("Hb", h), Y, T[dn][:, c0:c0 + 128], Op.mult), 128, ["vY" + hs, dn], ["Hb" + hs])
-        V(tt(T[sn][:, c0:c0 + 128], H("dge", h), T.sg[:, c0:c0 + 128], Op.add), 256, ["dge" + hs, "sg"], ["%s_%d" % (sn, h)])
-        select(t, h, "W0", 1)
-        samples(t, h, "v2")
+        V(ts(H("Xs", h, 0, 128, 16), best, FAKE - 8, None, Op.is_lt), 8, ["ks" + hs, "Xs" + hs], ["Xt" + hs])
+        V(tt(H("Xs", h, 128, 256, 16), H("rr", h), best, Op.subtract), 16, ["rr" + hs, "ks" + hs], ["Xd" + hs])
+        V(tt(H("Xs", h, 5, 128, 16), H("rr", h), best, Op.subtract), 16, ["rr" + hs, "ks" + hs], ["Xe" + hs])
+        V(scan(H("Xr", h), A0("RD"), H("Xs", h), Op.mult, Op.add), 128, ["RD", "Xt" + hs, "Xd" + hs, "Xe" + hs], ["Xr" + hs])
+        c = {}
+        P([mm(pb(c, 0, 128), H("Xr", h, 0, 128), A0("Ib")), mm(pb(c, 128, 256), H("Xr", h, 128, 256), A0("Ib"))], 256, ["Ib", "Xr" + hs], ["w" + hs], acq=c)
+        tag[0] = ("S", h, t)
+        V(tt(pb(c, 256, 384), pb(c, 128, 256), H("geb", h), Op.mult), 128, ["w" + hs, "geb" + hs], ["dge" + hs], use=c)
+        V(tt(T.SN[:, t, 128 * h:128 * h + 128], pb(c, 256, 384), T.sg[:, 128 * h:128 * h + 128], Op.add), 128, ["dge" + hs, "sg" + hs], ["sn%d%d" % (t, h)], use=c)
+        i = send(1, T.SL[:, t, 128 * h:128 * h + 128], T.SN[:, t, 128 * h:128 * h + 128], "rS%d%d" % (t, h), ["sn%d%d" % (t, h)], "S%d%d" % (t, h), 2.2)
+        if h == 1 and t < 2:
+            sendlog(t + 2, [i])
+        tag[0] = ("N", h, t)
+        V(tt(H("prod", h), pb(c, 0, 128), H("Left", h), Op.mult), 128, ["w" + hs, "Left" + hs], ["prod" + hs], use=c)
+        columns(h, [("Wv", H("prod", h), "prod" + hs, 512)], "v2", t)
 
     def counts(t):
-        tx = P([mm(T.sm[:, 0:1], H("Xr", 0, 0, 128), T.c205[:, 0:1], True, False), mm(T.sm[:, 0:1], H("Xr", 1, 0, 128), T.c205[:, 0:1], False, True)],
-               128, ["Xr0", "Xr1", "c205"], ["Aps"], acq="sm")
-        V(cp(T.am[:, 4 * t:4 * t + 1], T.sm[:, 0:1]), 1, ["Aps"], ["am%d" % t], use=tx)
-        send(t, "A", None, T.al[:, 4 * t + 4:4 * t + 5], T.am[:, 4 * t:4 * t + 1], "am%d" % t)
-
-    def send(t, kind, h, out, in_, key):
-        sem = "r%s%d%s" % (kind, t + 1, "" if h is None else h)
-        rid, pid, mask = nxt
-
-        def fn(last):
-            return g.remote_dma(out, in_, T.sem[sem], T.sem.loc, pid, rid, mask)
-        i = add("q", [fn], 0.9, [key], [], pin=("send",))
-        add("n", [], 3.0, [], ["%s%d%s" % (kind, t + 1, "" if h is None else h)], after=[i], pin=(sem, gs["neng"]))
+        c = {}
+        P([mm(pb(c, 0, 1, 1, 8), H("Xs", 0, 0, 128, 16), T.c205[:, 0:1], True, False), mm(pb(c, 0, 1, 1, 8), H("Xs", 1, 0, 128, 16), T.c205[:, 0:1], False, True)],
+          32, ["Xt0", "Xt1", "c205"], ["Aps"], acq=c)
+        out = T.CG[0:8, t + 1, 256:257]
+        VA(cp(out, pb(c, 0, 1, 1, 8)), 1, act(out, pb(c, 0, 1, 1, 8)), 1, ["Aps", "pad"], ["B%d" % (t + 1)], use=c)
 
     def finish(t, h):
         hs = str(h)
-        ex = None
-        for b in range(4 if h in EY else 0):
-            e = P([mm(T.yps[:, 32 * b:32 * b + 32, :], A0("Ib"), H("v2", h, 512 * b + 1, 512 * b + 513), True, False),
-                   mm(T.yps[:, 32 * b:32 * b + 32, :], A0("Im"), H("v2", h, 512 * b, 512 * b + 512), False, True)], 1024,
-                  ["v2%s_%d" % (hs, k) for k in sorted({b * GP // 4, min(b + 1, 3) * GP // 4})] + ["v2p" + hs, "Ib", "Im"], ["yps%s%d" % (hs, b)],
-                  **({"acq": "yps"} if b == 0 else {"use": ex, "after": [ex]}))
-            ex = e if b == 0 else ex
-            A(act(T.Vb[:, 128 * h + 32 * b:128 * h + 32 * b + 32, :], T.yps[:, 32 * b:32 * b + 32, 3:15], AF.Abs), 384,
-              ["yps%s%d" % (hs, b)], ["Vb%s%d" % (hs, b)], use=ex)
-        for q in range(0 if h in EY else 3):
-            fns = []
-            for w in range(4):
-                m = 4 + 4 * q + w
-                fns += [mm(T.dif[:, 128 * w:128 * w + 128], A0("Ib"), H("v2", h, m, 2048, 16), True, False),
-                        mm(T.dif[:, 128 * w:128 * w + 128], A0("Im"), H("v2", h, m - 1, 2048, 16), False, True)]
-            dx = P(fns, 1024, YK("v2", h) + ["Ib", "Im"], ["dif" + hs], acq="dif")
-            A(act(H("Va", h, 512 * q, 512 * q + 512), T.dif[:, :], AF.Abs), 512, ["dif" + hs], ["Va%s%d" % (hs, q)], use=dx)
-        fns = [mm(T.sm[:, 0:104], A0("w7"), A0("cpad"), True, False)]
-        for w in range(12):
-            fns.append(mm(T.sm[:, 12 - w:104:13], T.Vb[:, 128 * h:128 * h + 128, w] if h in EY else H("Va", h, 128 * w, 128 * w + 128), A0("G1"),
-                          False, w == 11))
-        tx = P(fns, 104 + 768, ["w7", "cpad", "G1"] + (["Vb%s%d" % (hs, b) for b in range(4)] if h in EY else ["Va%s%d" % (hs, q) for q in range(3)]),
-               ["S" + hs], acq="sm")
-        A(act(H("nx", h), T.sm[:, 0:104], AF.Relu, 26256.0, -32.0), 104, ["S" + hs], ["nx" + hs], use=tx)
-        V(scan(H("ns", h), A0("ONE"), H("nx", h), Op.add, Op.min), 104, ["ONE", "nx" + hs], ["ns" + hs])
-        V(cp(H("Xn", h, 0, 128, 16), H("ns", h, 12, None, 13)), 8, ["ns" + hs, "Xn" + hs], ["Xn" + hs])
-        V(scan(H("Xnr", h), T.RD[:, 0:128], H("Xn", h), Op.mult, Op.add), 64, ["RD", "Xn" + hs], ["Xnr" + hs])
-        tx = P([mm(T.sm[:, 0:128], A0("w7"), A0("c3"), True, False), mm(T.sm[:, 0:128], H("Xnr", h), A0("Ib"), False, True)], 256,
-               ["w7", "c3", "Xnr" + hs, "Ib"], ["n" + hs], acq="sm")
-        a = A(act(H("nsb", h), T.sm[:, 0:128]), 128, ["n" + hs], ["nsb" + hs], use=tx)
-        zo = T.zm[:, 256 * t + 128 * h:256 * t + 128 * h + 128]
-        V(tt(zo, H("zp", h), T.sm[:, 0:128], Op.add), 128, ["zp" + hs, "n" + hs], ["zm%d%d" % (t, h)], use=tx, after=[a])
-        send(t, "z", h, T.zl[:, 256 * t + 128 * h:256 * t + 128 * h + 128], zo, "zm%d%d" % (t, h))
-        tx = P([mm(T.sm[:, 0:32], A0("Ih"), A0("Qc"), True, False)] +
-               [mm(T.sm[:, 0:32], T.Wu[:, 128 * u:128 * u + 128], H("nsb", h, u, None, 4), False, u == 3) for u in range(4)], 320,
-               ["Ih", "Qc", "nsb" + hs] + ["Wu%d" % u for u in range(4)], ["Q" + hs], acq="sm")
-        V(cp(H("tof", h), T.sm[:, 0:32]), 32, ["Q" + hs], ["tof" + hs], use=tx)
-        to = T.ts[:, 1024 * t + 512 * h:1024 * t + 512 * h + 512]
-        A(act(to, H("v2", h, 0, 2048).indirect(H("tof", h))), 512 * 1.5, YK("v2", h) + ["tof" + hs], ["ts%d%d" % (t, h)])
-        send(t, "T", h, T["tl%d" % (t + 1)][:, 128 * h:128 * h + 128, :], to, "ts%d%d" % (t, h))
+        nb = prm["SB"][h]
+        bw, nu = 128 // nb, (3, 2)[nb - 1]
+        nw = 12 // nu
+        for b in range(nb):
+            for u in range(nu):
+                c, fns, n = {}, [], nu * b + u
+                for w in range(nw):
+                    m = 16 * bw * b + 4 + nw * u + w
+                    fns += [mm(pb(c, bw * w, bw * w + bw), A0("Ib"), H("v2", h, m, 16 * bw * (b + 1), 16), True, False),
+                            mm(pb(c, bw * w, bw * w + bw), A0("Im"), H("v2", h, m - 1, 16 * bw * (b + 1), 16), False, True)]
+                P(fns, 2 * nw * bw, YK("v2", h)[4 * b // nb:4 * (b + 1) // nb] + ["Ib", "Im"], ["st%s%d" % (hs, n)], acq=c)
+                A(act(H("Va", h, nw * bw * n, nw * bw * (n + 1)), pb(c, 0, nw * bw), AF.Abs), nw * bw, ["st%s%d" % (hs, n)], ["Va%s%d" % (hs, n)], use=c)
+        c, prev = {}, None
+        for n in range(nb * nu):
+            b, u = n // nu, n % nu
+            fns = [mm(pb(c, bw * b, bw * b + bw), T.Wx[:, 11 - nw * u - w:139 - nw * u - w], H("Va", h, bw * (nw * n + w), bw * (nw * n + w + 1)),
+                      u == 0 and w == 0, u == nu - 1 and w == nw - 1) for w in range(nw)]
+            extra = ["Va%s%d" % (hs, min(nb * nu - 1, prm.get("SUMAFT", 1)))] if n == 0 else []
+            prev = P(fns, nw * bw, ["Wx", "Va%s%d" % (hs, n)] + extra, ["ss%s%d" % (hs, n)], **({"acq": c} if n == 0 else {"use": c, "after": [prev]}))
+        VA(ts(H("r1", h), pb(c, 0, 128), -820.0, 0.0, Op.add, Op.max), 128, act(H("r1", h), pb(c, 0, 128), AF.Relu, -820.0), 128,
+           ["ss%s%d" % (hs, n) for n in range(nb * nu)], ["r1" + hs], use=c, name="r1")
+        c = {}
+        P([mm(pb(c, 0, 128), A0("Wp"), H("r1", h))], 128, ["Wp", "r1" + hs], ["pre" + hs], acq=c)
+        VA(ts(H("ind", h), pb(c, 0, 128), 0.5, None, Op.is_lt), 128, act(H("ind", h), pb(c, 0, 128), AF.Relu, 1.0, -1.0), 128, ["pre" + hs], ["ind" + hs], use=c, name="ind")
+        tag[0] = ("T", h, t)
+        c = {}
+        P([mm(pb(c, 0, 32), A0("Ih"), A0("Qc"), True, False)] +
+          [mm(pb(c, 0, 32), T.Wq[:, 12 - 4 * u:140 - 4 * u], H("ind", h, u, None, 4), False, u == 3) for u in range(4)], 320, ["Ih", "Qc", "Wq", "ind" + hs], ["Q" + hs], acq=c)
+        V(cp(H("tof", h), pb(c, 0, 32)), 32, ["Q" + hs], ["tof" + hs], use=c)
+        gather(H("tb", h), H("v2", h), H("tof", h), 512, YK("v2", h) + ["tof" + hs], ["tb" + hs], "gT")
 
     for t in range(NV):
         tag[0] = ("L", 0, t)
-        gatherlist(t)
+        tables(t)
         for h in range(2):
             tag[0] = ("F", h, t)
             front(t, h)
         for h in range(2):
             tag[0] = ("H", h, t)
-            heavy(t, h)
+            match(t, h)
             tag[0] = ("D", h, t)
             decide(t, h)
         if t < NV - 1:
             tag[0] = ("C", 0, t)
             counts(t)
         for h in range(2):
-            tag[0] = ("N", h, t)
-            fresh(t, h)
             tag[0] = ("E", h, t)
             finish(t, h)
     tag[0] = ("O", 0, 0)
 
-    st = "st%d" % (NV % 2)
-    V(ts(A0("li"), A0("LF"), T.al[:, 4 * NV - 4:4 * NV - 3], None, Op.subtract), 16, ["LF", "A%d" % (NV - 1)], ["li"])
-    C(ts(A0("lm"), A0("li"), 255, None, Op.bitwise_and), 16, ["li"], "lm")
-    C(cp(A0("lu"), A0("lm")), 16, ["lm"], "lu")
-    A(act(A0("ysb"), T[st][:, :].indirect(T.lu[:, :])), 256 * 1.5, ["lu", st + "_0", st + "_1"], ["ysb"])
-
     def store(out, in_, rd):
-        add("d", [lambda last: gs["d"].dma_start(out, in_)], 2.0, rd, [], pin=("sto", 16))
+        add({"d": [lambda last: gs["d"].dma_start(out, in_)]}, {"d": 0.05}, rd, [], pin=("dma", "sto", 2.0))
+    rotation(NV, "LF")
+    gather(A0("ysb"), T.SL[:, NV - 1, :], T.lu[:, :], 256, ["lu", "S%d0" % (NV - 1), "S%d1" % (NV - 1)], ["ysb"], "gY", bias=ZC)
     store(T.ys[:, :], T.ysb[:, :], ["ysb"])
     for h in range(2):
-        c = 256 * (NV - 1) + 128 * h
-        V(ts(T.zb[:, 128 * h:128 * h + 128], T.zl[:, c:c + 128], -9.0, None, Op.add), 128, ["z%d%d" % (NV, h)], ["z0%d" % h])
-        store(T.yz[:, 128 * h:128 * h + 128], T.zb[0:128:16, 128 * h:128 * h + 128], ["z0%d" % h])
+        c, zo = {}, T.zb[:, 128 * h:128 * h + 128]
+        position(NV, h, c, [])
+        VA(ts(zo, pb(c, 0, 128), ZC, None, Op.add), 128, act(zo, pb(c, 0, 128), AF.Identity, ZC), 128, ["zn%d" % h], ["zb%d" % h], use=c)
+        store(T.yz[:, 128 * h:128 * h + 128], T.zb[0:128:16, 128 * h:128 * h + 128], ["zb%d" % h])
     fin = []
     for h in range(2):
         for a in range(4):
-            src = T["tl%d" % NV][:, 128 * h:128 * h + 128, a]
             dst = T.ytb[:, 256 * a + 128 * h:256 * a + 128 * h + 128]
-            key = "yt%d%d" % (h, a)
-            fin.append(key)
-            if a < 2:
-                V(cp(dst, src), 64, ["T%d%d" % (NV, h)], [key])
-            else:
-                A(act(dst, src), 128, ["T%d%d" % (NV, h)], [key])
+            fin.append("yt%d%d" % (h, a))
+            VA(cp(dst, H("tb", h, a, None, 4)), 64, act(dst, H("tb", h, a, None, 4)), 128, ["tb%d" % h], [fin[-1]])
     store(T.yt[:, :], T.ytb[:, :], fin)
     return ops
 
 
-def schedule(ops):
+def schedule(ops, prm):
     n = len(ops)
     succ = [[] for _ in range(n)]
     for i, o in enumerate(ops):
+        o["lat"] = o["sym"][2] if o["sym"] and o["sym"][0] == "dma" else 0.0
         for d in o["deps"]:
             succ[d].append(i)
     pr = [0.0] * n
     for i in range(n - 1, -1, -1):
-        pr[i] = ops[i]["cost"] + 0.04 + max([pr[k] for k in succ[i]], default=0.0)
+        pr[i] = min(ops[i]["cost"].values()) + ops[i]["lat"] + max([pr[k] + (OWN if ops[k]["cost"].keys() & ops[i]["cost"].keys() else HOP) for k in succ[i]], default=0.0)
     pr = [pr[i] + ops[i]["bonus"] for i in range(n)]
     left = [len(o["deps"]) for o in ops]
-    members = {}
-    for i, o in enumerate(ops):
+    pend = {}
+    for o in ops:
         if o["use"] is not None:
-            members.setdefault(o["use"], []).append(i)
-    ready = {e: [] for e in "vapqdn"}
-    for i in range(n):
-        if left[i] == 0:
-            ready[ops[i]["eng"]].append(i)
-    free = {e: 0.0 for e in "vapqdn"}
-    end, order, holder, pend = [0.0] * n, [], {}, {}
-    dep_end = [0.0] * n
+            pend[o["use"]["first"]] = pend.get(o["use"]["first"], 0) + 1
+    ready = [i for i in range(n) if left[i] == 0]
+    free = {e: 0.0 for e in "vapqd"}
+    end, order, dep_end = [0.0] * n, [], [{} for _ in range(n)]
+    holder = {b: None for b in POOL}
+    users = {b: [] for b in POOL}
     while len(order) < n:
+        cand = {}
+        for i in ready:
+            o = ops[i]
+            est, bank = 0.0, None
+            if o["acq"] is not None:
+                open_ = [(max([end[m] + HOP for m in users[b]], default=0.0), b) for b in POOL if holder[b] is None or pend[holder[b]] == 0]
+                if not open_:
+                    continue
+                t0, bank = min(open_)
+                est = max(est, t0)
+            for e in o["cost"]:
+                t1 = max(est, free.get(e, 0.0), dep_end[i].get(e, 0.0))
+                if o["acq"] is None and o["use"] is not None:
+                    t1 = max([t1] + [end[m] + HOP for m in users[o["use"]["bank"]] if ops[m]["eng"] != e])
+                cand.setdefault(e, []).append((t1, i, bank))
         best = None
-        for e in "vapqdn":
-            cand = []
-            for i in ready[e]:
-                o = ops[i]
-                b = o["acq"]
-                est = dep_end[i]
-                if b is not None and b in holder:
-                    tx = holder[b]
-                    if pend[tx] > 0:
-                        continue
-                    est = max(est, max(end[m] for m in members[tx]) + 0.04)
-                if e in "vapq":
-                    est = max(est, free[e])
-                cand.append((est, i))
-            if not cand:
-                continue
-            lo = min(c[0] for c in cand) + WIN
-            est, i = max((c for c in cand if c[0] <= lo), key=lambda c: pr[c[1]])
-            if best is None or est < best[0]:
-                best = (est, i, e)
-        est, i, e = best
+        for e, cs in cand.items():
+            lo = min(c[0] for c in cs) + prm["WIN"]
+            c = max((c for c in cs if c[0] <= lo), key=lambda c: pr[c[1]])
+            if best is None or (c[0], -pr[c[1]]) < (best[0][0], -pr[best[0][1]]):
+                best = (c, e)
+        (est, i, bank), e = best
         o = ops[i]
-        ready[e].remove(i)
+        ready.remove(i)
+        o["eng"] = e
         if o["acq"] is not None:
-            b = o["acq"]
-            if b in holder:
-                for m in members[holder[b]]:
-                    o["deps"].setdefault(m, False)
-            holder[b] = i
-            pend[i] = len(members[i])
+            for m in users[bank]:
+                o["deps"].setdefault(m, False)
+            holder[bank], users[bank] = i, []
+            o["acq"]["bank"] = bank
         if o["use"] is not None:
-            pend[o["use"]] -= 1
-        end[i] = est + o["cost"]
-        if e in "vapq":
+            b = o["use"]["bank"]
+            for m in users[b]:
+                if ops[m]["eng"] != e:
+                    o["deps"].setdefault(m, False)
+            users[b].append(i)
+            pend[o["use"]["first"]] -= 1
+        end[i] = est + o["cost"][e]
+        if e in free:
             free[e] = end[i]
-        order.append((est, i))
+        end[i] += o["lat"]
+        order.append(i)
         for k in succ[i]:
             left[k] -= 1
-            dep_end[k] = max(dep_end[k], end[i] + 0.04)
+            for f in ops[k]["cost"]:
+                dep_end[k][f] = max(dep_end[k].get(f, 0.0), end[i] + (OWN if f == e or f == "n" else HOP))
             if left[k] == 0:
-                ready[ops[k]["eng"]].append(k)
-    return [i for _, i in order], end
+                ready.append(k)
+    return order, end
 
 
 def emit(ops, order, T, gs):
-    lastacc = {}
-    for i in order:
-        if ops[i]["eng"] == "p" and ops[i]["use"] is not None:
-            lastacc[ops[i]["use"]] = i
+    nxt, lastacc = {}, set()
+    for i in reversed(order):
+        if ops[i]["acc"] is not None and ops[i]["tag"] not in nxt:
+            nxt[ops[i]["tag"]] = i
+            lastacc.add(i)
     count = {}
     done = {}
     know = {e: {} for e in "vapqd"}
 
     def after(e, i, raw):
-        o = ops[i]
         sem, val, clk = done[i]
-        if o["eng"] == e == "p" and not raw:
+        if ops[i]["eng"] == e and (e == "p" or sem == "loc") and not raw:
             return
         if know[e].get(sem, 0) >= val:
             return
@@ -532,26 +621,21 @@ def emit(ops, order, T, gs):
         know[e][sem] = max(val, know[e].get(sem, 0))
     for i in order:
         o = ops[i]
-        e = o["eng"]
+        e, kind = o["eng"], (o["sym"] or ("",))[0]
         if e == "n":
-            done[i] = (o["sym"][0], o["sym"][1], {})
+            done[i] = (o["sym"][1], o["sym"][2], {})
             continue
-        ds = sorted(o["deps"].items(), key=lambda d: -done[d[0]][1] if d[0] in done else 0)
-        for d, raw in ds:
+        for d, raw in sorted(o["deps"].items(), key=lambda d: -done[d[0]][1]):
             after(e, d, raw)
-        for x, fn in enumerate(o["fns"]):
-            last = e == "p" and lastacc.get(o["use"]) == i and x == len(o["fns"]) - 1
-            c = fn(last)
-            if e in "vap" or (e == "q" and o["sym"] is None):
-                c.then_inc(T.sem[e], 1)
-                count[e] = count.get(e, 0) + 1
-            elif e == "d":
-                sem, add = o["sym"]
-                c.then_inc(T.sem[sem], add)
-                count[sem] = count.get(sem, 0) + add
+        sem = {"": e, "dma": o["sym"] and o["sym"][-2:-1] and o["sym"][1:2] and o["sym"][1:2][0], "send": "loc"}[kind]
+        for x, fn in enumerate(o["fns"][e]):
+            end = x == len(o["fns"][e]) - 1
+            c = fn(end and i in lastacc)
+            if kind == "send":
+                count[sem] = count.get(sem, 0) + gs["neng"]
             else:
-                count["loc"] = count.get("loc", 0) + gs["neng"]
-        sem = e if e in "vap" or (e == "q" and o["sym"] is None) else ("loc" if e == "q" else o["sym"][0])
+                c.then_inc(T.sem[sem], 16 if kind == "dma" else 1)
+                count[sem] = count.get(sem, 0) + (16 if kind == "dma" else 1)
         done[i] = (sem, count[sem], dict(know[e]))
     gs["d"].wait_ge(T.sem.sto, count["sto"])
     for sem in ("v", "a", "p", "q", "loc"):
@@ -562,9 +646,13 @@ def rank_program(g, core, T, topo):
     rank = T.rank_of(core)
     if rank is None:
         return
-    dst = T.cores[(rank + 1) % len(T.cores)]
-    rid, pid, _ = topo.addr(dst)
-    gs = {"v": g.vector, "a": g.scalar, "p": g.tensor, "q": g, "d": g.sync, "neng": len(topo.engines(core, dst))}
-    ops = build(T, gs, (rid, pid, topo.mask(core, dst)))
-    order, _ = schedule(ops)
+    n = len(T.cores)
+    to = {}
+    for d in range(1, n):
+        dst = T.cores[(rank - d) % n]
+        rid, pid, _ = topo.addr(dst)
+        to[d] = (rid, pid, topo.mask(core, dst))
+    gs = {"v": g.vector, "a": g.scalar, "p": g.tensor, "q": g, "d": g.sync, "neng": len(topo.engines(core, T.cores[(rank - 1) % n]))}
+    ops = build(T, gs, to, PRM)
+    order, _ = schedule(ops, PRM)
     emit(ops, order, T, gs)

@@ -1,24 +1,26 @@
-import numpy as np
-from concourse.mybir import dt, AluOpType as Op, ActivationFunctionType as AF
+from concourse.mybir import AluOpType as Op, ActivationFunctionType as AF
 
 NV = 8
 J = 13
+XP = 2
 PRM = dict(
-    JA=(11, 11),
-    NS=(2, 2),
-    SB=(1, 1),
-    NM=4,
-    XP=4,
-    WIN=0.02,
-    ENG={},
-    BONUS={},
+    JA=(10, 9),
+    NS=(4, 2),
+    SB=(2, 2),
+    NM=6,
+    OA=(0, 0),
+    SUMAFT=1,
+    FAST=(1, 1),
+    WIN=0.0,
+    LAM=10,
+    RANK={('L', 0): -49, ('F', 0): -75, ('L', 1): -171, ('F', 1): -64, ('G', 1): 121, ('G', 0): 73, ('H', 0): 88, ('D', 0): -119, ('S', 0): 80, ('N', 0): 59, ('M', 0): 175, ('E', 0): 58, ('T', 0): -55, ('D', 1): -101, ('H', 1): 238, ('S', 1): 110, ('C', 0): 17, ('N', 1): 1, ('E', 1): 298, ('T', 1): 88, ('X', 0): 6},
+    ENG={('y21', 0): 'va', ('y22', 0): 'va', ('v20', 0): 'va', ('v20', 1): 'va', ('v21', 1): 'va', ('v22', 1): 'va', ('v23', 0): 'v', ('v23', 1): 'va', ('gT', 1): 'a', ('gC', 0): 'a', ('gT', 0): 'a', ('gY', 0): 'a', ('r1', 0): 'v', ('Dc', 1): 'v', ('Lzb', 1): 'v', ('r1', 1): 'v', ('gS', 1): 'v', ('Dc', 0): 'a', ('ind', 1): 'a'},
+    BONUS={('Ssn', 1): 48, ('Lli', 0): 112, ('ysum', 1): 36, ('CAps', 0): -64, ('GOH', 1): 60, ('HK', 1): -72, ('v20', 1): 124, ('GoC', 0): 100, ('v21', 1): 40, ('GoS', 1): 4, ('v22', 1): 12, ('Fcnt', 0): -8, ('y21', 0): 20, ('Gcmp', 1): -48, ('gY', 0): -64, ('Fcmp', 1): -60, ('max', 0): -40, ('vsum', 0): 52, ('v22', 0): 12, ('DXr', 0): -28, ('Hyps', 0): 16, ('Ttof', 1): -40, ('Lzb', 1): 148, ('y22', 0): 24, ('FoS', 0): -28, ('NF', 1): 76, ('S', 1): -68, ('asum', 0): -32, ('asum', 1): -56, ('LdB', 0): -32, ('gS', 1): 40, ('TQ', 1): -68, ('Lcg', 0): 12, ('Est', 1): 76, ('EVa', 0): 40, ('Esum', 0): -32, ('FF', 1): 48, ('Dw', 1): 12, ('gT', 0): 20, ('ind', 0): 20, ('Ttof', 0): 128, ('Gcmp', 0): 24, ('y23', 1): 96, ('Fze', 1): -40, ('Llm', 0): 20, ('Nfi', 1): -20, ('GoC', 1): -8, ('DXt', 1): -64, ('Epre', 0): 40, ('Fze', 0): 20, ('GCr', 0): -20, ('EVa', 1): -20, ('FX', 0): -28, ('FX', 1): -80, ('Lsg', 1): -16, ('Lzn', 0): 20, ('Dks', 0): -28, ('DXd', 1): -20, ('Gcnt', 1): -60, ('Gz', 0): 8, ('Lzn', 1): -4, ('L', 1): -8, ('y22', 1): -28, ('GOH', 0): 68, ('v23', 0): 8, ('DXd', 0): 8, ('Nof', 0): 20, ('S', 0): -20, ('DXr', 1): -68, ('Gz', 1): -80, ('GoS', 0): -20, ('Fzn', 1): -4, ('Ffm', 1): 8, ('Ffi', 0): -40, ('Drr', 1): -16, ('ysum', 0): -8, ('DXt', 0): 20, ('X', 0): -8, ('GU', 1): 12, ('FOH', 0): -8, ('Nprod', 0): -40, ('TQ', 0): -40, ('ind', 1): -32, ('Fof', 0): 40, ('FHb', 1): -40, ('Dc', 0): 20, ('Lcg', 1): 68, ('FOH', 1): 60, ('Fgeb', 0): -40, ('Lsg', 0): -20, ('r1', 1): -20, ('Sdge', 0): -40, ('FF', 0): -20, ('Lzb', 0): -56, ('Fcnt', 1): 20, ('Lyt', 0): -28, ('Fof', 1): -20, ('Dks', 1): 8},
 )
-PRM.update({'JA': (8, 10), 'NS': (2, 4), 'NM': 4, 'XP': 4, 'WIN': 0.02, 'ENG': {('Dc', 0): 'v', ('v23', 1): 'va', ('y22', 0): 'va', ('gC', 1): 'va', ('v21', 1): 'va', ('v22', 1): 'v', ('gT', 1): 'va', ('y21', 1): 'va'}, 'BONUS': {('ysum', 0): -0.5, ('E', 1): -16.0, ('L', 0): 16.0, ('dif', 0): 4.0, ('F', 0): 1.0, ('H', 0): 0.5, ('T', 1): -0.5}, 'SUMAFT': 2, 'SB': (2, 2), 'DUP': 1})
-PRM.update({'JA': (11, 13), 'NS': (2, 4), 'SB': (1, 1), 'NM': 6, 'XP': 4, 'WIN': 0.02, 'ENG': {('Dc', 0): 'v', ('v23', 1): 'va', ('y22', 0): 'va', ('gC', 1): 'va', ('v21', 1): 'va', ('v22', 1): 'v', ('gT', 1): 'va', ('y21', 1): 'va', ('geb', 1): 'a', ('gT', 0): 'a'}, 'BONUS': {('ysum', 0): -0.5, ('E', 1): -8.0, ('L', 0): 0.0, ('dif', 0): 4.0, ('F', 0): 2.0, ('H', 0): 1.0, ('T', 1): -0.5, ('C', 0): 2.0, ('D', 0): -8.0, ('H', 1): 0.5, ('L', 1): -16.0}, 'SUMAFT': 2, 'DUP': 0})
-PRM.update({'JA': (8, 9), 'NS': (1, 2), 'NM': 6, 'XP': 4, 'WIN': 0.02, 'ENG': {('Dc', 0): 'va', ('v23', 1): 'va', ('y22', 0): 'va', ('gC', 1): 'a', ('v21', 1): 'v', ('v22', 1): 'v', ('gT', 1): 'va', ('y21', 1): 'va', ('geb', 1): 'va', ('ind', 1): 'a', ('gT', 0): 'v', ('gC', 0): 'a', ('Dc', 1): 'a'}, 'BONUS': {('ysum', 0): -1.5, ('E', 1): -15.0, ('L', 0): 8.0, ('dif', 0): 4.0, ('F', 0): 3.0, ('H', 0): 0.5, ('T', 1): -0.5, ('T', 0): -8.0, ('ysum', 1): -0.5, ('S', 1): 2.0, ('L', 1): 15.5, ('N', 1): -8.0, ('H', 1): -1.0, ('dif', 1): -0.5, ('C', 0): -16.0}, 'SUMAFT': 0, 'SB': (2, 2)})
-PRM.update({'JA': (11, 10), 'NS': (0, 3), 'SB': (2, 2), 'NM': 5, 'XP': 4, 'WIN': 0.02, 'ENG': {('v21', 1): 'v', ('y20', 0): 'va', ('gT', 0): 'va'}, 'BONUS': {('L', 0): -1.0, ('N', 1): -8.0, ('C', 0): 2.0, ('E', 0): -2.0}, 'SUMAFT': 0, 'FAST': (1, 0)})
-PRM.update({'JA': (10, 8), 'NS': (2, 4), 'SB': (2, 2), 'NM': 4, 'XP': 4, 'WIN': 0.0, 'ENG': {'y20': 'va', 'y21': 'va', 'y22': 'va', 'y23': 'va', 'v20': 'va', 'v21': 'va', 'v22': 'va', 'v23': 'va', ('gT', 1): 'a', ('y22', 1): 'v', ('y20', 0): 'v', ('gC', 0): 'a', ('v22', 0): 'v', ('ind', 0): 'a', ('v23', 0): 'a', ('gT', 0): 'v', ('v20', 0): 'a', ('v20', 1): 'a', ('y22', 0): 'v'}, 'BONUS': {('G', 0): -6.0, ('F', 0): -1.0, ('L', 0): -4.0, ('D', 0): 0.5, ('D', 1): 14.0, ('S', 0): -19.5, ('H', 1): -1.0, ('G', 1): 4.0, ('T', 0): 16.0, ('N', 0): 0.5, ('N', 1): -0.5, ('E', 0): -0.5, ('S', 1): -0.5, ('T', 1): 0.5, ('H', 0): -0.5}, 'SUMAFT': 1, 'DUP': 0, 'FAST': (1, 0)})
-CYC, PEC, HOP, OWN = 0.00083, 0.00042, 0.22, 0.01
+CYC, PEC, HOP, OWN = 0.00083, 0.00042, 0.24, 0.01
+SCN = 300
+LOC, FAR = 0.006, 0.013
+GAT = 1.56
 MAGIC = 201326592.0
 FAKE = 32.0 * 2344 + 16
 ZC = 1600.0
@@ -27,55 +29,51 @@ F32, BF, F16, I32, U16 = "float32", "bfloat16", "float16", "int32", "uint16"
 SCRATCH = {
     "t0s": ("sbuf", [128, 1024], BF), "ytb": ("sbuf", [128, 1024], BF),
     "s0s": ("sbuf", [128, 256], I32), "cfs": ("sbuf", [128, 256], I32), "z0s": ("sbuf", [8, 256], I32), "z0f": ("sbuf", [8, 256], F32),
-    "s0f": ("sbuf", [128, 256], F32), "c0f": ("sbuf", [128, 256], F32), "sg": ("sbuf", [128, 256], F32),
+    "sg": ("sbuf", [128, 256], F32),
     "CG": ("sbuf", [128, NV, 272], F32), "CL": ("sbuf", [128, NV, 272], F32),
     "SN": ("sbuf", [128, NV, 256], F32), "SL": ("sbuf", [128, NV, 256], F32),
     "ysb": ("sbuf", [128, 256], F32), "zb": ("sbuf", [128, 256], F32),
     "li": ("sbuf", [128, 16], I32), "lm": ("sbuf", [128, 16], I32), "lu": ("sbuf", [128, 16], U16),
-    "iP": ("sbuf", [128, 128], I32), "iQ": ("sbuf", [128, 128], I32), "iC": ("sbuf", [128, 104], I32), "iJ": ("sbuf", [128, 104], I32),
-    "iL": ("sbuf", [128, 16], I32), "i64": ("sbuf", [128, 32], I32),
-    "pg": ("sbuf", [128, 128], I32), "qg": ("sbuf", [128, 128], I32), "pm": ("sbuf", [128, 128], I32), "qm": ("sbuf", [128, 128], I32),
+    "iP": ("sbuf", [128, 1], I32), "iQ": ("sbuf", [128, 128], F32), "iL": ("sbuf", [128, 16], F32), "i64": ("sbuf", [128, 32], F32),
+    "pi": ("sbuf", [128, 8], I32), "pf": ("sbuf", [128, 5], F32), "qg": ("sbuf", [128, 128], F32), "qm": ("sbuf", [128, 128], F32),
     "l5": ("sbuf", [128, 16], I32), "LB": ("sbuf", [128, 16], F32), "LF": ("sbuf", [128, 16], F32),
     "E": ("sbuf", [128, 16], F32), "vec": ("sbuf", [128, 32], F32), "gf": ("sbuf", [128, 8], F32),
     "B32": ("sbuf", [128, 128], F32), "Bb": ("sbuf", [128, 128], BF), "Ib": ("sbuf", [128, 128], BF), "Im": ("sbuf", [128, 128], BF),
     "Ih": ("sbuf", [128, 128], F16), "R8": ("sbuf", [8, 128], F32), "R8n": ("sbuf", [8, 128], F32),
+    "Wy": ("sbuf", [128, 128], F32), "tm1": ("sbuf", [128, 128], F32),
     "Wx": ("sbuf", [128, 144], BF), "Wn": ("sbuf", [128, 144], F32), "Wc": ("sbuf", [128, 144], F16), "Wq": ("sbuf", [128, 144], BF),
     "Wu": ("sbuf", [128, 128], F16), "Wz1": ("sbuf", [128, 128], F16), "Wz": ("sbuf", [128, 128], F32), "Wp": ("sbuf", [128, 128], BF),
-    "Wy": ("sbuf", [128, 128], F32), "Wv": ("sbuf", [128, 128], F32), "tm1": ("sbuf", [128, 128], F32), "tm2": ("sbuf", [128, 128], F32),
+    "Wv": ("sbuf", [128, 128], F32), "tm2": ("sbuf", [128, 128], F32), "tm4": ("sbuf", [128, 128], F32),
     "Wd": ("sbuf", [128, 128], F16), "Wf": ("sbuf", [128, 128], F16), "Wk": ("sbuf", [128, 128], F16), "Wm": ("sbuf", [128, 128], F16),
-    "Bn": ("sbuf", [128, 128], F32),
-    "tm3": ("sbuf", [128, 128], F32), "tm4": ("sbuf", [128, 128], F32),
-    "G64": ("sbuf", [128, 8], BF), "Z": ("sbuf", [128, 8, 32], BF), "gr": ("sbuf", [128, 104], F32), "sg1": ("sbuf", [128, 104], F32),
-    "sg2": ("sbuf", [128, 104], F32), "RT0": ("sbuf", [128, 104], BF), "RT1": ("sbuf", [128, 104], BF), "cj": ("sbuf", [128, 104], BF),
-    "kd": ("sbuf", [128, 104], F32), "KD": ("sbuf", [128, 104], F32), "RD": ("sbuf", [128, 256], BF), "w7": ("sbuf", [128, 128], BF),
-    "c205": ("sbuf", [128, 8], BF), "sh": ("sbuf", [128, 32], I32), "q1": ("sbuf", [128, 32], I32), "q2": ("sbuf", [128, 32], I32),
+    "Bn": ("sbuf", [128, 128], F32), "one": ("sbuf", [128, 128], F16),
+    "G64": ("sbuf", [128, 8], BF), "Z": ("sbuf", [128, 8, 32], BF), "gr": ("sbuf", [128, 8, 13], F32),
+    "RT0": ("sbuf", [128, 8, 13], BF), "RT1": ("sbuf", [128, 8, 13], BF), "cj": ("sbuf", [128, 104], BF),
+    "KD": ("sbuf", [128, 104], F32), "RD": ("sbuf", [128, 256], BF), "w7": ("sbuf", [128, 128], BF), "c205": ("sbuf", [128, 8], BF),
     "Qc": ("sbuf", [128, 32], F16),
-    "yps": ("psum", [128, 128, 16], F32), "kb": ("psum", [128, 512], F32),
-    "pb0": ("psum", [128, 512], F32), "pb1": ("psum", [128, 512], F32), "pb2": ("psum", [128, 512], F32),
+    "kb": ("psum", [128, 512], F32), "yps": ("psum", [128, 128, 16], F32),
 }
 POOL = ("pb0", "pb1", "pb2")
+for _b in POOL:
+    SCRATCH[_b] = ("psum", [128, 512], F32)
 for _d in range(4):
     SCRATCH["x%d" % _d] = ("sbuf", [128, 4096], BF)
-    SCRATCH["j%d" % _d] = ("sbuf", [128, 4096], BF)
 _HALF = {"cmp": (256, BF), "geb": (128, BF), "ze": (128, F16), "oS": (256, F32), "oC": (256, F16), "Dc": (128, F32), "Hb": (128, F32), "Left": (128, F32),
          "prod": (128, F32), "fi": (128, I32), "fm": (128, I32), "of": (128, U16), "y2": (2048, BF), "v2": (2048, BF), "Va": (1536, BF),
          "ks": (104, F32), "rr": (8, F32), "Xs": (256, BF), "Xr": (256, BF), "r1": (128, BF), "ind": (128, BF), "tof": (32, U16),
-         "tb": (512, BF), "Ma": (512 * 6, BF)}
+         "tb": (512, BF), "Ma": (512 * 4, BF)}
 for _n, (_c, _d) in _HALF.items():
     SCRATCH[_n] = ("sbuf", [128, 2 * _c], _d)
 for _m in range(6):
     SCRATCH["mb%d" % _m] = ("sbuf", [128, 512], BF)
-SEMAPHORES = ["v", "a", "p", "q", "ls", "lc", "lz", "lt", "loc", "sto"] + ["lx%d" % _k for _k in range(4)]
-for _t in range(NV):
-    SEMAPHORES += ["rC%d" % _t, "rS%d0" % _t, "rS%d1" % _t]
-SEMAPHORES += ["rX%d%d" % (_d, _k) for _d in range(1, 4) for _k in range(8)]
+SEMAPHORES = ["v", "a", "p", "q", "loc", "sto", "ls", "lc", "lz", "lt"] + [_n + str(_k) for _n in ("lx", "rX1", "rX2", "rX3") for _k in range(XP)]
+SEMAPHORES += ["rS%d%d" % (_t, _h) for _t in range(NV) for _h in range(2)] + ["rC%d" % _t for _t in range(NV)]
 
 
 def build(T, gs, to, prm):
     ops, lastw, readers, accs, tag = [], {}, {}, {}, [("I", 0, 0)]
-    JA, NS, NM, XP = prm["JA"], prm["NS"], prm["NM"], prm["XP"]
+    JA, NS, NM = prm["JA"], prm["NS"], prm["NM"]
 
-    def add(fns, cost, rd=(), wr=(), acc=None, acq=None, use=None, after=(), pin=None, name=""):
+    def add(fns, cost, rd=(), wr=(), acc=None, acq=None, use=None, after=(), pin=None, name="", dflt="va"):
         i = len(ops)
         deps = {}
         for k in rd:
@@ -91,23 +89,23 @@ def build(T, gs, to, prm):
                     deps[o] = deps.get(o, False)
             lastw[k], readers[k], accs[k] = i, [], []
         for o in after:
-            deps[o] = deps.get(o, False)
+            deps.setdefault(o, None)
         if acq is not None:
             acq["first"] = i
             use = acq
-        ops.append(dict(fns=fns, cost=cost, deps=deps, acq=acq, use=use, sym=pin, acc=acc, tag=tag[0], name=name,
-                        bonus=prm["BONUS"].get(tag[0][:2], 0.0) + prm["BONUS"].get((name, tag[0][1]), 0.0)))
+        name = name or (tag[0][0] + (list(wr) + [""])[0]).rstrip("0123456789_")
+        ops.append(dict(fns=fns, cost=cost, deps=deps, acq=acq, use=use, sym=pin, acc=acc, tag=tag[0], bonus=0.0, name=name, dflt=dflt,
+                        lat=pin[2] + pin[3] if pin and pin[0] != "land" else 0.0))
         return i
 
     v, s, p, g = gs["v"], gs["a"], gs["p"], gs["q"]
 
-    def VA(fv, cv, fa, ca, rd=(), wr=(), dflt="va", **kw):
-        e = prm["ENG"].get((kw.get("name"), tag[0][1]), prm["ENG"].get(kw.get("name"), dflt))
+    def VA(fv, cv, fa, ca, rd=(), wr=(), **kw):
         fns, cost = {}, {}
-        if fv is not None and ("v" in e or fa is None):
+        if fv is not None:
             fns["v"], cost["v"] = [fv], 0.01 + max(64, cv) * CYC
-        if fa is not None and ("a" in e or fv is None):
-            fns["a"], cost["a"] = [fa], 0.065 + ca * CYC
+        if fa is not None:
+            fns["a"], cost["a"] = [fa], 0.09 + ca * CYC
         return add(fns, cost, rd, wr, **kw)
 
     def V(fn, c, rd=(), wr=(), **kw):
@@ -148,15 +146,20 @@ def build(T, gs, to, prm):
     def ms(out, val):
         return lambda last: v.memset(out, val)
 
-    def load(q, out, a, sem, key, lat):
-        i = add({q: [lambda last: gs[q].dma_start(out, a)]}, {q: 0.05}, (), [key], pin=("dma", sem, lat))
-        ops[i]["bonus"] = 1000.0 - 10.0 * i
-        return i
+    def dmas(pairs, rd, wr, sem, kb, behind=None):
+        return add({"d": [lambda last, x=x: gs["d"].dma_start(x[0], x[1]) for x in pairs]}, {"d": 0.05 * len(pairs)}, rd, wr,
+                   pin=("dma", sem, 0.2 * len(pairs) + kb * LOC, 3.2), after=[lastw[behind]] if behind in lastw else [])
 
-    def send(d, out, in_, sem, rd, key, lat, after=()):
-        rid, pid, mask = to[d]
-        i = add({"q": [lambda last: g.remote_dma(out, in_, T.sem[sem], T.sem.loc, pid, rid, mask)]}, {"q": 0.6}, rd, [], pin=("send",), after=after)
-        add({"n": []}, {"n": lat}, [], [key], after=[i], pin=("land", sem, gs["neng"]))
+    def load(pairs, sem, key, kb):
+        i = dmas(pairs, [], [key], sem, kb)
+        ops[i]["bonus"] = 1000.0 - 10.0 * i
+
+    def send(d, out, in_, sem, rd, key, kb, behind=None, loc="loc"):
+        rid, pid, mask, n = to[d]
+        i = add({"q": [lambda last: g.remote_dma(out, in_, T.sem[sem], T.sem[loc], pid, rid, mask)]}, {"q": 0.6}, rd, [], pin=("send", n, 0.8 + kb * FAR, 0.0, loc),
+                after=[lastw[behind]] if behind in lastw else [])
+        if key:
+            add({"n": []}, {"n": 1.4}, [], [key], after=[i], pin=("land", sem, n))
         return i
 
     def H(name, h, a=0, b=None, step=None):
@@ -165,61 +168,61 @@ def build(T, gs, to, prm):
 
     def gather(out, win, off, n, rd, wr, name, dflt="va", bias=None):
         if bias is None:
-            VA(cp(out, win.indirect(off)), n * 1.5, act(out, win.indirect(off)), n * 1.5, rd, wr, name=name, dflt=dflt)
+            VA(cp(out, win.indirect(off)), 48 + n * GAT, act(out, win.indirect(off)), n * GAT - 30, rd, wr, name=name, dflt=dflt)
         else:
-            VA(ts(out, win.indirect(off), bias, None, Op.add), n * 1.5, act(out, win.indirect(off), AF.Identity, bias), n * 1.5, rd, wr, name=name, dflt=dflt)
+            VA(ts(out, win.indirect(off), bias, None, Op.add), 48 + n * GAT, act(out, win.indirect(off), AF.Identity, bias), n * GAT - 30, rd, wr, name=name, dflt=dflt)
 
-    load("d", T.z0s[:, :], T.z0[:, :], "lz", "z0s", 2.2)
-    load("d", T.s0s[:, :], T.s0[:, :], "ls", "s0s", 2.6)
-    load("d", T.cfs[:, :], T.cf[:, :], "lc", "cfs", 3.0)
-    for k in range(2):
-        load("d", T.x0[:, 2048 * k:2048 * k + 2048], T.xl[:, 2048 * k:2048 * k + 2048], "lx%d" % k, "x0_%d" % k, 5.5 + 2.5 * k)
-    load("d", T.t0s[:, :], T.t0[:, :], "lt", "t0s", 9.0)
     xw = 4096 // XP
-    XK = {0: ["x0_0", "x0_1"]}
+    load([(T.z0s[:, :], T.z0[:, :])], "lz", "z0s", 8)
+    load([(T.s0s[:, :], T.s0[:, :])], "ls", "s0s", 128)
+    load([(T.cfs[:, :], T.cf[:, :])], "lc", "cfs", 128)
+    for k in range(XP):
+        load([(T.x0[:, xw * k:xw * k + xw], T.xl[:, xw * k:xw * k + xw])], "lx%d" % k, "x0_%d" % k, 1024 // XP)
+    load([(T.t0s[:, :], T.t0[:, :])], "lt", "t0s", 256)
+    XK = {d: ["x%d_%d" % (d, k) for k in range(XP)] for d in range(4)}
 
-    def sendlog(d, after):
-        XK[d] = []
+    def sendlog(d, behind):
         for k in range(XP):
-            send(d, T["x%d" % d][:, xw * k:xw * k + xw], T.x0[:, xw * k:xw * k + xw], "rX%d%d" % (d, k), ["x0_%d" % (xw * k // 2048), "x0_%d" % ((xw * k + xw - 1) // 2048)],
-                 "x%d_%d" % (d, k), 2.0 + 10.0 * (k + 1) / XP, after)
-            XK[d].append("x%d_%d" % (d, k))
-            if prm.get("DUP"):
-                send(d, T["j%d" % d][:, xw * k:xw * k + xw], T.x0[:, xw * k:xw * k + xw], "rX%d%d" % (d, k + 4), ["x0_0", "x0_1"], "j%d_%d" % (d, k), 2.0 + 10.0 * (k + 1) / XP, after)
-                XK[d].append("j%d_%d" % (d, k))
-    sendlog(1, ())
+            send(d, T["x%d" % d][:, xw * k:xw * k + xw], T.x0[:, xw * k:xw * k + xw], "rX%d%d" % (d, k), ["x0_%d" % k], "x%d_%d" % (d, k), 1024 // XP, behind)
+    sendlog(1, None)
 
-    def iota(name, pat, base, cm):
-        add({"q": [lambda last: g.iota(T[name][:, :], pat, base, cm)]}, {"q": 0.35}, (), [name])
-    iota("iP", [[0, 128]], 0, 1)
-    iota("iQ", [[1, 128]], 0, 0)
-    iota("iL", [[16, 16]], 0, 0)
-    iota("iC", [[1, 8], [0, 13]], 0, 0)
-    iota("iJ", [[0, 8], [1, 13]], 0, 0)
-    iota("i64", [[64, 32]], -4, 0)
+    def iota(out, key, pat, base, cm, n):
+        if key == "iP":
+            add({"q": [lambda last: g.iota(out, pat, base, cm)]}, {"q": 0.13 + 2 * n * CYC}, (), [key])
+        else:
+            add({"q": [lambda last: g.iota(out, pat, base, cm, allow_small_or_imprecise_dtypes=True)]}, {"q": 0.13 + 2 * n * CYC}, (), [key])
     A0 = lambda n, a=0, b=None: T[n][:, a:b] if b is not None else T[n][:, :]
+    iota(A0("iP"), "iP", [[0, 1]], 0, 1, 1)
+    iota(A0("iL"), "iL", [[16, 16]], 0, 0, 16)
+    iota(A0("qg"), "qg", [[1, 8], [0, 16]], 0, 0, 128)
+    iota(A0("qm"), "qm", [[0, 8], [1, 16]], 0, 0, 128)
+    iota(A0("iQ"), "iQ", [[1, 128]], 0, -1, 128)
+    iota(T.CG[:, :, 256:272], "pad", [[0, 128]], 0, 0, 128)
+    iota(T.cj[:, :], "cj", [[0, 8], [1, 13]], -6, 0, 104)
+    iota(T.gr[:, :, :], "iC", [[1, 8], [0, 13]], 0, 0, 104)
+    iota(A0("i64"), "i64", [[64, 32]], -4, 0, 32)
 
     def C(fn, c, rd, wr):
         return V(fn, c, rd, [wr])
 
-    def scaled(out, a, col, rd, wr, n):
-        VA(ts(out, a, col, None, Op.mult), n, act(out, a, AF.Identity, 0.0, col), n, rd, [wr])
-    C(ts(A0("pm"), A0("iP"), 15, None, Op.bitwise_and), 128, ["iP"], "pm")
-    C(tt(A0("LB"), A0("iL"), A0("pm", 0, 16), Op.add), 16, ["iL", "pm"], "LB")
+    def scaled(out, a, col, rd, wr, n, bias=0.0):
+        VA(ts(out, a, col, bias, Op.mult, Op.add), n, act(out, a, AF.Identity, bias, col), n, rd, [wr])
+    for x, (sh_, and_) in enumerate(((0, 15), (4, 7), (0, 3), (2, 3), (0, 127))):
+        C(ts(T.pi[:, x:x + 1], A0("iP"), sh_, and_, Op.arith_shift_right, Op.bitwise_and), 1, ["iP"], "pi%d" % x)
+    C(cp(A0("pf"), T.pi[:, 0:5]), 5, ["pi%d" % x for x in range(5)], "pf")
+    pm, pg, pa, pp = (T.pf[:, x:x + 1] for x in (0, 1, 3, 4))
+    scaled(A0("LB"), A0("iL"), 1.0, ["iL", "pf"], "LB", 16, pm)
     C(ts(A0("l5"), A0("LB"), 5.0, None, Op.mult), 16, ["LB"], "l5")
-    C(ts(A0("LF"), A0("LB"), 205.0, None, Op.mult), 16, ["LB"], "LF")
-    C(ts(A0("qg"), A0("iQ"), 4, None, Op.arith_shift_right), 128, ["iQ"], "qg")
-    C(ts(A0("pg"), A0("iP"), 4, None, Op.arith_shift_right), 128, ["iP"], "pg")
-    C(ts(A0("qm"), A0("iQ"), 15, None, Op.bitwise_and), 128, ["iQ"], "qm")
-    C(tt(A0("B32"), A0("pg"), A0("qg"), Op.is_equal), 256, ["pg", "qg"], "B32")
-    C(tt(T.R8[:, :], T.iP[0:8, :], T.qg[0:8, :], Op.is_equal), 256, ["iP", "qg"], "R8")
+    scaled(A0("LF"), A0("LB"), 205.0, ["LB"], "LF", 16)
+    C(ts(A0("B32"), A0("qg"), pg, None, Op.is_equal), 128, ["pf", "qg"], "B32")
+    C(ts(T.R8[:, :], T.qg[0:8, :], T.pf[0:8, 4:5], None, Op.is_equal), 128, ["pf", "qg"], "R8")
     scaled(T.R8n[:, :], T.R8[:, :], -1.0, ["R8"], "R8n", 128)
     scaled(A0("Bb"), A0("B32"), 1.0, ["B32"], "Bb", 128)
-    C(tt(A0("Ib"), A0("iP"), A0("iQ"), Op.is_equal), 256, ["iP", "iQ"], "Ib")
+    C(ts(A0("Ib"), A0("iQ"), 0.0, None, Op.is_equal), 128, ["iQ"], "Ib")
     scaled(A0("Im"), A0("Ib"), -1.0, ["Ib"], "Im", 128)
     scaled(A0("Ih"), A0("Ib"), 1.0, ["Ib"], "Ih", 128)
-    C(tt(A0("gf"), T.pg[:, 0:8], T.iQ[:, 0:8], Op.is_equal), 16, ["pg", "iQ"], "gf")
-    C(tt(A0("E"), T.pm[:, 0:16], T.iQ[:, 0:16], Op.is_equal), 32, ["pm", "iQ"], "E")
+    C(ts(A0("gf"), T.qm[:, 0:8], pg, None, Op.is_equal), 8, ["pf", "qm"], "gf")
+    C(ts(A0("E"), T.qm[:, 0:16], pm, None, Op.is_equal), 16, ["pf", "qm"], "E")
     nvec = [0]
 
     def column(terms):
@@ -227,86 +230,76 @@ def build(T, gs, to, prm):
         nvec[0] += 1
         out, key = T.vec[:, n:n + 1], "vec%d" % n
         for y, (x, c) in enumerate(terms.items()):
-            if y == 0:
-                C(ts(out, T.E[:, x:x + 1], float(c), None, Op.mult), 1, ["E"], key)
-            else:
-                C(ts(out, T.E[:, x:x + 1], float(c), out, Op.mult, Op.add), 1, ["E", key], key)
+            scaled(out, T.E[:, x:x + 1], float(c), ["E", key], key, 1, out if y else 0.0)
         return out, key
-
-    def affine(c0, c1):
-        n = nvec[0]
-        nvec[0] += 1
-        C(ts(T.vec[:, n:n + 1], T.pm[:, 0:1], c1, c0, Op.mult, Op.add), 1, ["pm"], "vec%d" % n)
-        return T.vec[:, n:n + 1], "vec%d" % n
-    rp1, rp1k = affine(1.0, 1.0)
+    rp1, rp1k = T.vec[:, 30:31], "vec30"
+    scaled(rp1, pm, 1.0, ["pf"], rp1k, 1, 1.0)
+    rn1, oh1, oh2 = ((T.vec[:, x:x + 1], "vec%d" % x) for x in (28, 27, 26))
+    scaled(rn1[0], rp1, -1.0, [rp1k], rn1[1], 1)
+    scaled(oh1[0], T.E[:, 0:1], 0.5, ["E", rn1[1]], oh1[1], 1, rn1[0])
+    scaled(oh2[0], T.E[:, 0:1], 0.5, ["E"], oh2[1], 1, 1.0)
     zsc, zsck = column({0: 1, 1: -1, 2: -1})
-    zbi, zbik = column({2: 16 - ZC, 3: 1})
-    dbs = column({1: -0.5, 2: 1, 4: -0.5, 5: -0.5, 6: 1, 7: 1, 9: 1})
+    zbi, zbik = column({2: ZC - 16, 3: 1})
+    dbs = column({1: -0.5, 2: 1, 4: -0.5, 6: 1, 7: 1, 9: 1})
     dbf = (T.vec[:, 31:32], "vec31")
-    C(tt(dbf[0], dbs[0], T.E[:, 0:1], Op.add), 1, [dbs[1], "E"], dbf[1])
+    scaled(dbf[0], T.E[:, 0:1], 1.0, [dbs[1], "E"], dbf[1], 1, dbs[0])
     for n_ in ("Wx", "Wc", "Wq", "Wu"):
         C(ms(A0(n_), 0.0), 72, [], n_)
     scaled(T.Wx[:, 15:128:16], A0("gf"), 1.0, ["gf", "Wx"], "Wx", 8)
     scaled(A0("Wn"), A0("Wx"), -1.0, ["Wx"], "Wn", 144)
-    for q_, c_ in ((3, 1.0), (4, 0.5), (8, 0.5)):
+    for q_, c_ in ((3, 1.0), (4, 0.5), (8, 1.0)):
         scaled(T.Wc[:, q_:128:16], A0("gf"), c_, ["gf", "Wc"], "Wc", 8)
-    C(cp(A0("Wd"), T.Wc[:, 3:131]), 64, ["Wc"], "Wd")
+    scaled(A0("Wd"), T.Wc[:, 3:131], 1.0, ["Wc"], "Wd", 128)
     C(ms(T.Wd[:, 0:128:16], 0.0), 8, ["Wd"], "Wd")
     scaled(A0("Bn"), A0("B32"), -1.0, ["B32"], "Bn", 128)
-    vK = column({3: -18.5})
-    scaled(A0("Wk"), A0("B32"), vK[0], ["B32", vK[1]], "Wk", 128)
-    C(ts(A0("tm4"), A0("qm"), 9.5, None, Op.add), 128, ["qm"], "tm4")
+    scaled(A0("Wk"), A0("B32"), -18.5 / 16, ["B32"], "Wk", 128)
+    C(ms(A0("one"), 1.0), 64, [], "one")
+    scaled(A0("tm4"), A0("qm"), 1.0, ["qm"], "tm4", 128, 9.5)
     C(tt(A0("Wm"), A0("tm4"), A0("B32"), Op.mult), 256, ["tm4", "B32"], "Wm")
     for q_ in range(12, 16):
         scaled(T.Wq[:, q_:128:16], A0("gf"), 1.0, ["gf", "Wq"], "Wq", 8)
-    vA, vB, vD, vE = column({0: 1, 1: -1}), column({0: 1, 1: -1, 2: 1, 3: -16}), column({2: -1, 3: 16}), (T.E[:, 3:4], "E")
+    vA, vB, vD, vE = column({0: 1, 1: -1}), column({0: 1, 1: -1, 2: 1, 3: -ZC}), column({2: -1, 3: ZC}), (T.E[:, 3:4], "E")
     for q_, (c_, k_) in ((0, vA), (1, vE), (2, vD), (3, vB), (4, vE), (5, vE), (6, vE), (7, vB), (9, vE)):
         scaled(T.Wu[:, q_:128:16], A0("gf"), c_, ["gf", "Wu", k_], "Wu", 8)
-    C(cp(A0("Wf"), A0("Wu")), 64, ["Wu"], "Wf")
+    scaled(A0("Wf"), A0("Wu"), 1.0, ["Wu"], "Wf", 128)
     C(ms(T.Wf[:, 0:128:16], 0.0), 8, ["Wf"], "Wf")
     scaled(A0("Wz1"), A0("B32"), vB[0], ["B32", vB[1]], "Wz1", 128)
     vZ = column({2: 1, 7: 1, 9: -1})
     scaled(A0("Wz"), A0("B32"), vZ[0], ["B32", vZ[1]], "Wz", 128)
-    for w_, tm_, al, be in (("Wy", "tm1", {1: 2, 6: 1}, {0: 1, 1: 19, 6: -9}),
-                            ("Wv", "tm2", {1: 2, 4: 2, 9: 1}, {0: 1, 3: 1, 1: 37, 4: 37, 5: -2, 6: -1})):
-        (a_, ak), (b_, bk) = column(al), column(be)
-        C(ts(A0(tm_), A0("qm"), a_, b_, Op.mult, Op.add), 128, ["qm", ak, bk], tm_)
-        C(tt(A0(w_), A0(tm_), A0("B32"), Op.mult), 256, [tm_, "B32"], w_)
-    C(ts(A0("tm3"), A0("qm"), rp1, -1.0, Op.subtract, Op.is_ge), 128, ["qm", rp1k], "tm3")
-    C(tt(A0("Wp"), A0("tm3"), A0("B32"), Op.mult), 256, ["tm3", "B32"], "Wp")
+    (a_, ak), (b_, bk) = column({1: 2, 6: 1}), column({0: 1, 1: 19, 6: -9})
+    scaled(A0("tm1"), A0("qm"), a_, ["qm", ak, bk], "tm1", 128, b_)
+    C(tt(A0("Wy"), A0("tm1"), A0("B32"), Op.mult), 256, ["tm1", "B32"], "Wy")
+    (a_, ak), (b_, bk) = column({1: 2, 4: 2, 9: 1}), column({0: 1, 3: 1, 1: 37, 4: 37, 5: -1})
+    scaled(A0("tm2"), A0("qm"), a_, ["qm", ak, bk], "tm2", 128, b_)
+    C(tt(A0("Wv"), A0("tm2"), A0("B32"), Op.mult), 256, ["tm2", "B32"], "Wv")
+    add({"q": [lambda last: g.affine_select(A0("Wp"), A0("Bb"), [[1, 128]], Op.is_ge, 0.0, 0, -1)]}, {"q": 0.4}, ["Bb"], ["Wp"])
     scaled(A0("G64"), A0("gf"), 64.0, ["gf"], "G64", 8)
     C(ms(T.Z[:, :, :], 0.0), 128, [], "Z")
     for k in range(4):
         scaled(T.Z[:, :, 16 + k], A0("gf"), -32.0, ["gf", "Z"], "Z", 8)
-    C(ts(A0("cj"), A0("iJ"), -6.0, None, Op.add), 104, ["iJ"], "cj")
-    C(ts(A0("kd"), A0("iJ"), 0.0, 2 * FAKE, Op.is_equal, Op.mult), 104, ["iJ"], "kd")
-    C(ts(A0("KD"), A0("kd"), -FAKE, None, Op.add), 104, ["kd"], "KD")
-    C(tt(A0("gr"), T.pg[:, 0:104], A0("iC"), Op.is_equal), 208, ["pg", "iC"], "gr")
-    for h in range(2 if JA[0] != JA[1] else 1):
-        C(ts(A0("sg1"), A0("iJ"), float(JA[h]), 64.0, Op.is_ge, Op.mult), 104, ["iJ"], "sg1")
-        C(ts(A0("sg2"), A0("sg1"), -32.0, None, Op.add), 104, ["sg1"], "sg2")
-        C(tt(A0("RT%d" % h), A0("sg2"), A0("gr"), Op.mult), 208, ["sg2", "gr"], "RT%d" % h)
+    C(ms(A0("KD"), -FAKE), 104, [], "KD")
+    C(ms(T.KD[:, 0:104:13], FAKE), 8, ["KD"], "KD")
+    C(ts(T.gr[:, :, :], T.gr[:, :, :], pg, None, Op.is_equal), 104, ["pf", "iC"], "gr")
     RT = ["RT0", "RT%d" % (JA[0] != JA[1])]
+    for h in range(2 if JA[0] != JA[1] else 1):
+        for a_, b_, c_ in ((0, JA[h], -32.0), (JA[h], J, 32.0)):
+            scaled(T[RT[h]][:, :, a_:b_], T.gr[:, :, a_:b_], c_, ["gr", RT[h]], RT[h], 8 * (b_ - a_))
     C(ms(A0("RD"), 1.0), 128, [], "RD")
     for a_, b_, c_ in ((0, 256, 0.0), (3, 128, -1.0), (5, 128, 0.0), (7, 128, 0.0)):
         C(ms(T.RD[:, a_:b_:16], c_), 16, ["RD"], "RD")
-    C(ts(A0("sh"), T.pm[:, 0:32], 2, None, Op.arith_shift_right), 32, ["pm"], "sh")
-    C(ts(A0("q1"), A0("sh"), 12.0, None, Op.mult), 32, ["sh"], "q1")
-    C(tt(A0("q2"), A0("q1"), T.pm[:, 0:32], Op.add), 64, ["q1", "pm"], "q2")
-    C(tt(A0("Qc"), A0("q2"), A0("i64"), Op.add), 64, ["q2", "i64"], "Qc")
+    scaled(T.vec[:, 29:30], pa, 12.0, ["pf"], "vec29", 1, pm)
+    scaled(A0("Qc"), A0("i64"), 1.0, ["i64", "vec29"], "Qc", 32, T.vec[:, 29:30])
     C(ms(A0("w7"), 2.0 ** -7), 64, [], "w7")
     C(ms(A0("c205"), 205.0), 8, [], "c205")
-    C(ms(T.CG[:, :, 256:272], 0.0), 128, [], "pad")
     C(ms(A0("Xs"), 0.0), 256, [], "Xs")
     for h in range(2):
         C(ms(H("Xs", h, 3, 128, 4), 1.0), 32, ["Xs"], "Xs%d" % h)
         C(ms(H("Xs", h, 11, 128, 16), 0.0), 8, ["Xs%d" % h], "Xs%d" % h)
         C(ms(H("Xs", h, 15, 128, 16), 0.0), 8, ["Xs%d" % h], "Xs%d" % h)
 
-    C(ts(T.z0f[:, :], T.z0s[:, :], -ZC, None, Op.add), 256, ["z0s"], "z0f")
-    C(ts(A0("s0f"), A0("s0s"), -ZC, None, Op.add), 256, ["s0s"], "s0f")
-    C(ts(A0("c0f"), A0("cfs"), 2.0, 1.0, Op.mult, Op.add), 256, ["cfs"], "c0f")
     for h in range(2):
+        hs = str(h)
+        C(ts(T.z0f[:, 128 * h:128 * h + 128], T.z0s[:, 128 * h:128 * h + 128], -ZC, None, Op.add), 128, ["z0s"], "z0f" + hs)
         for a in range(4):
             src = T.t0s[:, 256 * a + 128 * h:256 * a + 128 * h + 128]
             VA(cp(H("tb", h, a, None, 4), src), 64, act(H("tb", h, a, None, 4), src), 128, ["t0s"], ["tb%d" % h] if a == 0 else ["tb%d_%d" % (h, a)])
@@ -317,30 +310,36 @@ def build(T, gs, to, prm):
         if t == 0:
             C(ts(A0("lm"), A0("l5"), 255, None, Op.bitwise_and), 16, ["l5"], "lm")
         else:
-            c = {}
-            fns = [mm(pb(c, 0, 1), T.R8n[:, :], T.CL[0:8, t - 1, 256:257], True, t == NV)]
+            c, fns = {}, []
+            if t > 1:
+                fns.append(mm(pb(c, 0, 1), T.R8n[:, :], T.CL[0:8, t - 1, 256:257], True, t == NV))
             if t < NV:
-                fns.append(mm(pb(c, 0, 1), T.R8[:, :], T.CG[0:8, t, 256:257], False, True))
-            P(fns, 512, ["R8", "R8n", "C%d" % (t - 1)] + (["B%d" % t] if t < NV else []), ["dB"], acq=c)
+                fns.append(mm(pb(c, 0, 1), T.R8[:, :], T.CG[0:8, t, 256:257], t == 1, True))
+            P(fns, 256 * len(fns), ["R8", "R8n"] + (["C%d" % (t - 1)] if t > 1 else []) + (["B%d" % t] if t < NV else []), ["dB"], acq=c)
             V(ts(A0("li"), A0(base), pb(c, 0, 1), None, Op.add), 16, [base, "dB"], ["li"], use=c)
             C(ts(A0("lm"), A0("li"), 255, None, Op.bitwise_and), 16, ["li"], "lm")
         C(cp(A0("lu"), A0("lm")), 16, ["lm"], "lu")
 
     def tables(t):
         rotation(t, "LB")
-        sw, sk = (T.s0f[:, :], ["s0f"]) if t == 0 else (T.SL[:, t - 1, :], ["S%d0" % (t - 1), "S%d1" % (t - 1)])
-        cw, ck = (T.c0f[:, :], ["c0f"]) if t == 0 else (T.CL[:, t - 1, 0:256], ["C%d" % (t - 1)])
         for h in range(2):
             tag[0] = ("L", h, t)
-            gather(T.sg[:, 128 * h:128 * h + 128], sw, T.lu[:, 8 * h:8 * h + 8], 128, ["lu"] + sk, ["sg%d" % h], "gS")
-            gather(T.CG[:, t, 128 * h:128 * h + 128], cw, T.lu[:, 8 * h:8 * h + 8], 128, ["lu"] + ck, ["cg%d%d" % (t, h)], "gC")
+            hs, lu = str(h), A0("lu", 8 * h, 8 * h + 8)
+            sg, cg = T.sg[:, 128 * h:128 * h + 128], T.CG[:, t, 128 * h:128 * h + 128]
+            if t == 0:
+                V(ts(sg, A0("s0s").indirect(lu), -ZC, None, Op.add), 248, ["lu", "s0s"], ["sg" + hs])
+                V(ts(cg, A0("cfs").indirect(lu), 2.0, 1.0, Op.mult, Op.add), 248, ["lu", "cfs"], ["cg%d%d" % (t, h)])
+            else:
+                gather(sg, T.SL[:, t - 1, :], lu, 128, ["lu", "S%d0" % (t - 1), "S%d1" % (t - 1)], ["sg" + hs], "gS")
+                gather(cg, T.CL[:, t - 1, 0:256], lu, 128, ["lu", "C%d" % (t - 1)], ["cg%d%d" % (t, h)], "gC")
+        tag[0] = ("M", 0, t)
         a = 0 if t < NV - 1 else 256
-        send(1, T.CL[:, t, a:272], T.CG[:, t, a:272], "rC%d" % t, ["cg%d0" % t, "cg%d1" % t, "pad", "B%d" % t], "C%d" % t, 3.0)
+        send(1, T.CL[:, t, a:272], T.CG[:, t, a:272], "rC%d" % t, ["cg%d0" % t, "cg%d1" % t, "pad", "B%d" % t], "C%d" % t, (272 - a) // 2)
 
     def position(t, h, c, extra):
         hs = str(h)
         if t == 0:
-            P([mm(pb(c, 0, 128), T.R8[:, :], T.z0f[:, 128 * h:128 * h + 128])], 512, ["R8", "z0f"] + extra, ["zn" + hs], acq=c)
+            P([mm(pb(c, 0, 128), T.R8[:, :], T.z0f[:, 128 * h:128 * h + 128])], 512, ["R8", "z0f" + hs] + extra, ["zn" + hs], acq=c)
         else:
             P([mm(pb(c, 0, 128), A0("Wz"), H("prod", h), True, False), mm(pb(c, 0, 128), A0("Bb"), H("ind", h), False, True)], 640,
               ["Wz", "Bb", "prod" + hs, "ind" + hs] + extra, ["zn" + hs], acq=c)
@@ -360,58 +359,62 @@ def build(T, gs, to, prm):
     def front(t, h):
         hs = str(h)
         sg, cg, sk, ck = T.sg[:, 128 * h:128 * h + 128], T.CG[:, t, 128 * h:128 * h + 128], "sg" + hs, "cg%d%d" % (t, h)
-        c = {}
+        c, fast = {}, prm["FAST"][h]
         position(t, h, c, ["lu"])
-        A(act(H("ze", h), pb(c, 0, 128), AF.Relu, zbi, zsc), 128, ["zn" + hs, zsck, zbik], ["ze" + hs], use=c)
         V(tt(H("cmp", h, 0, 128), pb(c, 0, 128), sg, Op.is_ge), 128, ["zn" + hs, sk], ["cmp0" + hs], use=c)
-        fast = prm["FAST"][h]
         if fast:
             V(tt(pb(c, 128, 256), sg, pb(c, 0, 128), Op.subtract), 128, ["zn" + hs, sk], ["X" + hs], use=c)
             V(tt(H("Hb", h), pb(c, 128, 256), cg, Op.mult), 128, ["X" + hs, ck], ["Hb" + hs], use=c)
+        V(ts(H("ze", h), pb(c, 0, 128), zsc, zbi, Op.mult, Op.max), 128, ["zn" + hs, zsck, zbik], ["ze" + hs], use=c)
         for b in range(2):
             c, bs = {}, str(b) + hs
             if b == 1:
-                tag[0] = ("G" if fast else "F", h, t)
+                tag[0] = ("G", h, t)
                 P([mm(pb(c, 0, 128), A0("Wz1"), H("ze", h))], 128, ["Wz1", "ze" + hs], ["z1" + hs], acq=c)
                 V(tt(H("cmp", h, 128, 256), pb(c, 0, 128), sg, Op.is_ge), 128, ["z1" + hs, sk], ["cmp1" + hs], use=c)
                 c = {}
             src, srck = (H("Hb", h), "Hb" + hs) if fast and b == 0 else (sg, sk)
             P([mm(pb(c, 0, 128), A0("Bb"), H("cmp", h, 128 * b, 128 * b + 128))], 128, ["Bb", "cmp" + bs], ["cnt" + bs], acq=c)
-            V(ts(pb(c, 128, 256), pb(c, 0, 128), 1.0, rp1, Op.max, Op.is_equal), 128, ["cnt" + bs, rp1k], ["OH" + bs], use=c)
+            if b == 1 and prm["OA"][h]:
+                A(act(pb(c, 256, 384), pb(c, 0, 128), AF.Abs, oh1[0]), 128, ["cnt" + bs, oh1[1]], ["Oa" + hs], use=c)
+                A(act(pb(c, 128, 256), pb(c, 256, 384), AF.Relu, oh2[0], -1.0), 128, ["Oa" + hs, oh2[1]], ["OH" + bs], use=c)
+            else:
+                V(ts(pb(c, 128, 256), pb(c, 0, 128), 1.0, rp1, Op.max, Op.is_equal), 128, ["cnt" + bs, rp1k], ["OH" + bs], use=c)
             V(tt(H("oC", h, 128 * b, 128 * b + 128), pb(c, 128, 256), cg, Op.mult), 128, ["OH" + bs, ck], ["oC" + bs], use=c)
             V(tt(H("oS", h, 128 * b, 128 * b + 128), pb(c, 128, 256), src, Op.mult), 128, ["OH" + bs, srck], ["oS" + bs], use=c)
             if b == 0:
-                V(ts(H("geb", h), pb(c, 0, 128), rp1, None, Op.is_le), 128, ["cnt" + bs, rp1k], ["geb" + hs], use=c, name="geb")
+                V(ts(H("geb", h), pb(c, 0, 128), rp1, None, Op.is_le), 128, ["cnt" + bs, rp1k], ["geb" + hs], use=c)
                 if fast:
-                    columns(h, [("Wk", H("ze", h), "ze" + hs, 128), ("Wm", H("oC", h, 0, 128), "oC0" + hs, 128), ("Bn", H("oS", h, 0, 128), "oS0" + hs, 512)], "y2", t)
+                    columns(h, [("Wk", A0("one"), "one", 128), ("Wm", H("oC", h, 0, 128), "oC0" + hs, 128), ("Bn", H("oS", h, 0, 128), "oS0" + hs, 512)], "y2", t)
         c = {}
-        wu, wc, (db, dbk) = ("Wf", T.Wd[:, :], dbf) if fast else ("Wu", T.Wc[:, 3:131], dbs)
+        wu, wc, db = ("Wf", T.Wd[:, :], dbf) if fast else ("Wu", T.Wc[:, 3:131], dbs)
         P([mm(pb(c, 0, 128), A0(wu), H("ze", h), True, False), mm(pb(c, 0, 128), T.Wn[:, 15:143], H("oS", h, 0, 128), False, False),
            mm(pb(c, 0, 128), T.Wn[:, 12:140], H("oS", h, 128, 256), False, True)], 1152, [wu, "Wn", "ze" + hs, "oS0" + hs, "oS1" + hs], ["U" + hs], acq=c)
         P([mm(pb(c, 128, 256), wc, H("oC", h, 0, 128), True, False), mm(pb(c, 128, 256), T.Wc[:, 0:128], H("oC", h, 128, 256), False, True)], 256,
           ["Wc", "Wd", "oC0" + hs, "oC1" + hs], ["Cr" + hs], use=c, after=[c["first"]])
-        VA(ts(H("Dc", h), pb(c, 128, 256), db, None, Op.add), 128, act(H("Dc", h), pb(c, 128, 256), AF.Identity, db), 128, ["Cr" + hs, dbk], ["Dc" + hs], use=c, name="Dc")
+        VA(ts(H("Dc", h), pb(c, 128, 256), db[0], None, Op.add), 128, act(H("Dc", h), pb(c, 128, 256), AF.Identity, db[0]), 128, ["Cr" + hs, db[1]], ["Dc" + hs], use=c, name="Dc")
         V(tt(H("Left", h), pb(c, 0, 128), H("Dc", h), Op.mult), 128, ["U" + hs, "Dc" + hs], ["Left" + hs], use=c)
         if not fast:
+            tag[0] = ("F", h, t)
             columns(h, [("Wy", H("Left", h), "Left" + hs, 512)], "y2", t)
 
     def match(t, h):
         hs = str(h)
         TK = ["tb" + hs] + (["tb%d_%d" % (h, a) for a in (1, 2, 3)] if t == 0 else [])
         K = T.kb[:, 0:104]
-        P([mm(K, A0("w7"), A0("cj"), True, False)] + [mm(K, H("tb", h, a, None, 4), A0(RT[h]), False, False) for a in range(4)], 520,
+        P([mm(K, A0("w7"), A0("cj"), True, False)] + [mm(K, H("tb", h, a, None, 4), T[RT[h]][:, :, :], False, False) for a in range(4)], 520,
           ["w7", "cj", RT[h], "y2%s_0" % hs] + TK, ["K"])
-        P([mm(K, H("y2", h, m, None, 16), T.Z[:, :, 19 - m:32 - m], False, False) for m in range(16)], 1664, YK("y2", h) + ["Z"], [], acc="K", name="ysum")
+        y = lambda m: H("y2", h, m, None, 16)
+        P([mm(K, y(m), T.Z[:, :, 19 - m:32 - m], False, False) for m in range(16)], 1664, YK("y2", h) + ["Z"], [], acc="K", name="ysum")
         for b in range(4):
             P([mm(T.yps[:, 32 * b:32 * b + 32, :], A0("Ib"), H("y2", h, 512 * b, 512 * b + 512))], 512, ["y2%s_%d" % (hs, b), "Ib"], ["yps%d" % b])
         for x, j in enumerate(range(JA[h], J)):
             c = {}
-            P([mm(pb(c, 0, 512), A0("Im"), H("tb", h), True, False)] +
-              [mm(pb(c, a, 512, 4), A0("Ib"), H("y2", h, j + a, None, 16), False, a == 3) for a in range(4)], 1024,
+            P([mm(pb(c, 0, 512), A0("Im"), H("tb", h), True, False)] + [mm(pb(c, a, 512, 4), A0("Ib"), y(j + a), False, a == 3) for a in range(4)], 1024,
               YK("y2", h) + TK + ["Ib", "Im"], ["dif%s%d" % (hs, x)], acq=c, name="dif")
             A(act(H("Ma", h, 512 * x, 512 * x + 512), pb(c, 0, 512), AF.Relu), 512, ["dif%s%d" % (hs, x)], ["Ma%s%d" % (hs, x)], use=c)
             P([mm(T.kb[:, j:104:13], H("Ma", h, 512 * x + a, 512 * x + 512, 4), A0("G64"), False, False) for a in range(4)],
-              256, ["Ma%s%d" % (hs, x), "G64"], [], acc="K")
+              256, ["Ma%s%d" % (hs, x), "G64"], [], acc="K", name="asum")
         bufs = []
         for j in range(JA[h]):
             bufs.append(mcount[0] % NM)
@@ -421,37 +424,40 @@ def build(T, gs, to, prm):
         for j, b0, b1 in order:
             M, mk = T["mb%d" % bufs[j]], "mb%d" % bufs[j]
             prev = [V(tt(M[:, 128 * b0:128 * b1], T.yps[:, 32 * b0:32 * b1, j:j + 4], H("tb", h, 128 * b0, 128 * b1), Op.max), 128 * (b1 - b0),
-                      ["yps%d" % b for b in range(b0, b1)] + TK, [mk + "_%d" % b for b in range(b0, b1, 2)], after=prev)]
+                      ["yps%d" % b for b in range(b0, b1)] + TK, [mk + "_%d" % b for b in range(b0, b1, 2)], after=prev, name="max")]
             if b1 == 4:
-                P([mm(T.kb[:, j:104:13], M[:, a:512:4], A0("G64"), False, False) for a in range(4)], 256, [mk + "_0", mk + "_2", "G64"], [], acc="K")
-        V(scan(H("ks", h), A0("KD"), K, Op.max, Op.min), 104, ["K", "KD"], ["ks" + hs])
+                P([mm(T.kb[:, j:104:13], M[:, a:512:4], A0("G64"), False, False) for a in range(4)], 256, [mk + "_0", mk + "_2", "G64"], [], acc="K", name="vsum")
+        tag[0] = ("D", h, t)
+        V(scan(H("ks", h), A0("KD"), K, Op.max, Op.min), SCN + 104, ["K", "KD"], ["ks" + hs])
 
     def decide(t, h):
         hs = str(h)
         best = H("ks", h, 12, None, 13)
         V(ts(H("rr", h), best, MAGIC, MAGIC, Op.add, Op.subtract), 8, ["ks" + hs], ["rr" + hs])
+        c = {}
         V(ts(H("Xs", h, 0, 128, 16), best, FAKE - 8, None, Op.is_lt), 8, ["ks" + hs, "Xs" + hs], ["Xt" + hs])
         V(tt(H("Xs", h, 128, 256, 16), H("rr", h), best, Op.subtract), 16, ["rr" + hs, "ks" + hs], ["Xd" + hs])
-        V(tt(H("Xs", h, 5, 128, 16), H("rr", h), best, Op.subtract), 16, ["rr" + hs, "ks" + hs], ["Xe" + hs])
-        V(scan(H("Xr", h), A0("RD"), H("Xs", h), Op.mult, Op.add), 128, ["RD", "Xt" + hs, "Xd" + hs, "Xe" + hs], ["Xr" + hs])
-        c = {}
-        P([mm(pb(c, 0, 128), H("Xr", h, 0, 128), A0("Ib")), mm(pb(c, 128, 256), H("Xr", h, 128, 256), A0("Ib"))], 256, ["Ib", "Xr" + hs], ["w" + hs], acq=c)
-        tag[0] = ("S", h, t)
-        V(tt(pb(c, 256, 384), pb(c, 128, 256), H("geb", h), Op.mult), 128, ["w" + hs, "geb" + hs], ["dge" + hs], use=c)
-        V(tt(T.SN[:, t, 128 * h:128 * h + 128], pb(c, 256, 384), T.sg[:, 128 * h:128 * h + 128], Op.add), 128, ["dge" + hs, "sg" + hs], ["sn%d%d" % (t, h)], use=c)
-        i = send(1, T.SL[:, t, 128 * h:128 * h + 128], T.SN[:, t, 128 * h:128 * h + 128], "rS%d%d" % (t, h), ["sn%d%d" % (t, h)], "S%d%d" % (t, h), 2.2)
-        if h == 1 and t < 2:
-            sendlog(t + 2, [i])
+        V(scan(H("Xr", h), A0("RD"), H("Xs", h), Op.mult, Op.add), SCN + 128, ["RD", "Xt" + hs, "Xd" + hs], ["Xr" + hs])
+        P([mm(pb(c, 0, 128), H("Xr", h, 0, 128), A0("Ib"), True, False), mm(pb(c, 0, 128), H("Xs", h, 123, 251), A0("Ib"), False, True),
+           mm(pb(c, 128, 256), H("Xr", h, 128, 256), A0("Ib"))], 384, ["Ib", "Xr" + hs, "Xd" + hs], ["w" + hs], acq=c)
         tag[0] = ("N", h, t)
         V(tt(H("prod", h), pb(c, 0, 128), H("Left", h), Op.mult), 128, ["w" + hs, "Left" + hs], ["prod" + hs], use=c)
+        tag[0] = ("S", h, t)
+        sn = T.SN[:, t, 128 * h:128 * h + 128]
+        V(tt(pb(c, 256, 384), pb(c, 128, 256), H("geb", h), Op.mult), 128, ["w" + hs, "geb" + hs], ["dge" + hs], use=c)
+        V(tt(sn, pb(c, 256, 384), T.sg[:, 128 * h:128 * h + 128], Op.add), 128, ["dge" + hs, "sg" + hs], ["sn%d%d" % (t, h)], use=c)
+        lastw["sent"] = send(1, T.SL[:, t, 128 * h:128 * h + 128], sn, "rS%d%d" % (t, h), ["sn%d%d" % (t, h)], "S%d%d" % (t, h), 64)
+        if h == 1 and t < 2:
+            tag[0] = ("X", 0, t)
+            sendlog(t + 2, "sent")
+        tag[0] = ("N", h, t)
         columns(h, [("Wv", H("prod", h), "prod" + hs, 512)], "v2", t)
 
     def counts(t):
         c = {}
-        P([mm(pb(c, 0, 1, 1, 8), H("Xs", 0, 0, 128, 16), T.c205[:, 0:1], True, False), mm(pb(c, 0, 1, 1, 8), H("Xs", 1, 0, 128, 16), T.c205[:, 0:1], False, True)],
-          32, ["Xt0", "Xt1", "c205"], ["Aps"], acq=c)
+        P([mm(pb(c, 0, 1, 1, 8), H("Xs", h, 0, 128, 16), T.c205[:, 0:1], h == 0, h == 1) for h in range(2)], 128, ["Xt0", "Xt1", "c205"], ["Aps"], acq=c)
         out = T.CG[0:8, t + 1, 256:257]
-        VA(cp(out, pb(c, 0, 1, 1, 8)), 1, act(out, pb(c, 0, 1, 1, 8)), 1, ["Aps", "pad"], ["B%d" % (t + 1)], use=c)
+        VA(cp(out, pb(c, 0, 1, 1, 8)), 1, act(out, pb(c, 0, 1, 1, 8)), 1, ["Aps", "pad"], ["B%d" % (t + 1)], use=c, name="B")
 
     def finish(t, h):
         hs = str(h)
@@ -472,10 +478,10 @@ def build(T, gs, to, prm):
             b, u = n // nu, n % nu
             fns = [mm(pb(c, bw * b, bw * b + bw), T.Wx[:, 11 - nw * u - w:139 - nw * u - w], H("Va", h, bw * (nw * n + w), bw * (nw * n + w + 1)),
                       u == 0 and w == 0, u == nu - 1 and w == nw - 1) for w in range(nw)]
-            extra = ["Va%s%d" % (hs, min(nb * nu - 1, prm.get("SUMAFT", 1)))] if n == 0 else []
-            prev = P(fns, nw * bw, ["Wx", "Va%s%d" % (hs, n)] + extra, ["ss%s%d" % (hs, n)], **({"acq": c} if n == 0 else {"use": c, "after": [prev]}))
+            extra = ["Va%s%d" % (hs, min(nb * nu - 1, prm["SUMAFT"]))] if n == 0 else []
+            prev = P(fns, nw * bw, ["Wx", "Va%s%d" % (hs, n)] + extra, ["sum%s%d" % (hs, n)], **({"acq": c} if n == 0 else {"use": c, "after": [prev]}))
         VA(ts(H("r1", h), pb(c, 0, 128), -820.0, 0.0, Op.add, Op.max), 128, act(H("r1", h), pb(c, 0, 128), AF.Relu, -820.0), 128,
-           ["ss%s%d" % (hs, n) for n in range(nb * nu)], ["r1" + hs], use=c, name="r1")
+           ["sum%s%d" % (hs, n) for n in range(nb * nu)], ["r1" + hs], use=c, name="r1")
         c = {}
         P([mm(pb(c, 0, 128), A0("Wp"), H("r1", h))], 128, ["Wp", "r1" + hs], ["pre" + hs], acq=c)
         VA(ts(H("ind", h), pb(c, 0, 128), 0.5, None, Op.is_lt), 128, act(H("ind", h), pb(c, 0, 128), AF.Relu, 1.0, -1.0), 128, ["pre" + hs], ["ind" + hs], use=c, name="ind")
@@ -495,7 +501,6 @@ def build(T, gs, to, prm):
         for h in range(2):
             tag[0] = ("H", h, t)
             match(t, h)
-            tag[0] = ("D", h, t)
             decide(t, h)
         if t < NV - 1:
             tag[0] = ("C", 0, t)
@@ -503,25 +508,23 @@ def build(T, gs, to, prm):
         for h in range(2):
             tag[0] = ("E", h, t)
             finish(t, h)
-    tag[0] = ("O", 0, 0)
 
-    def store(out, in_, rd):
-        add({"d": [lambda last: gs["d"].dma_start(out, in_)]}, {"d": 0.05}, rd, [], pin=("dma", "sto", 2.0))
+    tag[0] = ("L", 0, NV)
     rotation(NV, "LF")
-    gather(A0("ysb"), T.SL[:, NV - 1, :], T.lu[:, :], 256, ["lu", "S%d0" % (NV - 1), "S%d1" % (NV - 1)], ["ysb"], "gY", bias=ZC)
-    store(T.ys[:, :], T.ysb[:, :], ["ysb"])
+    gather(A0("ysb"), T.SL[:, NV - 1, :], A0("lu"), 256, ["lu", "S%d0" % (NV - 1), "S%d1" % (NV - 1)], ["ysb"], "gY", bias=ZC)
+    dmas([(T.ys[:, :], T.ysb[:, :])], ["ysb"], [], "sto", 128)
+    fin = []
     for h in range(2):
+        tag[0] = ("L", h, NV)
         c, zo = {}, T.zb[:, 128 * h:128 * h + 128]
         position(NV, h, c, [])
         VA(ts(zo, pb(c, 0, 128), ZC, None, Op.add), 128, act(zo, pb(c, 0, 128), AF.Identity, ZC), 128, ["zn%d" % h], ["zb%d" % h], use=c)
-        store(T.yz[:, 128 * h:128 * h + 128], T.zb[0:128:16, 128 * h:128 * h + 128], ["zb%d" % h])
-    fin = []
-    for h in range(2):
+        dmas([(T.yz[:, 128 * h:128 * h + 128], T.zb[0:128:16, 128 * h:128 * h + 128])], ["zb%d" % h], [], "sto", 4)
         for a in range(4):
             dst = T.ytb[:, 256 * a + 128 * h:256 * a + 128 * h + 128]
             fin.append("yt%d%d" % (h, a))
-            VA(cp(dst, H("tb", h, a, None, 4)), 64, act(dst, H("tb", h, a, None, 4)), 128, ["tb%d" % h], [fin[-1]])
-    store(T.yt[:, :], T.ytb[:, :], fin)
+            V(cp(dst, H("tb", h, a, None, 4)), 64, ["tb%d" % h], [fin[-1]])
+    dmas([(T.yt[:, :], T.ytb[:, :])], fin, [], "sto", 256)
     return ops
 
 
@@ -529,73 +532,83 @@ def schedule(ops, prm):
     n = len(ops)
     succ = [[] for _ in range(n)]
     for i, o in enumerate(ops):
-        o["lat"] = o["sym"][2] if o["sym"] and o["sym"][0] == "dma" else 0.0
         for d in o["deps"]:
             succ[d].append(i)
-    pr = [0.0] * n
+    way_ = [0.0] * n
     for i in range(n - 1, -1, -1):
-        pr[i] = min(ops[i]["cost"].values()) + ops[i]["lat"] + max([pr[k] + (OWN if ops[k]["cost"].keys() & ops[i]["cost"].keys() else HOP) for k in succ[i]], default=0.0)
-    pr = [pr[i] + ops[i]["bonus"] for i in range(n)]
+        way_[i] = min(ops[i]["cost"].values()) + ops[i]["lat"] + max([way_[k] for k in succ[i]], default=0.0) + HOP
+    rank, bonus, win, lam = prm["RANK"], prm["BONUS"], prm["WIN"], prm["LAM"]
+    pr, cost = [], []
+    for i, o in enumerate(ops):
+        tag, key = o["tag"], (o["name"], o["tag"][1])
+        pr.append((0.01 * way_[i] - 100.0 * tag[2] - rank[tag[:2]] if tag[:2] in rank else way_[i]) + o["bonus"] + bonus.get(key, 0.0))
+        e = prm["ENG"].get(key, o["dflt"])
+        cost.append(list(o["cost"].items()) if len(o["cost"]) == 1 else [x for x in o["cost"].items() if x[0] in e])
+    first = [o["use"]["first"] if o["use"] is not None else -1 for o in ops]
     left = [len(o["deps"]) for o in ops]
-    pend = {}
-    for o in ops:
-        if o["use"] is not None:
-            pend[o["use"]["first"]] = pend.get(o["use"]["first"], 0) + 1
+    pend = [0] * n
+    for f in first:
+        pend[f] += f >= 0
     ready = [i for i in range(n) if left[i] == 0]
-    free = {e: 0.0 for e in "vapqd"}
-    end, order, dep_end = [0.0] * n, [], [{} for _ in range(n)]
+    free, busy = {e: 0.0 for e in "vapqdn"}, 0.0
+    end, order, eng, more, banks = [0.0] * n, [], [None] * n, {}, {}
+    dep_end = [dict.fromkeys([x[0] for x in c], 0.0) for c in cost]
     holder = {b: None for b in POOL}
     users = {b: [] for b in POOL}
+    last = {b: {} for b in POOL}
     while len(order) < n:
         cand = {}
+        open_ = min([(max(last[b].values(), default=-HOP) + HOP, b) for b in POOL if holder[b] is None or pend[holder[b]] == 0], default=None)
         for i in ready:
-            o = ops[i]
-            est, bank = 0.0, None
-            if o["acq"] is not None:
-                open_ = [(max([end[m] + HOP for m in users[b]], default=0.0), b) for b in POOL if holder[b] is None or pend[holder[b]] == 0]
-                if not open_:
-                    continue
-                t0, bank = min(open_)
-                est = max(est, t0)
-            for e in o["cost"]:
-                t1 = max(est, free.get(e, 0.0), dep_end[i].get(e, 0.0))
-                if o["acq"] is None and o["use"] is not None:
-                    t1 = max([t1] + [end[m] + HOP for m in users[o["use"]["bank"]] if ops[m]["eng"] != e])
-                cand.setdefault(e, []).append((t1, i, bank))
+            f = first[i]
+            if f == i and open_ is None:
+                continue
+            for e, t1 in dep_end[i].items():
+                if t1 < free[e]:
+                    t1 = free[e]
+                if f == i:
+                    t1 = max(t1, open_[0])
+                elif f >= 0:
+                    for x, t2 in last[banks[f]].items():
+                        if x != e and t2 + HOP > t1:
+                            t1 = t2 + HOP
+                cand.setdefault(e, []).append((t1, i))
         best = None
         for e, cs in cand.items():
-            lo = min(c[0] for c in cs) + prm["WIN"]
-            c = max((c for c in cs if c[0] <= lo), key=lambda c: pr[c[1]])
+            lo = min(cs)[0] + win
+            c = max((c for c in cs if c[0] <= lo), key=lambda c: pr[c[1]] - lam * c[0])
             if best is None or (c[0], -pr[c[1]]) < (best[0][0], -pr[best[0][1]]):
                 best = (c, e)
-        (est, i, bank), e = best
-        o = ops[i]
+        (est, i), e = best
+        o, f = ops[i], first[i]
         ready.remove(i)
-        o["eng"] = e
-        if o["acq"] is not None:
-            for m in users[bank]:
-                o["deps"].setdefault(m, False)
-            holder[bank], users[bank] = i, []
-            o["acq"]["bank"] = bank
-        if o["use"] is not None:
-            b = o["use"]["bank"]
-            for m in users[b]:
-                if ops[m]["eng"] != e:
-                    o["deps"].setdefault(m, False)
-            users[b].append(i)
-            pend[o["use"]["first"]] -= 1
+        eng[i] = e
         end[i] = est + o["cost"][e]
-        if e in free:
+        if f == i:
+            more[i] = users[open_[1]]
+            holder[open_[1]], users[open_[1]], last[open_[1]], banks[i] = i, [], {}, open_[1]
+        if f >= 0:
+            b = banks[f]
+            more[i] = more.get(i, []) + [m for m in users[b] if eng[m] != e]
+            users[b].append(i)
+            last[b][e] = end[i]
+            pend[f] -= 1
+        if e != "n":
             free[e] = end[i]
-        end[i] += o["lat"]
+        if o["lat"]:
+            busy = max(busy, end[i]) + o["sym"][2]
+            end[i] = busy + o["sym"][3]
         order.append(i)
         for k in succ[i]:
             left[k] -= 1
-            for f in ops[k]["cost"]:
-                dep_end[k][f] = max(dep_end[k].get(f, 0.0), end[i] + (OWN if f == e or f == "n" else HOP))
+            de = dep_end[k]
+            for x in de:
+                t1 = end[i] + (OWN if x == e or x == "n" else HOP)
+                if t1 > de[x]:
+                    de[x] = t1
             if left[k] == 0:
                 ready.append(k)
-    return order, end
+    return order, end, eng, more, banks
 
 
 def emit(ops, order, T, gs):
@@ -610,7 +623,7 @@ def emit(ops, order, T, gs):
 
     def after(e, i, raw):
         sem, val, clk = done[i]
-        if ops[i]["eng"] == e and (e == "p" or sem == "loc") and not raw:
+        if ops[i]["eng"] == e and not raw and (e == "p" or sem == "loc" or raw is None):
             return
         if know[e].get(sem, 0) >= val:
             return
@@ -627,12 +640,11 @@ def emit(ops, order, T, gs):
             continue
         for d, raw in sorted(o["deps"].items(), key=lambda d: -done[d[0]][1]):
             after(e, d, raw)
-        sem = {"": e, "dma": o["sym"] and o["sym"][-2:-1] and o["sym"][1:2] and o["sym"][1:2][0], "send": "loc"}[kind]
+        sem = e if kind == "" else o["sym"][4] if kind == "send" else o["sym"][1]
         for x, fn in enumerate(o["fns"][e]):
-            end = x == len(o["fns"][e]) - 1
-            c = fn(end and i in lastacc)
+            c = fn(x == len(o["fns"][e]) - 1 and i in lastacc)
             if kind == "send":
-                count[sem] = count.get(sem, 0) + gs["neng"]
+                count[sem] = count.get(sem, 0) + o["sym"][1]
             else:
                 c.then_inc(T.sem[sem], 16 if kind == "dma" else 1)
                 count[sem] = count.get(sem, 0) + (16 if kind == "dma" else 1)
@@ -642,17 +654,24 @@ def emit(ops, order, T, gs):
         gs["q"].wait_ge(T.sem[sem], count[sem])
 
 
+def way(topo, src, dst):
+    rid, pid, _ = topo.addr(dst)
+    return rid, pid, topo.mask(src, dst), len(topo.engines(src, dst))
+
+
 def rank_program(g, core, T, topo):
     rank = T.rank_of(core)
     if rank is None:
         return
     n = len(T.cores)
-    to = {}
-    for d in range(1, n):
-        dst = T.cores[(rank - d) % n]
-        rid, pid, _ = topo.addr(dst)
-        to[d] = (rid, pid, topo.mask(core, dst))
-    gs = {"v": g.vector, "a": g.scalar, "p": g.tensor, "q": g, "d": g.sync, "neng": len(topo.engines(core, T.cores[(rank - 1) % n]))}
+    to = {d: way(topo, core, T.cores[(rank - d) % n]) for d in range(1, n)}
+    gs = {"v": g.vector, "a": g.scalar, "p": g.tensor, "q": g, "d": g.sync}
     ops = build(T, gs, to, PRM)
-    order, _ = schedule(ops, PRM)
+    order, _, eng, more, banks = schedule(ops, PRM)
+    for i, o in enumerate(ops):
+        o["eng"] = eng[i]
+        for m in more.get(i, []):
+            o["deps"].setdefault(m, False)
+        if i in banks:
+            o["acq"]["bank"] = banks[i]
     emit(ops, order, T, gs)

from concourse.mybir import AluOpType as Op, ActivationFunctionType as AF

NV = 8
J = 13
XP = 2
PRM = dict(
    JA=(10, 9),
    NS=(4, 2),
    SB=(2, 2),
    NM=6,
    OA=(0, 0),
    SUMAFT=1,
    FAST=(1, 1),
    WIN=0.0,
    LAM=10,
    RANK={('L', 0): -49, ('F', 0): -75, ('L', 1): -171, ('F', 1): -64, ('G', 1): 121, ('G', 0): 73, ('H', 0): 88, ('D', 0): -119, ('S', 0): 80, ('N', 0): 59, ('M', 0): 175, ('E', 0): 58, ('T', 0): -55, ('D', 1): -101, ('H', 1): 238, ('S', 1): 110, ('C', 0): 17, ('N', 1): 1, ('E', 1): 298, ('T', 1): 88, ('X', 0): 6},
    ENG={('y21', 0): 'va', ('y22', 0): 'va', ('v20', 0): 'va', ('v20', 1): 'va', ('v21', 1): 'va', ('v22', 1): 'va', ('v23', 0): 'v', ('v23', 1): 'va', ('gT', 1): 'a', ('gC', 0): 'a', ('gT', 0): 'a', ('gY', 0): 'a', ('r1', 0): 'v', ('Dc', 1): 'v', ('Lzb', 1): 'v', ('r1', 1): 'v', ('gS', 1): 'v', ('Dc', 0): 'a', ('ind', 1): 'a'},
    BONUS={('Ssn', 1): 48, ('Lli', 0): 112, ('ysum', 1): 36, ('CAps', 0): -64, ('GOH', 1): 60, ('HK', 1): -72, ('v20', 1): 124, ('GoC', 0): 100, ('v21', 1): 40, ('GoS', 1): 4, ('v22', 1): 12, ('Fcnt', 0): -8, ('y21', 0): 20, ('Gcmp', 1): -48, ('gY', 0): -64, ('Fcmp', 1): -60, ('max', 0): -40, ('vsum', 0): 52, ('v22', 0): 12, ('DXr', 0): -28, ('Hyps', 0): 16, ('Ttof', 1): -40, ('Lzb', 1): 148, ('y22', 0): 24, ('FoS', 0): -28, ('NF', 1): 76, ('S', 1): -68, ('asum', 0): -32, ('asum', 1): -56, ('LdB', 0): -32, ('gS', 1): 40, ('TQ', 1): -68, ('Lcg', 0): 12, ('Est', 1): 76, ('EVa', 0): 40, ('Esum', 0): -32, ('FF', 1): 48, ('Dw', 1): 12, ('gT', 0): 20, ('ind', 0): 20, ('Ttof', 0): 128, ('Gcmp', 0): 24, ('y23', 1): 96, ('Fze', 1): -40, ('Llm', 0): 20, ('Nfi', 1): -20, ('GoC', 1): -8, ('DXt', 1): -64, ('Epre', 0): 40, ('Fze', 0): 20, ('GCr', 0): -20, ('EVa', 1): -20, ('FX', 0): -28, ('FX', 1): -80, ('Lsg', 1): -16, ('Lzn', 0): 20, ('Dks', 0): -28, ('DXd', 1): -20, ('Gcnt', 1): -60, ('Gz', 0): 8, ('Lzn', 1): -4, ('L', 1): -8, ('y22', 1): -28, ('GOH', 0): 68, ('v23', 0): 8, ('DXd', 0): 8, ('Nof', 0): 20, ('S', 0): -20, ('DXr', 1): -68, ('Gz', 1): -80, ('GoS', 0): -20, ('Fzn', 1): -4, ('Ffm', 1): 8, ('Ffi', 0): -40, ('Drr', 1): -16, ('ysum', 0): -8, ('DXt', 0): 20, ('X', 0): -8, ('GU', 1): 12, ('FOH', 0): -8, ('Nprod', 0): -40, ('TQ', 0): -40, ('ind', 1): -32, ('Fof', 0): 40, ('FHb', 1): -40, ('Dc', 0): 20, ('Lcg', 1): 68, ('FOH', 1): 60, ('Fgeb', 0): -40, ('Lsg', 0): -20, ('r1', 1): -20, ('Sdge', 0): -40, ('FF', 0): -20, ('Lzb', 0): -56, ('Fcnt', 1): 20, ('Lyt', 0): -28, ('Fof', 1): -20, ('Dks', 1): 8},
)
CYC, PEC, HOP, OWN = 0.00083, 0.00042, 0.24, 0.01
SCN = 300
LOC, FAR = 0.006, 0.013
GAT = 1.56
MAGIC = 201326592.0
FAKE = 32.0 * 2344 + 16
ZC = 1600.0

F32, BF, F16, I32, U16 = "float32", "bfloat16", "float16", "int32", "uint16"
SCRATCH = {
    "t0s": ("sbuf", [128, 1024], BF), "ytb": ("sbuf", [128, 1024], BF),
    "s0s": ("sbuf", [128, 256], I32), "cfs": ("sbuf", [128, 256], I32), "z0s": ("sbuf", [8, 256], I32), "z0f": ("sbuf", [8, 256], F32),
    "sg": ("sbuf", [128, 256], F32),
    "CG": ("sbuf", [128, NV, 272], F32), "CL": ("sbuf", [128, NV, 272], F32),
    "SN": ("sbuf", [128, NV, 256], F32), "SL": ("sbuf", [128, NV, 256], F32),
    "ysb": ("sbuf", [128, 256], F32), "zb": ("sbuf", [128, 256], F32),
    "li": ("sbuf", [128, 16], I32), "lm": ("sbuf", [128, 16], I32), "lu": ("sbuf", [128, 16], U16),
    "iP": ("sbuf", [128, 1], I32), "iQ": ("sbuf", [128, 128], F32), "iL": ("sbuf", [128, 16], F32), "i64": ("sbuf", [128, 32], F32),
    "pi": ("sbuf", [128, 8], I32), "pf": ("sbuf", [128, 5], F32), "qg": ("sbuf", [128, 128], F32), "qm": ("sbuf", [128, 128], F32),
    "l5": ("sbuf", [128, 16], I32), "LB": ("sbuf", [128, 16], F32), "LF": ("sbuf", [128, 16], F32),
    "E": ("sbuf", [128, 16], F32), "vec": ("sbuf", [128, 32], F32), "gf": ("sbuf", [128, 8], F32),
    "B32": ("sbuf", [128, 128], F32), "Bb": ("sbuf", [128, 128], BF), "Ib": ("sbuf", [128, 128], BF), "Im": ("sbuf", [128, 128], BF),
    "Ih": ("sbuf", [128, 128], F16), "R8": ("sbuf", [8, 128], F32), "R8n": ("sbuf", [8, 128], F32),
    "Wy": ("sbuf", [128, 128], F32), "tm1": ("sbuf", [128, 128], F32),
    "Wx": ("sbuf", [128, 144], BF), "Wn": ("sbuf", [128, 144], F32), "Wc": ("sbuf", [128, 144], F16), "Wq": ("sbuf", [128, 144], BF),
    "Wu": ("sbuf", [128, 128], F16), "Wz1": ("sbuf", [128, 128], F16), "Wz": ("sbuf", [128, 128], F32), "Wp": ("sbuf", [128, 128], BF),
    "Wv": ("sbuf", [128, 128], F32), "tm2": ("sbuf", [128, 128], F32), "tm4": ("sbuf", [128, 128], F32),
    "Wd": ("sbuf", [128, 128], F16), "Wf": ("sbuf", [128, 128], F16), "Wk": ("sbuf", [128, 128], F16), "Wm": ("sbuf", [128, 128], F16),
    "Bn": ("sbuf", [128, 128], F32), "one": ("sbuf", [128, 128], F16),
    "G64": ("sbuf", [128, 8], BF), "Z": ("sbuf", [128, 8, 32], BF), "gr": ("sbuf", [128, 8, 13], F32),
    "RT0": ("sbuf", [128, 8, 13], BF), "RT1": ("sbuf", [128, 8, 13], BF), "cj": ("sbuf", [128, 104], BF),
    "KD": ("sbuf", [128, 104], F32), "RD": ("sbuf", [128, 256], BF), "w7": ("sbuf", [128, 128], BF), "c205": ("sbuf", [128, 8], BF),
    "Qc": ("sbuf", [128, 32], F16),
    "kb": ("psum", [128, 512], F32), "yps": ("psum", [128, 128, 16], F32),
}
POOL = ("pb0", "pb1", "pb2")
for _b in POOL:
    SCRATCH[_b] = ("psum", [128, 512], F32)
for _d in range(4):
    SCRATCH["x%d" % _d] = ("sbuf", [128, 4096], BF)
_HALF = {"cmp": (256, BF), "geb": (128, BF), "ze": (128, F16), "oS": (256, F32), "oC": (256, F16), "Dc": (128, F32), "Hb": (128, F32), "Left": (128, F32),
         "prod": (128, F32), "fi": (128, I32), "fm": (128, I32), "of": (128, U16), "y2": (2048, BF), "v2": (2048, BF), "Va": (1536, BF),
         "ks": (104, F32), "rr": (8, F32), "Xs": (256, BF), "Xr": (256, BF), "r1": (128, BF), "ind": (128, BF), "tof": (32, U16),
         "tb": (512, BF), "Ma": (512 * 4, BF)}
for _n, (_c, _d) in _HALF.items():
    SCRATCH[_n] = ("sbuf", [128, 2 * _c], _d)
for _m in range(6):
    SCRATCH["mb%d" % _m] = ("sbuf", [128, 512], BF)
SEMAPHORES = ["v", "a", "p", "q", "loc", "sto", "ls", "lc", "lz", "lt"] + [_n + str(_k) for _n in ("lx", "rX1", "rX2", "rX3") for _k in range(XP)]
SEMAPHORES += ["rS%d%d" % (_t, _h) for _t in range(NV) for _h in range(2)] + ["rC%d" % _t for _t in range(NV)]


def build(T, gs, to, prm):
    ops, lastw, readers, accs, tag = [], {}, {}, {}, [("I", 0, 0)]
    JA, NS, NM = prm["JA"], prm["NS"], prm["NM"]

    def add(fns, cost, rd=(), wr=(), acc=None, acq=None, use=None, after=(), pin=None, name="", dflt="va"):
        i = len(ops)
        deps = {}
        for k in rd:
            for o in ([lastw[k]] if k in lastw else []) + accs.get(k, []):
                deps[o] = True
            readers.setdefault(k, []).append(i)
        if acc is not None:
            deps[lastw[acc]] = deps.get(lastw[acc], False)
            accs.setdefault(acc, []).append(i)
        for k in wr:
            for o in readers.get(k, []) + ([lastw[k]] if k in lastw else []) + accs.get(k, []):
                if o != i:
                    deps[o] = deps.get(o, False)
            lastw[k], readers[k], accs[k] = i, [], []
        for o in after:
            deps.setdefault(o, None)
        if acq is not None:
            acq["first"] = i
            use = acq
        name = name or (tag[0][0] + (list(wr) + [""])[0]).rstrip("0123456789_")
        ops.append(dict(fns=fns, cost=cost, deps=deps, acq=acq, use=use, sym=pin, acc=acc, tag=tag[0], bonus=0.0, name=name, dflt=dflt,
                        lat=pin[2] + pin[3] if pin and pin[0] != "land" else 0.0))
        return i

    v, s, p, g = gs["v"], gs["a"], gs["p"], gs["q"]

    def VA(fv, cv, fa, ca, rd=(), wr=(), **kw):
        fns, cost = {}, {}
        if fv is not None:
            fns["v"], cost["v"] = [fv], 0.01 + max(64, cv) * CYC
        if fa is not None:
            fns["a"], cost["a"] = [fa], 0.09 + ca * CYC
        return add(fns, cost, rd, wr, **kw)

    def V(fn, c, rd=(), wr=(), **kw):
        return VA(fn, c, None, 0, rd, wr, **kw)

    def A(fn, c, rd=(), wr=(), **kw):
        return VA(None, 0, fn, c, rd, wr, **kw)

    def P(fns, c, rd=(), wr=(), **kw):
        return add({"p": fns}, {"p": c * PEC}, rd, wr, **kw)

    def ap(x):
        return T[x[0]["bank"]][x[1]] if isinstance(x, tuple) else x

    def pb(cell, a, b, step=1, rows=128):
        return (cell, (slice(0, rows), slice(a, b, step)))

    def mm(out, l, r, start=True, stop=True):
        return lambda last: p.matmul(ap(out), l, r, start, stop or last)

    def ts(out, a, s1, s2, o0, o1=None):
        if o1 is None:
            return lambda last: v.tensor_scalar(ap(out), ap(a), ap(s1), None, o0)
        return lambda last: v.tensor_scalar(ap(out), ap(a), ap(s1), ap(s2), o0, o1)

    def tt(out, a, b, o):
        return lambda last: v.tensor_tensor(ap(out), ap(a), ap(b), o)

    def cp(out, a):
        return lambda last: v.tensor_copy(ap(out), ap(a))

    def act(out, a, f=AF.Copy, bias=0.0, scale=1.0):
        return lambda last: s.activation(ap(out), ap(a), f, bias=bias, scale=scale)

    def scan(out, a, b, o0, o1):
        return lambda last: v.tensor_tensor_scan(out, a, b, 0.0, o0, o1)

    def ms(out, val):
        return lambda last: v.memset(out, val)

    def dmas(pairs, rd, wr, sem, kb, behind=None):
        return add({"d": [lambda last, x=x: gs["d"].dma_start(x[0], x[1]) for x in pairs]}, {"d": 0.05 * len(pairs)}, rd, wr,
                   pin=("dma", sem, 0.2 * len(pairs) + kb * LOC, 3.2), after=[lastw[behind]] if behind in lastw else [])

    def load(pairs, sem, key, kb):
        i = dmas(pairs, [], [key], sem, kb)
        ops[i]["bonus"] = 1000.0 - 10.0 * i

    def send(d, out, in_, sem, rd, key, kb, behind=None, loc="loc"):
        rid, pid, mask, n = to[d]
        i = add({"q": [lambda last: g.remote_dma(out, in_, T.sem[sem], T.sem[loc], pid, rid, mask)]}, {"q": 0.6}, rd, [], pin=("send", n, 0.8 + kb * FAR, 0.0, loc),
                after=[lastw[behind]] if behind in lastw else [])
        if key:
            add({"n": []}, {"n": 1.4}, [], [key], after=[i], pin=("land", sem, n))
        return i

    def H(name, h, a=0, b=None, step=None):
        n = _HALF[name][0]
        return T[name][:, n * h + a: n * h + (n if b is None else b): (step or 1)]

    def gather(out, win, off, n, rd, wr, name, dflt="va", bias=None):
        if bias is None:
            VA(cp(out, win.indirect(off)), 48 + n * GAT, act(out, win.indirect(off)), n * GAT - 30, rd, wr, name=name, dflt=dflt)
        else:
            VA(ts(out, win.indirect(off), bias, None, Op.add), 48 + n * GAT, act(out, win.indirect(off), AF.Identity, bias), n * GAT - 30, rd, wr, name=name, dflt=dflt)

    xw = 4096 // XP
    load([(T.z0s[:, :], T.z0[:, :])], "lz", "z0s", 8)
    load([(T.s0s[:, :], T.s0[:, :])], "ls", "s0s", 128)
    load([(T.cfs[:, :], T.cf[:, :])], "lc", "cfs", 128)
    for k in range(XP):
        load([(T.x0[:, xw * k:xw * k + xw], T.xl[:, xw * k:xw * k + xw])], "lx%d" % k, "x0_%d" % k, 1024 // XP)
    load([(T.t0s[:, :], T.t0[:, :])], "lt", "t0s", 256)
    XK = {d: ["x%d_%d" % (d, k) for k in range(XP)] for d in range(4)}

    def sendlog(d, behind):
        for k in range(XP):
            send(d, T["x%d" % d][:, xw * k:xw * k + xw], T.x0[:, xw * k:xw * k + xw], "rX%d%d" % (d, k), ["x0_%d" % k], "x%d_%d" % (d, k), 1024 // XP, behind)
    sendlog(1, None)

    def iota(out, key, pat, base, cm, n):
        if key == "iP":
            add({"q": [lambda last: g.iota(out, pat, base, cm)]}, {"q": 0.13 + 2 * n * CYC}, (), [key])
        else:
            add({"q": [lambda last: g.iota(out, pat, base, cm, allow_small_or_imprecise_dtypes=True)]}, {"q": 0.13 + 2 * n * CYC}, (), [key])
    A0 = lambda n, a=0, b=None: T[n][:, a:b] if b is not None else T[n][:, :]
    iota(A0("iP"), "iP", [[0, 1]], 0, 1, 1)
    iota(A0("iL"), "iL", [[16, 16]], 0, 0, 16)
    iota(A0("qg"), "qg", [[1, 8], [0, 16]], 0, 0, 128)
    iota(A0("qm"), "qm", [[0, 8], [1, 16]], 0, 0, 128)
    iota(A0("iQ"), "iQ", [[1, 128]], 0, -1, 128)
    iota(T.CG[:, :, 256:272], "pad", [[0, 128]], 0, 0, 128)
    iota(T.cj[:, :], "cj", [[0, 8], [1, 13]], -6, 0, 104)
    iota(T.gr[:, :, :], "iC", [[1, 8], [0, 13]], 0, 0, 104)
    iota(A0("i64"), "i64", [[64, 32]], -4, 0, 32)

    def C(fn, c, rd, wr):
        return V(fn, c, rd, [wr])

    def scaled(out, a, col, rd, wr, n, bias=0.0):
        VA(ts(out, a, col, bias, Op.mult, Op.add), n, act(out, a, AF.Identity, bias, col), n, rd, [wr])
    for x, (sh_, and_) in enumerate(((0, 15), (4, 7), (0, 3), (2, 3), (0, 127))):
        C(ts(T.pi[:, x:x + 1], A0("iP"), sh_, and_, Op.arith_shift_right, Op.bitwise_and), 1, ["iP"], "pi%d" % x)
    C(cp(A0("pf"), T.pi[:, 0:5]), 5, ["pi%d" % x for x in range(5)], "pf")
    pm, pg, pa, pp = (T.pf[:, x:x + 1] for x in (0, 1, 3, 4))
    scaled(A0("LB"), A0("iL"), 1.0, ["iL", "pf"], "LB", 16, pm)
    C(ts(A0("l5"), A0("LB"), 5.0, None, Op.mult), 16, ["LB"], "l5")
    scaled(A0("LF"), A0("LB"), 205.0, ["LB"], "LF", 16)
    C(ts(A0("B32"), A0("qg"), pg, None, Op.is_equal), 128, ["pf", "qg"], "B32")
    C(ts(T.R8[:, :], T.qg[0:8, :], T.pf[0:8, 4:5], None, Op.is_equal), 128, ["pf", "qg"], "R8")
    scaled(T.R8n[:, :], T.R8[:, :], -1.0, ["R8"], "R8n", 128)
    scaled(A0("Bb"), A0("B32"), 1.0, ["B32"], "Bb", 128)
    C(ts(A0("Ib"), A0("iQ"), 0.0, None, Op.is_equal), 128, ["iQ"], "Ib")
    scaled(A0("Im"), A0("Ib"), -1.0, ["Ib"], "Im", 128)
    scaled(A0("Ih"), A0("Ib"), 1.0, ["Ib"], "Ih", 128)
    C(ts(A0("gf"), T.qm[:, 0:8], pg, None, Op.is_equal), 8, ["pf", "qm"], "gf")
    C(ts(A0("E"), T.qm[:, 0:16], pm, None, Op.is_equal), 16, ["pf", "qm"], "E")
    nvec = [0]

    def column(terms):
        n = nvec[0]
        nvec[0] += 1
        out, key = T.vec[:, n:n + 1], "vec%d" % n
        for y, (x, c) in enumerate(terms.items()):
            scaled(out, T.E[:, x:x + 1], float(c), ["E", key], key, 1, out if y else 0.0)
        return out, key
    rp1, rp1k = T.vec[:, 30:31], "vec30"
    scaled(rp1, pm, 1.0, ["pf"], rp1k, 1, 1.0)
    rn1, oh1, oh2 = ((T.vec[:, x:x + 1], "vec%d" % x) for x in (28, 27, 26))
    scaled(rn1[0], rp1, -1.0, [rp1k], rn1[1], 1)
    scaled(oh1[0], T.E[:, 0:1], 0.5, ["E", rn1[1]], oh1[1], 1, rn1[0])
    scaled(oh2[0], T.E[:, 0:1], 0.5, ["E"], oh2[1], 1, 1.0)
    zsc, zsck = column({0: 1, 1: -1, 2: -1})
    zbi, zbik = column({2: ZC - 16, 3: 1})
    dbs = column({1: -0.5, 2: 1, 4: -0.5, 6: 1, 7: 1, 9: 1})
    dbf = (T.vec[:, 31:32], "vec31")
    scaled(dbf[0], T.E[:, 0:1], 1.0, [dbs[1], "E"], dbf[1], 1, dbs[0])
    for n_ in ("Wx", "Wc", "Wq", "Wu"):
        C(ms(A0(n_), 0.0), 72, [], n_)
    scaled(T.Wx[:, 15:128:16], A0("gf"), 1.0, ["gf", "Wx"], "Wx", 8)
    scaled(A0("Wn"), A0("Wx"), -1.0, ["Wx"], "Wn", 144)
    for q_, c_ in ((3, 1.0), (4, 0.5), (8, 1.0)):
        scaled(T.Wc[:, q_:128:16], A0("gf"), c_, ["gf", "Wc"], "Wc", 8)
    scaled(A0("Wd"), T.Wc[:, 3:131], 1.0, ["Wc"], "Wd", 128)
    C(ms(T.Wd[:, 0:128:16], 0.0), 8, ["Wd"], "Wd")
    scaled(A0("Bn"), A0("B32"), -1.0, ["B32"], "Bn", 128)
    scaled(A0("Wk"), A0("B32"), -18.5 / 16, ["B32"], "Wk", 128)
    C(ms(A0("one"), 1.0), 64, [], "one")
    scaled(A0("tm4"), A0("qm"), 1.0, ["qm"], "tm4", 128, 9.5)
    C(tt(A0("Wm"), A0("tm4"), A0("B32"), Op.mult), 256, ["tm4", "B32"], "Wm")
    for q_ in range(12, 16):
        scaled(T.Wq[:, q_:128:16], A0("gf"), 1.0, ["gf", "Wq"], "Wq", 8)
    vA, vB, vD, vE = column({0: 1, 1: -1}), column({0: 1, 1: -1, 2: 1, 3: -ZC}), column({2: -1, 3: ZC}), (T.E[:, 3:4], "E")
    for q_, (c_, k_) in ((0, vA), (1, vE), (2, vD), (3, vB), (4, vE), (5, vE), (6, vE), (7, vB), (9, vE)):
        scaled(T.Wu[:, q_:128:16], A0("gf"), c_, ["gf", "Wu", k_], "Wu", 8)
    scaled(A0("Wf"), A0("Wu"), 1.0, ["Wu"], "Wf", 128)
    C(ms(T.Wf[:, 0:128:16], 0.0), 8, ["Wf"], "Wf")
    scaled(A0("Wz1"), A0("B32"), vB[0], ["B32", vB[1]], "Wz1", 128)
    vZ = column({2: 1, 7: 1, 9: -1})
    scaled(A0("Wz"), A0("B32"), vZ[0], ["B32", vZ[1]], "Wz", 128)
    (a_, ak), (b_, bk) = column({1: 2, 6: 1}), column({0: 1, 1: 19, 6: -9})
    scaled(A0("tm1"), A0("qm"), a_, ["qm", ak, bk], "tm1", 128, b_)
    C(tt(A0("Wy"), A0("tm1"), A0("B32"), Op.mult), 256, ["tm1", "B32"], "Wy")
    (a_, ak), (b_, bk) = column({1: 2, 4: 2, 9: 1}), column({0: 1, 3: 1, 1: 37, 4: 37, 5: -1})
    scaled(A0("tm2"), A0("qm"), a_, ["qm", ak, bk], "tm2", 128, b_)
    C(tt(A0("Wv"), A0("tm2"), A0("B32"), Op.mult), 256, ["tm2", "B32"], "Wv")
    add({"q": [lambda last: g.affine_select(A0("Wp"), A0("Bb"), [[1, 128]], Op.is_ge, 0.0, 0, -1)]}, {"q": 0.4}, ["Bb"], ["Wp"])
    scaled(A0("G64"), A0("gf"), 64.0, ["gf"], "G64", 8)
    C(ms(T.Z[:, :, :], 0.0), 128, [], "Z")
    for k in range(4):
        scaled(T.Z[:, :, 16 + k], A0("gf"), -32.0, ["gf", "Z"], "Z", 8)
    C(ms(A0("KD"), -FAKE), 104, [], "KD")
    C(ms(T.KD[:, 0:104:13], FAKE), 8, ["KD"], "KD")
    C(ts(T.gr[:, :, :], T.gr[:, :, :], pg, None, Op.is_equal), 104, ["pf", "iC"], "gr")
    RT = ["RT0", "RT%d" % (JA[0] != JA[1])]
    for h in range(2 if JA[0] != JA[1] else 1):
        for a_, b_, c_ in ((0, JA[h], -32.0), (JA[h], J, 32.0)):
            scaled(T[RT[h]][:, :, a_:b_], T.gr[:, :, a_:b_], c_, ["gr", RT[h]], RT[h], 8 * (b_ - a_))
    C(ms(A0("RD"), 1.0), 128, [], "RD")
    for a_, b_, c_ in ((0, 256, 0.0), (3, 128, -1.0), (5, 128, 0.0), (7, 128, 0.0)):
        C(ms(T.RD[:, a_:b_:16], c_), 16, ["RD"], "RD")
    scaled(T.vec[:, 29:30], pa, 12.0, ["pf"], "vec29", 1, pm)
    scaled(A0("Qc"), A0("i64"), 1.0, ["i64", "vec29"], "Qc", 32, T.vec[:, 29:30])
    C(ms(A0("w7"), 2.0 ** -7), 64, [], "w7")
    C(ms(A0("c205"), 205.0), 8, [], "c205")
    C(ms(A0("Xs"), 0.0), 256, [], "Xs")
    for h in range(2):
        C(ms(H("Xs", h, 3, 128, 4), 1.0), 32, ["Xs"], "Xs%d" % h)
        C(ms(H("Xs", h, 11, 128, 16), 0.0), 8, ["Xs%d" % h], "Xs%d" % h)
        C(ms(H("Xs", h, 15, 128, 16), 0.0), 8, ["Xs%d" % h], "Xs%d" % h)

    for h in range(2):
        hs = str(h)
        C(ts(T.z0f[:, 128 * h:128 * h + 128], T.z0s[:, 128 * h:128 * h + 128], -ZC, None, Op.add), 128, ["z0s"], "z0f" + hs)
        for a in range(4):
            src = T.t0s[:, 256 * a + 128 * h:256 * a + 128 * h + 128]
            VA(cp(H("tb", h, a, None, 4), src), 64, act(H("tb", h, a, None, 4), src), 128, ["t0s"], ["tb%d" % h] if a == 0 else ["tb%d_%d" % (h, a)])

    mcount = [0]

    def rotation(t, base):
        if t == 0:
            C(ts(A0("lm"), A0("l5"), 255, None, Op.bitwise_and), 16, ["l5"], "lm")
        else:
            c, fns = {}, []
            if t > 1:
                fns.append(mm(pb(c, 0, 1), T.R8n[:, :], T.CL[0:8, t - 1, 256:257], True, t == NV))
            if t < NV:
                fns.append(mm(pb(c, 0, 1), T.R8[:, :], T.CG[0:8, t, 256:257], t == 1, True))
            P(fns, 256 * len(fns), ["R8", "R8n"] + (["C%d" % (t - 1)] if t > 1 else []) + (["B%d" % t] if t < NV else []), ["dB"], acq=c)
            V(ts(A0("li"), A0(base), pb(c, 0, 1), None, Op.add), 16, [base, "dB"], ["li"], use=c)
            C(ts(A0("lm"), A0("li"), 255, None, Op.bitwise_and), 16, ["li"], "lm")
        C(cp(A0("lu"), A0("lm")), 16, ["lm"], "lu")

    def tables(t):
        rotation(t, "LB")
        for h in range(2):
            tag[0] = ("L", h, t)
            hs, lu = str(h), A0("lu", 8 * h, 8 * h + 8)
            sg, cg = T.sg[:, 128 * h:128 * h + 128], T.CG[:, t, 128 * h:128 * h + 128]
            if t == 0:
                V(ts(sg, A0("s0s").indirect(lu), -ZC, None, Op.add), 248, ["lu", "s0s"], ["sg" + hs])
                V(ts(cg, A0("cfs").indirect(lu), 2.0, 1.0, Op.mult, Op.add), 248, ["lu", "cfs"], ["cg%d%d" % (t, h)])
            else:
                gather(sg, T.SL[:, t - 1, :], lu, 128, ["lu", "S%d0" % (t - 1), "S%d1" % (t - 1)], ["sg" + hs], "gS")
                gather(cg, T.CL[:, t - 1, 0:256], lu, 128, ["lu", "C%d" % (t - 1)], ["cg%d%d" % (t, h)], "gC")
        tag[0] = ("M", 0, t)
        a = 0 if t < NV - 1 else 256
        send(1, T.CL[:, t, a:272], T.CG[:, t, a:272], "rC%d" % t, ["cg%d0" % t, "cg%d1" % t, "pad", "B%d" % t], "C%d" % t, (272 - a) // 2)

    def position(t, h, c, extra):
        hs = str(h)
        if t == 0:
            P([mm(pb(c, 0, 128), T.R8[:, :], T.z0f[:, 128 * h:128 * h + 128])], 512, ["R8", "z0f" + hs] + extra, ["zn" + hs], acq=c)
        else:
            P([mm(pb(c, 0, 128), A0("Wz"), H("prod", h), True, False), mm(pb(c, 0, 128), A0("Bb"), H("ind", h), False, True)], 640,
              ["Wz", "Bb", "prod" + hs, "ind" + hs] + extra, ["zn" + hs], acq=c)

    def columns(h, terms, buf, t):
        hs, c = str(h), {}
        P([mm(pb(c, 0, 128), A0(x[0]), x[1], y == 0, y == len(terms) - 1) for y, x in enumerate(terms)], sum(x[3] for x in terms),
          [x[0] for x in terms] + [x[2] for x in terms], ["F" + hs], acq=c)
        V(cp(H("fi", h), pb(c, 0, 128)), 128, ["F" + hs], ["fi" + hs], use=c)
        V(ts(H("fm", h), H("fi", h), 4095, None, Op.bitwise_and), 128, ["fi" + hs], ["fm" + hs])
        V(cp(H("of", h), H("fm", h)), 128, ["fm" + hs], ["of" + hs])
        for q in range(4):
            gather(H(buf, h, 512 * q, 512 * q + 512), T["x%d" % (t % 4)][:, :], H("of", h, 32 * q, 32 * q + 32), 512, XK[t % 4] + ["of" + hs],
                   [buf + hs + "_%d" % q], buf + str(q), dflt="a")
    YK = lambda b, h: [b + str(h) + "_%d" % q for q in range(4)]

    def front(t, h):
        hs = str(h)
        sg, cg, sk, ck = T.sg[:, 128 * h:128 * h + 128], T.CG[:, t, 128 * h:128 * h + 128], "sg" + hs, "cg%d%d" % (t, h)
        c, fast = {}, prm["FAST"][h]
        position(t, h, c, ["lu"])
        V(tt(H("cmp", h, 0, 128), pb(c, 0, 128), sg, Op.is_ge), 128, ["zn" + hs, sk], ["cmp0" + hs], use=c)
        if fast:
            V(tt(pb(c, 128, 256), sg, pb(c, 0, 128), Op.subtract), 128, ["zn" + hs, sk], ["X" + hs], use=c)
            V(tt(H("Hb", h), pb(c, 128, 256), cg, Op.mult), 128, ["X" + hs, ck], ["Hb" + hs], use=c)
        V(ts(H("ze", h), pb(c, 0, 128), zsc, zbi, Op.mult, Op.max), 128, ["zn" + hs, zsck, zbik], ["ze" + hs], use=c)
        for b in range(2):
            c, bs = {}, str(b) + hs
            if b == 1:
                tag[0] = ("G", h, t)
                P([mm(pb(c, 0, 128), A0("Wz1"), H("ze", h))], 128, ["Wz1", "ze" + hs], ["z1" + hs], acq=c)
                V(tt(H("cmp", h, 128, 256), pb(c, 0, 128), sg, Op.is_ge), 128, ["z1" + hs, sk], ["cmp1" + hs], use=c)
                c = {}
            src, srck = (H("Hb", h), "Hb" + hs) if fast and b == 0 else (sg, sk)
            P([mm(pb(c, 0, 128), A0("Bb"), H("cmp", h, 128 * b, 128 * b + 128))], 128, ["Bb", "cmp" + bs], ["cnt" + bs], acq=c)
            if b == 1 and prm["OA"][h]:
                A(act(pb(c, 256, 384), pb(c, 0, 128), AF.Abs, oh1[0]), 128, ["cnt" + bs, oh1[1]], ["Oa" + hs], use=c)
                A(act(pb(c, 128, 256), pb(c, 256, 384), AF.Relu, oh2[0], -1.0), 128, ["Oa" + hs, oh2[1]], ["OH" + bs], use=c)
            else:
                V(ts(pb(c, 128, 256), pb(c, 0, 128), 1.0, rp1, Op.max, Op.is_equal), 128, ["cnt" + bs, rp1k], ["OH" + bs], use=c)
            V(tt(H("oC", h, 128 * b, 128 * b + 128), pb(c, 128, 256), cg, Op.mult), 128, ["OH" + bs, ck], ["oC" + bs], use=c)
            V(tt(H("oS", h, 128 * b, 128 * b + 128), pb(c, 128, 256), src, Op.mult), 128, ["OH" + bs, srck], ["oS" + bs], use=c)
            if b == 0:
                V(ts(H("geb", h), pb(c, 0, 128), rp1, None, Op.is_le), 128, ["cnt" + bs, rp1k], ["geb" + hs], use=c)
                if fast:
                    columns(h, [("Wk", A0("one"), "one", 128), ("Wm", H("oC", h, 0, 128), "oC0" + hs, 128), ("Bn", H("oS", h, 0, 128), "oS0" + hs, 512)], "y2", t)
        c = {}
        wu, wc, db = ("Wf", T.Wd[:, :], dbf) if fast else ("Wu", T.Wc[:, 3:131], dbs)
        P([mm(pb(c, 0, 128), A0(wu), H("ze", h), True, False), mm(pb(c, 0, 128), T.Wn[:, 15:143], H("oS", h, 0, 128), False, False),
           mm(pb(c, 0, 128), T.Wn[:, 12:140], H("oS", h, 128, 256), False, True)], 1152, [wu, "Wn", "ze" + hs, "oS0" + hs, "oS1" + hs], ["U" + hs], acq=c)
        P([mm(pb(c, 128, 256), wc, H("oC", h, 0, 128), True, False), mm(pb(c, 128, 256), T.Wc[:, 0:128], H("oC", h, 128, 256), False, True)], 256,
          ["Wc", "Wd", "oC0" + hs, "oC1" + hs], ["Cr" + hs], use=c, after=[c["first"]])
        VA(ts(H("Dc", h), pb(c, 128, 256), db[0], None, Op.add), 128, act(H("Dc", h), pb(c, 128, 256), AF.Identity, db[0]), 128, ["Cr" + hs, db[1]], ["Dc" + hs], use=c, name="Dc")
        V(tt(H("Left", h), pb(c, 0, 128), H("Dc", h), Op.mult), 128, ["U" + hs, "Dc" + hs], ["Left" + hs], use=c)
        if not fast:
            tag[0] = ("F", h, t)
            columns(h, [("Wy", H("Left", h), "Left" + hs, 512)], "y2", t)

    def match(t, h):
        hs = str(h)
        TK = ["tb" + hs] + (["tb%d_%d" % (h, a) for a in (1, 2, 3)] if t == 0 else [])
        K = T.kb[:, 0:104]
        P([mm(K, A0("w7"), A0("cj"), True, False)] + [mm(K, H("tb", h, a, None, 4), T[RT[h]][:, :, :], False, False) for a in range(4)], 520,
          ["w7", "cj", RT[h], "y2%s_0" % hs] + TK, ["K"])
        y = lambda m: H("y2", h, m, None, 16)
        P([mm(K, y(m), T.Z[:, :, 19 - m:32 - m], False, False) for m in range(16)], 1664, YK("y2", h) + ["Z"], [], acc="K", name="ysum")
        for b in range(4):
            P([mm(T.yps[:, 32 * b:32 * b + 32, :], A0("Ib"), H("y2", h, 512 * b, 512 * b + 512))], 512, ["y2%s_%d" % (hs, b), "Ib"], ["yps%d" % b])
        for x, j in enumerate(range(JA[h], J)):
            c = {}
            P([mm(pb(c, 0, 512), A0("Im"), H("tb", h), True, False)] + [mm(pb(c, a, 512, 4), A0("Ib"), y(j + a), False, a == 3) for a in range(4)], 1024,
              YK("y2", h) + TK + ["Ib", "Im"], ["dif%s%d" % (hs, x)], acq=c, name="dif")
            A(act(H("Ma", h, 512 * x, 512 * x + 512), pb(c, 0, 512), AF.Relu), 512, ["dif%s%d" % (hs, x)], ["Ma%s%d" % (hs, x)], use=c)
            P([mm(T.kb[:, j:104:13], H("Ma", h, 512 * x + a, 512 * x + 512, 4), A0("G64"), False, False) for a in range(4)],
              256, ["Ma%s%d" % (hs, x), "G64"], [], acc="K", name="asum")
        bufs = []
        for j in range(JA[h]):
            bufs.append(mcount[0] % NM)
            mcount[0] += 1
        order = [(j, 0, 2) for j in range(NS[h])] + [(j, 2, 4) for j in range(NS[h])] + [(j, 0, 4) for j in range(NS[h], JA[h])]
        prev = []
        for j, b0, b1 in order:
            M, mk = T["mb%d" % bufs[j]], "mb%d" % bufs[j]
            prev = [V(tt(M[:, 128 * b0:128 * b1], T.yps[:, 32 * b0:32 * b1, j:j + 4], H("tb", h, 128 * b0, 128 * b1), Op.max), 128 * (b1 - b0),
                      ["yps%d" % b for b in range(b0, b1)] + TK, [mk + "_%d" % b for b in range(b0, b1, 2)], after=prev, name="max")]
            if b1 == 4:
                P([mm(T.kb[:, j:104:13], M[:, a:512:4], A0("G64"), False, False) for a in range(4)], 256, [mk + "_0", mk + "_2", "G64"], [], acc="K", name="vsum")
        tag[0] = ("D", h, t)
        V(scan(H("ks", h), A0("KD"), K, Op.max, Op.min), SCN + 104, ["K", "KD"], ["ks" + hs])

    def decide(t, h):
        hs = str(h)
        best = H("ks", h, 12, None, 13)
        V(ts(H("rr", h), best, MAGIC, MAGIC, Op.add, Op.subtract), 8, ["ks" + hs], ["rr" + hs])
        c = {}
        V(ts(H("Xs", h, 0, 128, 16), best, FAKE - 8, None, Op.is_lt), 8, ["ks" + hs, "Xs" + hs], ["Xt" + hs])
        V(tt(H("Xs", h, 128, 256, 16), H("rr", h), best, Op.subtract), 16, ["rr" + hs, "ks" + hs], ["Xd" + hs])
        V(scan(H("Xr", h), A0("RD"), H("Xs", h), Op.mult, Op.add), SCN + 128, ["RD", "Xt" + hs, "Xd" + hs], ["Xr" + hs])
        P([mm(pb(c, 0, 128), H("Xr", h, 0, 128), A0("Ib"), True, False), mm(pb(c, 0, 128), H("Xs", h, 123, 251), A0("Ib"), False, True),
           mm(pb(c, 128, 256), H("Xr", h, 128, 256), A0("Ib"))], 384, ["Ib", "Xr" + hs, "Xd" + hs], ["w" + hs], acq=c)
        tag[0] = ("N", h, t)
        V(tt(H("prod", h), pb(c, 0, 128), H("Left", h), Op.mult), 128, ["w" + hs, "Left" + hs], ["prod" + hs], use=c)
        tag[0] = ("S", h, t)
        sn = T.SN[:, t, 128 * h:128 * h + 128]
        V(tt(pb(c, 256, 384), pb(c, 128, 256), H("geb", h), Op.mult), 128, ["w" + hs, "geb" + hs], ["dge" + hs], use=c)
        V(tt(sn, pb(c, 256, 384), T.sg[:, 128 * h:128 * h + 128], Op.add), 128, ["dge" + hs, "sg" + hs], ["sn%d%d" % (t, h)], use=c)
        lastw["sent"] = send(1, T.SL[:, t, 128 * h:128 * h + 128], sn, "rS%d%d" % (t, h), ["sn%d%d" % (t, h)], "S%d%d" % (t, h), 64)
        if h == 1 and t < 2:
            tag[0] = ("X", 0, t)
            sendlog(t + 2, "sent")
        tag[0] = ("N", h, t)
        columns(h, [("Wv", H("prod", h), "prod" + hs, 512)], "v2", t)

    def counts(t):
        c = {}
        P([mm(pb(c, 0, 1, 1, 8), H("Xs", h, 0, 128, 16), T.c205[:, 0:1], h == 0, h == 1) for h in range(2)], 128, ["Xt0", "Xt1", "c205"], ["Aps"], acq=c)
        out = T.CG[0:8, t + 1, 256:257]
        VA(cp(out, pb(c, 0, 1, 1, 8)), 1, act(out, pb(c, 0, 1, 1, 8)), 1, ["Aps", "pad"], ["B%d" % (t + 1)], use=c, name="B")

    def finish(t, h):
        hs = str(h)
        nb = prm["SB"][h]
        bw, nu = 128 // nb, (3, 2)[nb - 1]
        nw = 12 // nu
        for b in range(nb):
            for u in range(nu):
                c, fns, n = {}, [], nu * b + u
                for w in range(nw):
                    m = 16 * bw * b + 4 + nw * u + w
                    fns += [mm(pb(c, bw * w, bw * w + bw), A0("Ib"), H("v2", h, m, 16 * bw * (b + 1), 16), True, False),
                            mm(pb(c, bw * w, bw * w + bw), A0("Im"), H("v2", h, m - 1, 16 * bw * (b + 1), 16), False, True)]
                P(fns, 2 * nw * bw, YK("v2", h)[4 * b // nb:4 * (b + 1) // nb] + ["Ib", "Im"], ["st%s%d" % (hs, n)], acq=c)
                A(act(H("Va", h, nw * bw * n, nw * bw * (n + 1)), pb(c, 0, nw * bw), AF.Abs), nw * bw, ["st%s%d" % (hs, n)], ["Va%s%d" % (hs, n)], use=c)
        c, prev = {}, None
        for n in range(nb * nu):
            b, u = n // nu, n % nu
            fns = [mm(pb(c, bw * b, bw * b + bw), T.Wx[:, 11 - nw * u - w:139 - nw * u - w], H("Va", h, bw * (nw * n + w), bw * (nw * n + w + 1)),
                      u == 0 and w == 0, u == nu - 1 and w == nw - 1) for w in range(nw)]
            extra = ["Va%s%d" % (hs, min(nb * nu - 1, prm["SUMAFT"]))] if n == 0 else []
            prev = P(fns, nw * bw, ["Wx", "Va%s%d" % (hs, n)] + extra, ["sum%s%d" % (hs, n)], **({"acq": c} if n == 0 else {"use": c, "after": [prev]}))
        VA(ts(H("r1", h), pb(c, 0, 128), -820.0, 0.0, Op.add, Op.max), 128, act(H("r1", h), pb(c, 0, 128), AF.Relu, -820.0), 128,
           ["sum%s%d" % (hs, n) for n in range(nb * nu)], ["r1" + hs], use=c, name="r1")
        c = {}
        P([mm(pb(c, 0, 128), A0("Wp"), H("r1", h))], 128, ["Wp", "r1" + hs], ["pre" + hs], acq=c)
        VA(ts(H("ind", h), pb(c, 0, 128), 0.5, None, Op.is_lt), 128, act(H("ind", h), pb(c, 0, 128), AF.Relu, 1.0, -1.0), 128, ["pre" + hs], ["ind" + hs], use=c, name="ind")
        tag[0] = ("T", h, t)
        c = {}
        P([mm(pb(c, 0, 32), A0("Ih"), A0("Qc"), True, False)] +
          [mm(pb(c, 0, 32), T.Wq[:, 12 - 4 * u:140 - 4 * u], H("ind", h, u, None, 4), False, u == 3) for u in range(4)], 320, ["Ih", "Qc", "Wq", "ind" + hs], ["Q" + hs], acq=c)
        V(cp(H("tof", h), pb(c, 0, 32)), 32, ["Q" + hs], ["tof" + hs], use=c)
        gather(H("tb", h), H("v2", h), H("tof", h), 512, YK("v2", h) + ["tof" + hs], ["tb" + hs], "gT")

    for t in range(NV):
        tag[0] = ("L", 0, t)
        tables(t)
        for h in range(2):
            tag[0] = ("F", h, t)
            front(t, h)
        for h in range(2):
            tag[0] = ("H", h, t)
            match(t, h)
            decide(t, h)
        if t < NV - 1:
            tag[0] = ("C", 0, t)
            counts(t)
        for h in range(2):
            tag[0] = ("E", h, t)
            finish(t, h)

    tag[0] = ("L", 0, NV)
    rotation(NV, "LF")
    gather(A0("ysb"), T.SL[:, NV - 1, :], A0("lu"), 256, ["lu", "S%d0" % (NV - 1), "S%d1" % (NV - 1)], ["ysb"], "gY", bias=ZC)
    dmas([(T.ys[:, :], T.ysb[:, :])], ["ysb"], [], "sto", 128)
    fin = []
    for h in range(2):
        tag[0] = ("L", h, NV)
        c, zo = {}, T.zb[:, 128 * h:128 * h + 128]
        position(NV, h, c, [])
        VA(ts(zo, pb(c, 0, 128), ZC, None, Op.add), 128, act(zo, pb(c, 0, 128), AF.Identity, ZC), 128, ["zn%d" % h], ["zb%d" % h], use=c)
        dmas([(T.yz[:, 128 * h:128 * h + 128], T.zb[0:128:16, 128 * h:128 * h + 128])], ["zb%d" % h], [], "sto", 4)
        for a in range(4):
            dst = T.ytb[:, 256 * a + 128 * h:256 * a + 128 * h + 128]
            fin.append("yt%d%d" % (h, a))
            V(cp(dst, H("tb", h, a, None, 4)), 64, ["tb%d" % h], [fin[-1]])
    dmas([(T.yt[:, :], T.ytb[:, :])], fin, [], "sto", 256)
    return ops


def schedule(ops, prm):
    n = len(ops)
    succ = [[] for _ in range(n)]
    for i, o in enumerate(ops):
        for d in o["deps"]:
            succ[d].append(i)
    way_ = [0.0] * n
    for i in range(n - 1, -1, -1):
        way_[i] = min(ops[i]["cost"].values()) + ops[i]["lat"] + max([way_[k] for k in succ[i]], default=0.0) + HOP
    rank, bonus, win, lam = prm["RANK"], prm["BONUS"], prm["WIN"], prm["LAM"]
    pr, cost = [], []
    for i, o in enumerate(ops):
        tag, key = o["tag"], (o["name"], o["tag"][1])
        pr.append((0.01 * way_[i] - 100.0 * tag[2] - rank[tag[:2]] if tag[:2] in rank else way_[i]) + o["bonus"] + bonus.get(key, 0.0))
        e = prm["ENG"].get(key, o["dflt"])
        cost.append(list(o["cost"].items()) if len(o["cost"]) == 1 else [x for x in o["cost"].items() if x[0] in e])
    first = [o["use"]["first"] if o["use"] is not None else -1 for o in ops]
    left = [len(o["deps"]) for o in ops]
    pend = [0] * n
    for f in first:
        pend[f] += f >= 0
    ready = [i for i in range(n) if left[i] == 0]
    free, busy = {e: 0.0 for e in "vapqdn"}, 0.0
    end, order, eng, more, banks = [0.0] * n, [], [None] * n, {}, {}
    dep_end = [dict.fromkeys([x[0] for x in c], 0.0) for c in cost]
    holder = {b: None for b in POOL}
    users = {b: [] for b in POOL}
    last = {b: {} for b in POOL}
    while len(order) < n:
        cand = {}
        open_ = min([(max(last[b].values(), default=-HOP) + HOP, b) for b in POOL if holder[b] is None or pend[holder[b]] == 0], default=None)
        for i in ready:
            f = first[i]
            if f == i and open_ is None:
                continue
            for e, t1 in dep_end[i].items():
                if t1 < free[e]:
                    t1 = free[e]
                if f == i:
                    t1 = max(t1, open_[0])
                elif f >= 0:
                    for x, t2 in last[banks[f]].items():
                        if x != e and t2 + HOP > t1:
                            t1 = t2 + HOP
                cand.setdefault(e, []).append((t1, i))
        best = None
        for e, cs in cand.items():
            lo = min(cs)[0] + win
            c = max((c for c in cs if c[0] <= lo), key=lambda c: pr[c[1]] - lam * c[0])
            if best is None or (c[0], -pr[c[1]]) < (best[0][0], -pr[best[0][1]]):
                best = (c, e)
        (est, i), e = best
        o, f = ops[i], first[i]
        ready.remove(i)
        eng[i] = e
        end[i] = est + o["cost"][e]
        if f == i:
            more[i] = users[open_[1]]
            holder[open_[1]], users[open_[1]], last[open_[1]], banks[i] = i, [], {}, open_[1]
        if f >= 0:
            b = banks[f]
            more[i] = more.get(i, []) + [m for m in users[b] if eng[m] != e]
            users[b].append(i)
            last[b][e] = end[i]
            pend[f] -= 1
        if e != "n":
            free[e] = end[i]
        if o["lat"]:
            busy = max(busy, end[i]) + o["sym"][2]
            end[i] = busy + o["sym"][3]
        order.append(i)
        for k in succ[i]:
            left[k] -= 1
            de = dep_end[k]
            for x in de:
                t1 = end[i] + (OWN if x == e or x == "n" else HOP)
                if t1 > de[x]:
                    de[x] = t1
            if left[k] == 0:
                ready.append(k)
    return order, end, eng, more, banks


def emit(ops, order, T, gs):
    nxt, lastacc = {}, set()
    for i in reversed(order):
        if ops[i]["acc"] is not None and ops[i]["tag"] not in nxt:
            nxt[ops[i]["tag"]] = i
            lastacc.add(i)
    count = {}
    done = {}
    know = {e: {} for e in "vapqd"}

    def after(e, i, raw):
        sem, val, clk = done[i]
        if ops[i]["eng"] == e and not raw and (e == "p" or sem == "loc" or raw is None):
            return
        if know[e].get(sem, 0) >= val:
            return
        gs[e].wait_ge(T.sem[sem], val)
        for k, w in clk.items():
            if know[e].get(k, 0) < w:
                know[e][k] = w
        know[e][sem] = max(val, know[e].get(sem, 0))
    for i in order:
        o = ops[i]
        e, kind = o["eng"], (o["sym"] or ("",))[0]
        if e == "n":
            done[i] = (o["sym"][1], o["sym"][2], {})
            continue
        for d, raw in sorted(o["deps"].items(), key=lambda d: -done[d[0]][1]):
            after(e, d, raw)
        sem = e if kind == "" else o["sym"][4] if kind == "send" else o["sym"][1]
        for x, fn in enumerate(o["fns"][e]):
            c = fn(x == len(o["fns"][e]) - 1 and i in lastacc)
            if kind == "send":
                count[sem] = count.get(sem, 0) + o["sym"][1]
            else:
                c.then_inc(T.sem[sem], 16 if kind == "dma" else 1)
                count[sem] = count.get(sem, 0) + (16 if kind == "dma" else 1)
        done[i] = (sem, count[sem], dict(know[e]))
    gs["d"].wait_ge(T.sem.sto, count["sto"])
    for sem in ("v", "a", "p", "q", "loc"):
        gs["q"].wait_ge(T.sem[sem], count[sem])


def way(topo, src, dst):
    rid, pid, _ = topo.addr(dst)
    return rid, pid, topo.mask(src, dst), len(topo.engines(src, dst))


def rank_program(g, core, T, topo):
    rank = T.rank_of(core)
    if rank is None:
        return
    n = len(T.cores)
    to = {d: way(topo, core, T.cores[(rank - d) % n]) for d in range(1, n)}
    gs = {"v": g.vector, "a": g.scalar, "p": g.tensor, "q": g, "d": g.sync}
    ops = build(T, gs, to, PRM)
    order, _, eng, more, banks = schedule(ops, PRM)
    for i, o in enumerate(ops):
        o["eng"] = eng[i]
        for m in more.get(i, []):
            o["deps"].setdefault(m, False)
        if i in banks:
            o["acq"]["bank"] = banks[i]
    emit(ops, order, T, gs)
